import numpy as np
import ml_dtypes


def mxq(x, axis, fmt="e4m3"):
    dtype, down = {"e4m3": (ml_dtypes.float8_e4m3fn, 7), "e5m2": (ml_dtypes.float8_e5m2, 14)}[fmt]
    v = np.moveaxis(np.asarray(x, np.float32).astype(ml_dtypes.bfloat16).astype(np.float64), axis, -1)
    blocks = v.reshape(v.shape[:-1] + (-1, 32))
    amax = np.abs(blocks).max(-1, keepdims=True)
    byte = np.maximum(np.where(amax > 0, np.frexp(amax)[1] - 1 + 127, 0) - down, 1)
    scale = np.exp2(byte - 127.0)
    codes = (blocks / scale).astype(np.float32).astype(dtype).astype(np.float64)
    return np.moveaxis((codes * scale).reshape(v.shape), -1, axis)


WIDE = False


def mx_kscale(k):
    if not WIDE:
        return np.ones(k)
    levels = np.array([10, -10, 5, -5, 0])
    if k % 512:
        return np.exp2(np.random.permutation(np.resize(levels, k // 32))).repeat(32)
    a = np.empty((k // 512, 16))
    for p in range(k // 512):
        a[p, :8] = np.random.permutation(np.resize(levels, 8))
        for g in range(8):
            far = levels[np.abs(levels - a[p, g]) >= 10]
            a[p, g + 8] = far[np.random.randint(len(far))]
    return np.exp2(a.ravel()).repeat(32)


def f64(x):
    return np.asarray(x).astype(np.float64)


def striped(idx):
    return np.tile(idx.reshape(-1, 16).T, (8, 1)).astype(np.uint16)


def unstriped(offs):
    return offs[:16].T.reshape(-1).astype(np.int64)


E2M1 = np.array([0.0, 0.5, 1.0, 1.5, 2.0, 3.0, 4.0, 6.0, -0.0, -0.5, -1.0, -1.5, -2.0, -3.0, -4.0, -6.0])


def pack_weight(w, fmt):
    k, n = w.shape
    w = f64(np.asarray(w, np.float32).astype(ml_dtypes.bfloat16)).reshape(k // 32, 32, n)
    amax = np.abs(w).max(1)
    if fmt == "e4m3":
        byte = np.frexp(amax)[1] - 1 + 127 - 7
    else:
        mant, ex = np.frexp(amax / 6.0)
        byte = np.where(mant > 0.5, ex, ex - 1) + 127
    byte = np.clip(np.where(amax > 0, byte, 1), 1, 254)
    scaled = (w * np.exp2(127.0 - byte)[:, None, :]).reshape(k, n).astype(np.float32)
    by_word = np.ascontiguousarray(scaled.reshape(k // 512, 128, 4, n).transpose(0, 1, 3, 2))
    if fmt == "e4m3":
        words = by_word.astype(ml_dtypes.float8_e4m3fn).view(np.uint8)
    else:
        c = by_word.astype(ml_dtypes.float4_e2m1fn).view(np.uint8) & 0xF
        words = (c[..., 0::2] | (c[..., 1::2] << 4)).reshape(k // 512, 128, 2 * n)
    return np.ascontiguousarray(words), np.ascontiguousarray(byte.astype(np.uint8).reshape(k // 512, 16, n))


def unpack_weight(words, scales, fmt):
    g, _, n = scales.shape
    words = np.ascontiguousarray(words).reshape(g, 128, n, -1)
    if fmt == "e4m3":
        vals = words.view(ml_dtypes.float8_e4m3fn).astype(np.float64)
    else:
        nib = np.empty((g, 128, n, 4), np.uint8)
        nib[..., 0::2] = words & 0xF
        nib[..., 1::2] = words >> 4
        vals = E2M1[nib]
    vals = vals * np.repeat(np.exp2(scales.astype(np.float64) - 127.0), 8, axis=1)[..., None]
    return vals.transpose(0, 1, 3, 2).reshape(g * 512, n)


def relu(v):
    return np.maximum(v, 0.0)


K, T, E, C, H, N = 1536, 768, 2, 256, 512, 128


def by_expert(wq, xq):
    return np.concatenate([wq[e].T @ xq[:, e * C:(e + 1) * C] for e in range(E)], axis=1)


def setup_inputs():
    n = np.random.standard_normal
    s = mx_kscale(K)[:, None]
    u = mx_kscale(H)
    w1 = [pack_weight(m, "e2m1") for m in n((E + 1, K, H)) / np.sqrt(K) / s[None] * u[None, None, :]]
    w2 = [pack_weight(m, "e2m1") for m in n((E + 1, H, N)) / np.sqrt(H) / u[None, :, None]]
    return {
        "xT": (n((K, T)) * s).astype(np.float32),
        "w1_words": np.stack([m[0] for m in w1]),
        "w1_scales": np.stack([m[1] for m in w1]),
        "w2_words": np.stack([m[0] for m in w2]),
        "w2_scales": np.stack([m[1] for m in w2]),
        "gate": np.tile(np.random.uniform(0.2, 1.0, E * C), (N, 1)).astype(np.float32),
        "offs": striped(np.random.permutation(T)[:E * C]),
    }


def reference(xT, w1_words, w1_scales, w2_words, w2_scales, gate, offs):
    idx = unstriped(offs)
    w1 = np.stack([unpack_weight(w1_words[e], w1_scales[e], "e2m1") for e in range(E + 1)])
    w2 = np.stack([unpack_weight(w2_words[e], w2_scales[e], "e2m1") for e in range(E + 1)])
    w1q, w2q = w1, w2
    xs = mxq(f64(xT), 0, "e4m3")
    hs = relu(w1q[E].T @ xs)
    ys = w2q[E].T @ mxq(hs, 0, "e4m3")
    xq = mxq(f64(xT)[:, idx], 0, "e4m3")
    h = relu(by_expert(w1q, xq))
    y = by_expert(w2q, mxq(h, 0, "e4m3"))
    out = ys
    out[:, idx] += f64(gate) * y
    return out

@@ -1,0 +1,329 @@
+from contextlib import ExitStack
+
+import concourse.mybir as mybir
+from concourse.masks import make_identity
+
+K, T, E, C, H, N = 1536, 768, 2, 256, 512, 128
+
+P = 128
+S = E * C
+K_PASS = 512
+PASSES = K // K_PASS
+QUADRANTS = 4
+SHARED = E
+UNIT = 2 * P
+
+FLOPS = 2 * (S + T) * (K * H + H * N)
+
+F32 = mybir.dt.float32
+BF16 = mybir.dt.bfloat16
+I32 = mybir.dt.int32
+U32 = mybir.dt.uint32
+U16 = mybir.dt.uint16
+U8 = mybir.dt.uint8
+FP8X4 = mybir.dt.float8_e4m3fn_x4
+FP4X4 = mybir.dt.float4_e2m1fn_x4
+
+RELU = mybir.ActivationFunctionType.Relu
+MULT = mybir.AluOpType.mult
+ADD = mybir.AluOpType.add
+
+SPLIT = 512
+
+STREAMED = (("token", 4), ("token", 5), ("slot", 0), ("slot", 1), ("slot", 3))
+
+
+def tile_moe_shr_mlp_relu_kernel(
+    tc, xT, w1_words, w1_scales, w2_words, w2_scales, gate, offs, out
+):
+    nc = tc.nc
+    with ExitStack() as ctx:
+        keep = ctx.enter_context(tc.tile_pool(name="keep", bufs=1))
+        psum = ctx.enter_context(tc.psum_pool(name="psum", bufs=1))
+
+        offsets = keep.tile([P, S // 16], U16, name="offsets")
+        gate_sb = keep.tile([P, S], F32, name="gate_sb")
+        w2_codes = keep.tile([P, E + 1, 2 * N], U8, align_bytes=64, name="w2_codes")
+        w1_planes = keep.tile([P, (E + 1) * PASSES, H], U8, align_bytes=64, name="w1_planes")
+        w2_planes = keep.tile([P, E + 1, N], U8, align_bytes=64, name="w2_planes")
+        ident = keep.tile([P, P], F32, name="ident")
+        routed = keep.tile([P, T], F32, name="routed")
+        routed_y = keep.tile([P, S], F32, name="routed_y")
+        result = keep.tile([P, T], F32, name="result")
+
+        x_raw, w1_codes, x_pairs, slot_pairs = {}, {}, {}, {}
+        quads, codes, planes = {}, {}, {}
+        for s in range(PASSES):
+            x_raw[s] = keep.tile([P, 4, T], F32, name=f"x_raw{s}")
+            w1_codes[s] = keep.tile([P, E + 1, 2 * H], U8, align_bytes=64, name=f"w1_codes{s}")
+            x_pairs[s] = keep.tile([P, 2, T, 2], BF16, align_bytes=64, name=f"x_pairs{s}")
+            slot_pairs[s] = keep.tile([P, 2, S, 2], BF16, align_bytes=64, name=f"slot_pairs{s}")
+        h_rows, h_quads, h_codes, h_planes = {}, {}, {}, {}
+        for kind, n in (("slot", S), ("token", T)):
+            for s in range(PASSES):
+                quads[kind, s] = keep.tile([P, n, 4], BF16, align_bytes=64, name=f"{kind}_quads{s}")
+                codes[kind, s] = keep.tile([P, n], U32, align_bytes=64, name=f"{kind}_codes{s}")
+                planes[kind, s] = keep.tile([P, n], U8, align_bytes=64, name=f"{kind}_planes{s}")
+            h_rows[kind] = keep.tile([P, n // P, H], BF16, align_bytes=64, name=f"{kind}_h_rows")
+            h_quads[kind] = keep.tile([P, n, 4], BF16, align_bytes=64, name=f"{kind}_h_quads")
+            h_codes[kind] = keep.tile([P, n], U32, align_bytes=64, name=f"{kind}_h_codes")
+            h_planes[kind] = keep.tile([P, n], U8, align_bytes=64, name=f"{kind}_h_planes")
+
+        warm = keep.tile([P, 1], F32, name="warm")
+        nc.vector.memset(warm[:], 0.0)
+        nc.scalar.activation(warm[:], warm[:], RELU)
+
+        w1_plane_words = w1_planes[:].rearrange("p a i -> p (a i)").bitcast(I32)
+        w2_plane_words = w2_planes[:].rearrange("p a i -> p (a i)").bitcast(I32)
+        half = (E + 1) * PASSES * H // 4 // 2
+        nc.vector.memset(w1_plane_words[:, :half], 0)
+        nc.gpsimd.memset(w1_plane_words[:, half:], 0)
+        nc.gpsimd.memset(w2_plane_words, 0)
+
+        def load_x(s, u, first, end):
+            rows = xT[K_PASS * s : K_PASS * (s + 1), :].rearrange("(p d) t -> p d t", d=4)
+            pair = slice(2 * u, 2 * u + 2)
+            nc.sync.dma_start(x_raw[s][:, pair, first:end], rows[:, pair, first:end])
+
+        def load_codes(tile, words):
+            experts = E + 1
+            nc.sync.dma_start(
+                tile[:].rearrange("p e b -> p (e b)").bitcast(I32).rearrange("p (e b) -> p e b", e=experts),
+                words.rearrange("e p b -> p e b"),
+            )
+
+        for first in range(0, T, UNIT):
+            load_x(0, 0, first, first + UNIT)
+        nc.sync.dma_start(offsets[:], offs)
+        for q in range(QUADRANTS):
+            nc.gpsimd.dma_start(
+                w1_plane_words.rearrange("p (a i) -> p a i", i=H // 4)[32 * q : 32 * q + 4],
+                w1_scales.bitcast(I32)[:, :, 4 * q : 4 * q + 4, :].rearrange("e s q i -> q (e s) i"),
+            )
+        load_x(0, 1, 0, T)
+        load_x(1, 0, 0, T)
+        load_x(1, 1, 0, T)
+        load_x(2, 0, 0, T)
+        load_codes(w1_codes[0], w1_words.bitcast(I32)[:, 0])
+        load_x(2, 1, 0, T)
+        load_codes(w1_codes[1], w1_words.bitcast(I32)[:, 1])
+        load_codes(w1_codes[2], w1_words.bitcast(I32)[:, 2])
+        load_codes(w2_codes, w2_words.bitcast(I32)[:, 0])
+        nc.sync.dma_start(gate_sb[:], gate)
+        for q in range(QUADRANTS):
+            nc.sync.dma_start(
+                w2_plane_words.rearrange("p (a i) -> p a i", i=N // 4)[32 * q : 32 * q + 4],
+                w2_scales.bitcast(I32)[:, 0, 4 * q : 4 * q + 4, :].rearrange("e q i -> q e i"),
+            )
+
+        make_identity(nc, ident[:])
+        nc.gpsimd.memset(routed[:], 0.0)
+
+        def copy(engine, dst, src):
+            if engine == "vector":
+                nc.vector.tensor_copy(dst, src)
+            else:
+                nc.scalar.copy(dst, src)
+
+        def as_words(tile, columns):
+            return tile[:, columns].rearrange("p c d -> p (c d)").bitcast(F32).rearrange("p (c u) -> p c u", u=2)
+
+        def round_x(engine, s, u, first, end):
+            copy(
+                engine,
+                x_pairs[s][:, u, first:end, :],
+                x_raw[s][:, 2 * u : 2 * u + 2, first:end].rearrange("p d t -> p t d"),
+            )
+
+        def gather(s, u, first, end):
+            nc.vector.tensor_copy(
+                slot_pairs[s][:, u, first:end].rearrange("p c d -> p (c d)").bitcast(U32),
+                x_pairs[s][:, u].rearrange("p t d -> p (t d)").bitcast(U32).indirect(offsets[:, first // 16 : end // 16]),
+            )
+
+        def interleave(engine, kind, s, first, end):
+            pairs = slot_pairs[s] if kind == "slot" else x_pairs[s]
+            words = pairs[:].rearrange("p u c d -> p (u c d)").bitcast(F32).rearrange("p (u c) -> p c u", u=2)
+            copy(engine, as_words(quads[kind, s], slice(first, end)), words[:, first:end])
+
+        def quantise_x(kind, s, first, end):
+            nc.vector.quantize_mx(
+                out=codes[kind, s][:, first:end].bitcast(FP8X4),
+                scales=planes[kind, s][:, first:end],
+                in_=quads[kind, s][:, first:end].rearrange("p c d -> p (c d)"),
+            )
+
+        def expert_of(kind, block):
+            return block * P // C if kind == "slot" else SHARED
+
+        bank = {}
+
+        def first_layer(kind, block, s):
+            if s == 0:
+                bank[kind, block] = psum.tile([P, H], F32, tag="sums", bufs=5, name="sums")
+            e = expert_of(kind, block)
+            columns = slice(P * block, P * (block + 1))
+            nc.tensor.matmul_mx(
+                out=bank[kind, block][:],
+                lhsT=codes[kind, s][:, columns].bitcast(FP8X4),
+                lhsT_scale=planes[kind, s][:, columns],
+                rhs=w1_codes[s][:, e, :].bitcast(FP4X4),
+                rhs_scale=w1_planes[:, e * PASSES + s, :],
+                start=(s == 0),
+                stop=(s == PASSES - 1),
+            )
+
+        def relu(engine, kind, block):
+            if engine == "vector":
+                nc.vector.tensor_scalar_max(h_rows[kind][:, block], bank[kind, block][:], 0.0)
+            else:
+                nc.scalar.activation(h_rows[kind][:, block], bank[kind, block][:], RELU)
+
+        turned = {}
+
+        def turn(kind, block):
+            unit, b = divmod(block, 2)
+            if b == 0:
+                turned[kind, unit] = psum.tile([P, 2, 2, P], F32, tag="turned", bufs=2, name="turned")
+            words = h_rows[kind][:, block].bitcast(F32)
+            for u in range(2):
+                nc.tensor.transpose(turned[kind, unit][:, b, u, :], words[:, u : H // 2 : 2], ident[:])
+
+        def unit_columns(unit):
+            return slice(UNIT * unit, UNIT * (unit + 1))
+
+        def spread(kind, unit):
+            nc.scalar.copy(
+                as_words(h_quads[kind], unit_columns(unit)).rearrange("p (b c) u -> p b c u", b=2),
+                turned[kind, unit][:].rearrange("p b u c -> p b c u"),
+            )
+
+        def quantise_h(kind, unit):
+            columns = unit_columns(unit)
+            nc.vector.quantize_mx(
+                out=h_codes[kind][:, columns].bitcast(FP8X4),
+                scales=h_planes[kind][:, columns],
+                in_=h_quads[kind][:, columns].rearrange("p c d -> p (c d)"),
+            )
+
+        y = {}
+
+        def second_layer(kind, unit):
+            columns = unit_columns(unit)
+            e = expert_of(kind, 2 * unit)
+            if kind == "slot":
+                y[kind, unit] = psum.tile([P, UNIT], F32, tag="y", bufs=1, name="y")
+            else:
+                y[kind, unit] = psum.tile([P, UNIT], F32, tag="sums", bufs=5, name="ys")
+            nc.tensor.matmul_mx(
+                out=y[kind, unit][:],
+                lhsT=w2_codes[:, e, :].bitcast(FP4X4),
+                lhsT_scale=w2_planes[:, e, :],
+                rhs=h_codes[kind][:, columns].bitcast(FP8X4),
+                rhs_scale=h_planes[kind][:, columns],
+                start=True,
+                stop=True,
+            )
+
+        def take_y(unit):
+            nc.scalar.copy(routed_y[:, unit_columns(unit)], y["slot", unit][:])
+
+        def scatter(unit):
+            columns = unit_columns(unit)
+            nc.vector.tensor_tensor(
+                routed[:].indirect(offsets[:, UNIT // 16 * unit : UNIT // 16 * (unit + 1)]),
+                routed_y[:, columns],
+                gate_sb[:, columns],
+                MULT,
+            )
+
+        def finish(unit):
+            columns = unit_columns(unit)
+            nc.vector.tensor_tensor(result[:, columns], y["token", unit][:], routed[:, columns], ADD)
+            nc.sync.dma_start(out[:, columns], result[:, columns])
+
+        for s in range(PASSES):
+            for u in range(2):
+                round_x("scalar", s, u, 0, SPLIT)
+                round_x("vector", s, u, SPLIT, T)
+                if s > 0 and u == 0:
+                    interleave("scalar", "slot", s - 1, 0, S)
+                    quantise_x("token", s - 1, SPLIT, T)
+                if s > 0 and u == 1:
+                    quantise_x("slot", s - 1, 0, S)
+                    for kind, block in STREAMED:
+                        first_layer(kind, block, s - 1)
+                if u == 1:
+                    interleave("scalar", "token", s, SPLIT, T)
+                if (s, u) == (PASSES - 1, 1):
+                    for e in range(E):
+                        gather(s, u, C * e, C * (e + 1))
+                        interleave("scalar", "slot", s, C * e, C * (e + 1))
+                else:
+                    gather(s, u, 0, S)
+                if (s, u) == (1, 0):
+                    interleave("vector", "token", 0, 0, SPLIT)
+
+        last = PASSES - 1
+        quantise_x("token", last, SPLIT, T)
+        quantise_x("slot", last, 0, C)
+        for block in (4, 5):
+            first_layer("token", block, last)
+            relu("scalar", "token", block)
+        interleave("vector", "token", 2, 0, SPLIT)
+        quantise_x("slot", last, C, S)
+        quantise_x("token", 2, 0, SPLIT)
+        for block in (0, 1, 3):
+            first_layer("slot", block, last)
+        for s in range(last):
+            first_layer("slot", 2, s)
+        for block in (0, 1, 3):
+            relu("vector" if block == 3 else "scalar", "slot", block)
+        for b in range(2):
+            turn("token", 4 + b)
+            turn("slot", b)
+        spread("token", 2)
+        spread("slot", 0)
+        quantise_x("token", 0, 0, SPLIT)
+        first_layer("slot", 2, last)
+        interleave("vector", "token", 1, 0, SPLIT)
+        relu("vector", "slot", 2)
+        quantise_x("token", 1, 0, SPLIT)
+
+        for block in range(4):
+            first_layer("token", block, 0)
+        for block in (2, 3):
+            turn("slot", block)
+        quantise_h("slot", 0)
+        quantise_h("token", 2)
+        spread("slot", 1)
+        for block in (2, 3):
+            first_layer("token", block, 1)
+        second_layer("slot", 0)
+        take_y(0)
+        quantise_h("slot", 1)
+        scatter(0)
+        for block in (2, 3):
+            first_layer("token", block, 2)
+            relu("scalar", "token", block)
+        second_layer("slot", 1)
+        for block in (0, 1):
+            first_layer("token", block, 1)
+            first_layer("token", block, 2)
+        take_y(1)
+        scatter(1)
+        second_layer("token", 2)
+
+        for block in (0, 1):
+            relu("scalar", "token", block)
+        for block in (2, 3, 0, 1):
+            turn("token", block)
+        spread("token", 1)
+        spread("token", 0)
+        quantise_h("token", 1)
+        finish(2)
+        second_layer("token", 1)
+        quantise_h("token", 0)
+        finish(1)
+        second_layer("token", 0)
+        finish(0)

@@ -28,9 +28,21 @@ RELU = mybir.ActivationFunctionType.Relu
 MULT = mybir.AluOpType.mult
 ADD = mybir.AluOpType.add
 
-SPLIT = 512
+BANK = {("slot", 0): 0, ("slot", 1): 1, ("slot", 2): 2, ("slot", 3): 3, ("token", 0): 4, ("token", 1): 5, ("token", 2): 6, ("token", 3): 7, ("token", 4): 1, ("token", 5): 3}
 
-STREAMED = (("token", 4), ("token", 5), ("slot", 0), ("slot", 1), ("slot", 3))
+
+def staging(kind, s, first):
+    return kind, s, first
+
+
+def y_bank(kind, unit):
+    if kind == "token" and unit < 2:
+        return (3, 7)[unit]
+    return BANK[kind, 2 * unit]
+
+
+def h_slot(kind, block):
+    return block % 4
 
 
 def tile_moe_shr_mlp_relu_kernel(
@@ -54,20 +66,24 @@ def tile_moe_shr_mlp_relu_kernel(
         x_raw, w1_codes, x_pairs, slot_pairs = {}, {}, {}, {}
         quads, codes, planes = {}, {}, {}
         for s in range(PASSES):
-            x_raw[s] = keep.tile([P, 4, T], F32, name=f"x_raw{s}")
-            w1_codes[s] = keep.tile([P, E + 1, 2 * H], U8, align_bytes=64, name=f"w1_codes{s}")
-            x_pairs[s] = keep.tile([P, 2, T, 2], BF16, align_bytes=64, name=f"x_pairs{s}")
-            slot_pairs[s] = keep.tile([P, 2, S, 2], BF16, align_bytes=64, name=f"slot_pairs{s}")
+            for u in range(2):
+                x_raw[s, u] = keep.tile([P, 2, T], F32, name=f"x_raw{s}{u}")
+            w1_codes[s] = keep.tile([P, (E + 1) * 2 * H], U8, align_bytes=64, name=f"w1_codes{s}")
+            x_pairs[s] = keep.tile([P, 2 * T * 2], BF16, align_bytes=64, name=f"x_pairs{s}")
+            slot_pairs[s] = keep.tile([P, 2 * S * 2], BF16, align_bytes=64, name=f"slot_pairs{s}")
         h_rows, h_quads, h_codes, h_planes = {}, {}, {}, {}
         for kind, n in (("slot", S), ("token", T)):
             for s in range(PASSES):
-                quads[kind, s] = keep.tile([P, n, 4], BF16, align_bytes=64, name=f"{kind}_quads{s}")
+                quads[kind, s] = keep.tile([P, n * 4], BF16, align_bytes=64, name=f"{kind}_quads{s}")
                 codes[kind, s] = keep.tile([P, n], U32, align_bytes=64, name=f"{kind}_codes{s}")
                 planes[kind, s] = keep.tile([P, n], U8, align_bytes=64, name=f"{kind}_planes{s}")
-            h_rows[kind] = keep.tile([P, n // P, H], BF16, align_bytes=64, name=f"{kind}_h_rows")
-            h_quads[kind] = keep.tile([P, n, 4], BF16, align_bytes=64, name=f"{kind}_h_quads")
-            h_codes[kind] = keep.tile([P, n], U32, align_bytes=64, name=f"{kind}_h_codes")
-            h_planes[kind] = keep.tile([P, n], U8, align_bytes=64, name=f"{kind}_h_planes")
+            for block in range(n // P):
+                if h_slot(kind, block) not in h_rows:
+                    h_rows[h_slot(kind, block)] = keep.tile([P, H], BF16, align_bytes=64, name=f"{kind}_h_rows{block}")
+            for unit in range(n // UNIT):
+                h_quads[kind, unit] = keep.tile([P, UNIT * 4], BF16, align_bytes=64, name=f"{kind}_h_quads{unit}")
+                h_codes[kind, unit] = keep.tile([P, UNIT], U32, align_bytes=64, name=f"{kind}_h_codes{unit}")
+                h_planes[kind, unit] = keep.tile([P, UNIT], U8, align_bytes=64, name=f"{kind}_h_planes{unit}")
 
         warm = keep.tile([P, 1], F32, name="warm")
         nc.vector.memset(warm[:], 0.0)
@@ -75,49 +91,63 @@ def tile_moe_shr_mlp_relu_kernel(
 
         w1_plane_words = w1_planes[:].rearrange("p a i -> p (a i)").bitcast(I32)
         w2_plane_words = w2_planes[:].rearrange("p a i -> p (a i)").bitcast(I32)
-        half = (E + 1) * PASSES * H // 4 // 2
-        nc.vector.memset(w1_plane_words[:, :half], 0)
-        nc.gpsimd.memset(w1_plane_words[:, half:], 0)
-        nc.gpsimd.memset(w2_plane_words, 0)
+        make_identity(nc, ident[:])
+        nc.vector.memset(w1_plane_words, 0)
+        nc.vector.memset(w2_plane_words, 0)
+        nc.vector.memset(routed[:], 0.0)
 
         def load_x(s, u, first, end):
             rows = xT[K_PASS * s : K_PASS * (s + 1), :].rearrange("(p d) t -> p d t", d=4)
-            pair = slice(2 * u, 2 * u + 2)
-            nc.sync.dma_start(x_raw[s][:, pair, first:end], rows[:, pair, first:end])
+            nc.sync.dma_start(x_raw[s, u][:, :, first:end], rows[:, 2 * u : 2 * u + 2, first:end])
 
-        def load_codes(tile, words):
-            experts = E + 1
+        def load_offsets():
+            nc.sync.dma_start(offsets[:], offs)
+
+        def load_w1(s, first, end):
             nc.sync.dma_start(
-                tile[:].rearrange("p e b -> p (e b)").bitcast(I32).rearrange("p (e b) -> p e b", e=experts),
-                words.rearrange("e p b -> p e b"),
+                w1_codes[s][:, 2 * H * first : 2 * H * end].bitcast(I32).rearrange("p (e b) -> p e b", b=H // 2),
+                w1_words.bitcast(I32)[first:end, s].rearrange("e p b -> p e b"),
             )
+
+        def load_w1_scales(queue, first, end):
+            engine = nc.gpsimd if queue == "gpsimd" else nc.sync
+            for q in range(QUADRANTS):
+                if end - first == 1:
+                    engine.dma_start(
+                        w1_plane_words.rearrange("p (e s i) -> p e s i", s=PASSES, i=H // 4)[32 * q : 32 * q + 4, :, first],
+                        w1_scales.bitcast(I32)[:, first, 4 * q : 4 * q + 4, :].rearrange("e q i -> q e i"),
+                    )
+                else:
+                    engine.dma_start(
+                        w1_plane_words.rearrange("p (a i) -> p a i", i=H // 4)[32 * q : 32 * q + 4],
+                        w1_scales.bitcast(I32)[:, :, 4 * q : 4 * q + 4, :].rearrange("e s q i -> q (e s) i"),
+                    )
+
+        def load_rest():
+            nc.sync.dma_start(
+                w2_codes[:].rearrange("p e b -> p (e b)").bitcast(I32).rearrange("p (e b) -> p e b", e=E + 1),
+                w2_words.bitcast(I32)[:, 0].rearrange("e p b -> p e b"),
+            )
+            for q in range(QUADRANTS):
+                nc.sync.dma_start(
+                    w2_plane_words.rearrange("p (a i) -> p a i", i=N // 4)[32 * q : 32 * q + 4],
+                    w2_scales.bitcast(I32)[:, 0, 4 * q : 4 * q + 4, :].rearrange("e q i -> q e i"),
+                )
+            nc.sync.dma_start(gate_sb[:], gate)
 
         for first in range(0, T, UNIT):
             load_x(0, 0, first, first + UNIT)
-        nc.sync.dma_start(offsets[:], offs)
-        for q in range(QUADRANTS):
-            nc.gpsimd.dma_start(
-                w1_plane_words.rearrange("p (a i) -> p a i", i=H // 4)[32 * q : 32 * q + 4],
-                w1_scales.bitcast(I32)[:, :, 4 * q : 4 * q + 4, :].rearrange("e s q i -> q (e s) i"),
-            )
+        load_offsets()
         load_x(0, 1, 0, T)
         load_x(1, 0, 0, T)
         load_x(1, 1, 0, T)
+        load_w1_scales("sync", 0, PASSES)
+        load_w1(0, 0, E + 1)
         load_x(2, 0, 0, T)
-        load_codes(w1_codes[0], w1_words.bitcast(I32)[:, 0])
         load_x(2, 1, 0, T)
-        load_codes(w1_codes[1], w1_words.bitcast(I32)[:, 1])
-        load_codes(w1_codes[2], w1_words.bitcast(I32)[:, 2])
-        load_codes(w2_codes, w2_words.bitcast(I32)[:, 0])
-        nc.sync.dma_start(gate_sb[:], gate)
-        for q in range(QUADRANTS):
-            nc.sync.dma_start(
-                w2_plane_words.rearrange("p (a i) -> p a i", i=N // 4)[32 * q : 32 * q + 4],
-                w2_scales.bitcast(I32)[:, 0, 4 * q : 4 * q + 4, :].rearrange("e q i -> q e i"),
-            )
-
-        make_identity(nc, ident[:])
-        nc.gpsimd.memset(routed[:], 0.0)
+        load_w1(1, 0, E + 1)
+        load_w1(2, 0, E + 1)
+        load_rest()
 
         def copy(engine, dst, src):
             if engine == "vector":
@@ -125,108 +155,114 @@ def tile_moe_shr_mlp_relu_kernel(
             else:
                 nc.scalar.copy(dst, src)
 
-        def as_words(tile, columns):
-            return tile[:, columns].rearrange("p c d -> p (c d)").bitcast(F32).rearrange("p (c u) -> p c u", u=2)
-
         def round_x(engine, s, u, first, end):
             copy(
                 engine,
-                x_pairs[s][:, u, first:end, :],
-                x_raw[s][:, 2 * u : 2 * u + 2, first:end].rearrange("p d t -> p t d"),
+                x_pairs[s][:, 2 * (T * u + first) : 2 * (T * u + end)].rearrange("p (t d) -> p t d", d=2),
+                x_raw[s, u][:, :, first:end].rearrange("p d t -> p t d"),
             )
 
         def gather(s, u, first, end):
             nc.vector.tensor_copy(
-                slot_pairs[s][:, u, first:end].rearrange("p c d -> p (c d)").bitcast(U32),
-                x_pairs[s][:, u].rearrange("p t d -> p (t d)").bitcast(U32).indirect(offsets[:, first // 16 : end // 16]),
+                slot_pairs[s][:, 2 * (S * u + first) : 2 * (S * u + end)].bitcast(U32),
+                x_pairs[s][:, 2 * T * u : 2 * T * (u + 1)].bitcast(U32).indirect(offsets[:, first // 16 : end // 16]),
             )
+
+        def staged(kind, s, first, end):
+            kind2, s2, first2 = staging(kind, s, first)
+            return quads[kind2, s2][:, 4 * first2 : 4 * (first2 + end - first)]
 
         def interleave(engine, kind, s, first, end):
             pairs = slot_pairs[s] if kind == "slot" else x_pairs[s]
-            words = pairs[:].rearrange("p u c d -> p (u c d)").bitcast(F32).rearrange("p (u c) -> p c u", u=2)
-            copy(engine, as_words(quads[kind, s], slice(first, end)), words[:, first:end])
+            words = pairs[:].bitcast(F32).rearrange("p (u c) -> p c u", u=2)
+            copy(
+                engine,
+                staged(kind, s, first, end).bitcast(F32).rearrange("p (c u) -> p c u", u=2),
+                words[:, first:end],
+            )
 
         def quantise_x(kind, s, first, end):
             nc.vector.quantize_mx(
                 out=codes[kind, s][:, first:end].bitcast(FP8X4),
                 scales=planes[kind, s][:, first:end],
-                in_=quads[kind, s][:, first:end].rearrange("p c d -> p (c d)"),
+                in_=staged(kind, s, first, end),
             )
 
         def expert_of(kind, block):
             return block * P // C if kind == "slot" else SHARED
 
-        bank = {}
+        def in_bank(kind, block, shape, name):
+            return psum.tile(shape, F32, tag=f"bank{BANK[kind, block]}", bufs=1, name=name)
+
+        sums = {}
 
         def first_layer(kind, block, s):
             if s == 0:
-                bank[kind, block] = psum.tile([P, H], F32, tag="sums", bufs=5, name="sums")
+                sums[kind, block] = in_bank(kind, block, [P, H], "sums")
             e = expert_of(kind, block)
             columns = slice(P * block, P * (block + 1))
             nc.tensor.matmul_mx(
-                out=bank[kind, block][:],
+                out=sums[kind, block][:],
                 lhsT=codes[kind, s][:, columns].bitcast(FP8X4),
                 lhsT_scale=planes[kind, s][:, columns],
-                rhs=w1_codes[s][:, e, :].bitcast(FP4X4),
+                rhs=w1_codes[s][:, 2 * H * e : 2 * H * (e + 1)].bitcast(FP4X4),
                 rhs_scale=w1_planes[:, e * PASSES + s, :],
                 start=(s == 0),
                 stop=(s == PASSES - 1),
             )
 
         def relu(engine, kind, block):
+            dst = h_rows[h_slot(kind, block)][:].rearrange("c (u p d) -> c u p d", u=2, d=2)
+            src = sums[kind, block][:].rearrange("c (p u d) -> c u p d", u=2, d=2)
             if engine == "vector":
-                nc.vector.tensor_scalar_max(h_rows[kind][:, block], bank[kind, block][:], 0.0)
+                nc.vector.tensor_scalar_max(dst, src, 0.0)
             else:
-                nc.scalar.activation(h_rows[kind][:, block], bank[kind, block][:], RELU)
+                nc.scalar.activation(dst, src, RELU)
 
         turned = {}
 
         def turn(kind, block):
             unit, b = divmod(block, 2)
             if b == 0:
-                turned[kind, unit] = psum.tile([P, 2, 2, P], F32, tag="turned", bufs=2, name="turned")
-            words = h_rows[kind][:, block].bitcast(F32)
+                turned[kind, unit] = in_bank(kind, block, [P, 2, 2, P], "turned")
+            words = h_rows[h_slot(kind, block)][:].bitcast(F32)
             for u in range(2):
-                nc.tensor.transpose(turned[kind, unit][:, b, u, :], words[:, u : H // 2 : 2], ident[:])
+                nc.tensor.transpose(turned[kind, unit][:, b, u, :], words[:, P * u : P * (u + 1)], ident[:])
 
         def unit_columns(unit):
             return slice(UNIT * unit, UNIT * (unit + 1))
 
-        def spread(kind, unit):
-            nc.scalar.copy(
-                as_words(h_quads[kind], unit_columns(unit)).rearrange("p (b c) u -> p b c u", b=2),
+        def spread(engine, kind, unit):
+            copy(
+                engine,
+                h_quads[kind, unit][:].bitcast(F32).rearrange("p (b c u) -> p b c u", b=2, u=2),
                 turned[kind, unit][:].rearrange("p b u c -> p b c u"),
             )
 
         def quantise_h(kind, unit):
-            columns = unit_columns(unit)
             nc.vector.quantize_mx(
-                out=h_codes[kind][:, columns].bitcast(FP8X4),
-                scales=h_planes[kind][:, columns],
-                in_=h_quads[kind][:, columns].rearrange("p c d -> p (c d)"),
+                out=h_codes[kind, unit][:].bitcast(FP8X4),
+                scales=h_planes[kind, unit][:],
+                in_=h_quads[kind, unit][:],
             )
 
         y = {}
 
         def second_layer(kind, unit):
-            columns = unit_columns(unit)
             e = expert_of(kind, 2 * unit)
-            if kind == "slot":
-                y[kind, unit] = psum.tile([P, UNIT], F32, tag="y", bufs=1, name="y")
-            else:
-                y[kind, unit] = psum.tile([P, UNIT], F32, tag="sums", bufs=5, name="ys")
+            y[kind, unit] = psum.tile([P, UNIT], F32, tag=f"bank{y_bank(kind, unit)}", bufs=1, name="y")
             nc.tensor.matmul_mx(
                 out=y[kind, unit][:],
                 lhsT=w2_codes[:, e, :].bitcast(FP4X4),
                 lhsT_scale=w2_planes[:, e, :],
-                rhs=h_codes[kind][:, columns].bitcast(FP8X4),
-                rhs_scale=h_planes[kind][:, columns],
+                rhs=h_codes[kind, unit][:].bitcast(FP8X4),
+                rhs_scale=h_planes[kind, unit][:],
                 start=True,
                 stop=True,
             )
 
-        def take_y(unit):
-            nc.scalar.copy(routed_y[:, unit_columns(unit)], y["slot", unit][:])
+        def take_y(engine, unit):
+            copy(engine, routed_y[:, unit_columns(unit)], y["slot", unit][:])
 
         def scatter(unit):
             columns = unit_columns(unit)
@@ -242,88 +278,81 @@ def tile_moe_shr_mlp_relu_kernel(
             nc.vector.tensor_tensor(result[:, columns], y["token", unit][:], routed[:, columns], ADD)
             nc.sync.dma_start(out[:, columns], result[:, columns])
 
-        for s in range(PASSES):
-            for u in range(2):
-                round_x("scalar", s, u, 0, SPLIT)
-                round_x("vector", s, u, SPLIT, T)
-                if s > 0 and u == 0:
-                    interleave("scalar", "slot", s - 1, 0, S)
-                    quantise_x("token", s - 1, SPLIT, T)
-                if s > 0 and u == 1:
-                    quantise_x("slot", s - 1, 0, S)
-                    for kind, block in STREAMED:
-                        first_layer(kind, block, s - 1)
-                if u == 1:
-                    interleave("scalar", "token", s, SPLIT, T)
-                if (s, u) == (PASSES - 1, 1):
-                    for e in range(E):
-                        gather(s, u, C * e, C * (e + 1))
-                        interleave("scalar", "slot", s, C * e, C * (e + 1))
-                else:
-                    gather(s, u, 0, S)
-                if (s, u) == (1, 0):
-                    interleave("vector", "token", 0, 0, SPLIT)
-
+        slots = [("slot", b) for b in range(4)]
+        tokens = [("token", b) for b in range(4)]
         last = PASSES - 1
-        quantise_x("token", last, SPLIT, T)
-        quantise_x("slot", last, 0, C)
-        for block in (4, 5):
+        round_x("scalar", 0, 0, 0, 256)
+        round_x("scalar", 0, 0, 256, 512)
+        round_x("vector", 0, 0, 512, T)
+        gather(0, 0, 0, S)
+        round_x("scalar", 0, 1, 0, 256)
+        round_x("vector", 0, 1, 256, T)
+        gather(0, 1, 0, S)
+        interleave("scalar", "token", 0, 0, 512)
+        round_x("scalar", 1, 0, 0, T)
+        gather(1, 0, 0, S)
+        round_x("scalar", 1, 1, 0, 512)
+        round_x("vector", 1, 1, 512, T)
+        gather(1, 1, 0, S)
+        interleave("vector", "slot", 0, 0, S)
+        quantise_x("slot", 0, 0, S)
+        quantise_x("token", 0, 0, 512)
+        for kind, block in slots + tokens:
+            first_layer(kind, block, 0)
+        round_x("scalar", 2, 0, 0, 256)
+        round_x("vector", 2, 0, 256, T)
+        gather(2, 0, 0, S)
+        interleave("scalar", "slot", 1, 0, S)
+        quantise_x("slot", 1, 0, S)
+        round_x("scalar", last, 1, 0, 512)
+        round_x("vector", last, 1, 512, T)
+        interleave("scalar", "token", 1, 0, 512)
+        quantise_x("token", 1, 0, 512)
+        for kind, block in slots + tokens:
+            first_layer(kind, block, 1)
+        for e in range(E):
+            gather(last, 1, C * e, C * (e + 1))
+        interleave("scalar", "token", last, 0, 256)
+        quantise_x("token", last, 0, 256)
+        for e in range(E):
+            interleave("scalar", "slot", last, C * e, C * (e + 1))
+        for e in range(E):
+            quantise_x("slot", last, C * e, C * (e + 1))
+            first_layer("slot", 2 * e, last)
+            first_layer("slot", 2 * e + 1, last)
+        interleave("scalar", "token", last, 256, T)
+        for block in range(2):
             first_layer("token", block, last)
-            relu("scalar", "token", block)
-        interleave("vector", "token", 2, 0, SPLIT)
-        quantise_x("slot", last, C, S)
-        quantise_x("token", 2, 0, SPLIT)
-        for block in (0, 1, 3):
-            first_layer("slot", block, last)
-        for s in range(last):
-            first_layer("slot", 2, s)
-        for block in (0, 1, 3):
-            relu("vector" if block == 3 else "scalar", "slot", block)
-        for b in range(2):
-            turn("token", 4 + b)
-            turn("slot", b)
-        spread("token", 2)
-        spread("slot", 0)
-        quantise_x("token", 0, 0, SPLIT)
-        first_layer("slot", 2, last)
-        interleave("vector", "token", 1, 0, SPLIT)
-        relu("vector", "slot", 2)
-        quantise_x("token", 1, 0, SPLIT)
-
-        for block in range(4):
-            first_layer("token", block, 0)
-        for block in (2, 3):
-            turn("slot", block)
-        quantise_h("slot", 0)
-        quantise_h("token", 2)
-        spread("slot", 1)
-        for block in (2, 3):
-            first_layer("token", block, 1)
-        second_layer("slot", 0)
-        take_y(0)
-        quantise_h("slot", 1)
-        scatter(0)
-        for block in (2, 3):
-            first_layer("token", block, 2)
-            relu("scalar", "token", block)
-        second_layer("slot", 1)
-        for block in (0, 1):
-            first_layer("token", block, 1)
-            first_layer("token", block, 2)
-        take_y(1)
-        scatter(1)
-        second_layer("token", 2)
-
-        for block in (0, 1):
-            relu("scalar", "token", block)
-        for block in (2, 3, 0, 1):
-            turn("token", block)
-        spread("token", 1)
-        spread("token", 0)
-        quantise_h("token", 1)
-        finish(2)
-        second_layer("token", 1)
-        quantise_h("token", 0)
-        finish(1)
-        second_layer("token", 0)
-        finish(0)
+        for e in range(E):
+            relu("scalar", "slot", 2 * e)
+            relu("vector", "slot", 2 * e + 1)
+            turn("slot", 2 * e)
+            turn("slot", 2 * e + 1)
+            spread("scalar", "slot", e)
+            quantise_h("slot", e)
+            second_layer("slot", e)
+            take_y("scalar", e)
+        for s in range(PASSES - 1):
+            interleave("scalar", "token", s, 512, T)
+        quantise_x("token", last, 256, T)
+        for block in range(2, 4):
+            first_layer("token", block, last)
+        for s in range(PASSES - 1):
+            quantise_x("token", s, 512, T)
+        for block in (4, 5):
+            for s in range(PASSES):
+                first_layer("token", block, s)
+        for unit in range(3):
+            relu("vector" if unit == 0 else "scalar", "token", 2 * unit)
+            relu("vector" if unit == 0 else "scalar", "token", 2 * unit + 1)
+            turn("token", 2 * unit)
+            turn("token", 2 * unit + 1)
+        for unit in range(3):
+            spread("scalar", "token", unit)
+            quantise_h("token", unit)
+        for unit in range(3):
+            second_layer("token", unit)
+        for e in range(E):
+            scatter(e)
+        for unit in range(3):
+            finish(unit)

@@ -32,17 +32,20 @@ BANK = {("slot", 0): 0, ("slot", 1): 1, ("slot", 2): 2, ("slot", 3): 3, ("token"
 
 
 def staging(kind, s, first):
+    if kind == "token":
+        unit = first // 256
+        return (("token", s, 0), ("raw", 4, 256 * s), ("raw", 5, 256 * s))[unit]
     return kind, s, first
 
 
 def y_bank(kind, unit):
     if kind == "token" and unit < 2:
-        return (3, 7)[unit]
+        return 3
     return BANK[kind, 2 * unit]
 
 
 def h_slot(kind, block):
-    return block % 4
+    return kind, block
 
 
 def tile_moe_shr_mlp_relu_kernel(
@@ -67,10 +70,11 @@ def tile_moe_shr_mlp_relu_kernel(
         quads, codes, planes = {}, {}, {}
         for s in range(PASSES):
             for u in range(2):
-                x_raw[s, u] = keep.tile([P, 2, T], F32, name=f"x_raw{s}{u}")
-            w1_codes[s] = keep.tile([P, (E + 1) * 2 * H], U8, align_bytes=64, name=f"w1_codes{s}")
+                x_raw[s, u] = keep.tile([P, 2 * T], F32, align_bytes=64, name=f"x_raw{s}{u}")
             x_pairs[s] = keep.tile([P, 2 * T * 2], BF16, align_bytes=64, name=f"x_pairs{s}")
             slot_pairs[s] = keep.tile([P, 2 * S * 2], BF16, align_bytes=64, name=f"slot_pairs{s}")
+        for e in range(E + 1):
+            w1_codes[e] = keep.tile([P, PASSES * 2 * H], U8, align_bytes=64, name=f"w1_codes{e}")
         h_rows, h_quads, h_codes, h_planes = {}, {}, {}, {}
         for kind, n in (("slot", S), ("token", T)):
             for s in range(PASSES):
@@ -98,29 +102,29 @@ def tile_moe_shr_mlp_relu_kernel(
 
         def load_x(s, u, first, end):
             rows = xT[K_PASS * s : K_PASS * (s + 1), :].rearrange("(p d) t -> p d t", d=4)
-            nc.sync.dma_start(x_raw[s, u][:, :, first:end], rows[:, 2 * u : 2 * u + 2, first:end])
+            nc.sync.dma_start(x_raw[s, u][:].rearrange("p (d t) -> p d t", d=2)[:, :, first:end], rows[:, 2 * u : 2 * u + 2, first:end])
 
         def load_offsets():
             nc.sync.dma_start(offsets[:], offs)
 
-        def load_w1(s, first, end):
+        def load_w1_expert(e):
             nc.sync.dma_start(
-                w1_codes[s][:, 2 * H * first : 2 * H * end].bitcast(I32).rearrange("p (e b) -> p e b", b=H // 2),
-                w1_words.bitcast(I32)[first:end, s].rearrange("e p b -> p e b"),
+                w1_codes[e][:].bitcast(I32).rearrange("p (s b) -> p s b", s=PASSES),
+                w1_words.bitcast(I32)[e].rearrange("s p b -> p s b"),
             )
 
         def load_w1_scales(queue, first, end):
-            engine = nc.gpsimd if queue == "gpsimd" else nc.sync
-            for q in range(QUADRANTS):
+            planes_of = w1_plane_words.rearrange("p (e s i) -> p e s i", s=PASSES, i=H // 4)
+            for r in range(4):
                 if end - first == 1:
-                    engine.dma_start(
-                        w1_plane_words.rearrange("p (e s i) -> p e s i", s=PASSES, i=H // 4)[32 * q : 32 * q + 4, :, first],
-                        w1_scales.bitcast(I32)[:, first, 4 * q : 4 * q + 4, :].rearrange("e q i -> q e i"),
+                    nc.sync.dma_start(
+                        planes_of[r:P:32, :, first],
+                        w1_scales.bitcast(I32)[:, first, r:16:4, :].rearrange("e q i -> q e i"),
                     )
                 else:
-                    engine.dma_start(
-                        w1_plane_words.rearrange("p (a i) -> p a i", i=H // 4)[32 * q : 32 * q + 4],
-                        w1_scales.bitcast(I32)[:, :, 4 * q : 4 * q + 4, :].rearrange("e s q i -> q (e s) i"),
+                    nc.sync.dma_start(
+                        w1_plane_words.rearrange("p (a i) -> p a i", i=H // 4)[r:P:32],
+                        w1_scales.bitcast(I32)[:, :, r:16:4, :].rearrange("e s q i -> q (e s) i"),
                     )
 
         def load_rest():
@@ -128,25 +132,23 @@ def tile_moe_shr_mlp_relu_kernel(
                 w2_codes[:].rearrange("p e b -> p (e b)").bitcast(I32).rearrange("p (e b) -> p e b", e=E + 1),
                 w2_words.bitcast(I32)[:, 0].rearrange("e p b -> p e b"),
             )
-            for q in range(QUADRANTS):
+            for r in range(4):
                 nc.sync.dma_start(
-                    w2_plane_words.rearrange("p (a i) -> p a i", i=N // 4)[32 * q : 32 * q + 4],
-                    w2_scales.bitcast(I32)[:, 0, 4 * q : 4 * q + 4, :].rearrange("e q i -> q e i"),
+                    w2_plane_words.rearrange("p (a i) -> p a i", i=N // 4)[r:P:32],
+                    w2_scales.bitcast(I32)[:, 0, r:16:4, :].rearrange("e q i -> q e i"),
                 )
             nc.sync.dma_start(gate_sb[:], gate)
 
-        for first in range(0, T, UNIT):
-            load_x(0, 0, first, first + UNIT)
+        load_x(0, 0, 0, T)
         load_offsets()
         load_x(0, 1, 0, T)
         load_x(1, 0, 0, T)
         load_x(1, 1, 0, T)
-        load_w1_scales("sync", 0, PASSES)
-        load_w1(0, 0, E + 1)
         load_x(2, 0, 0, T)
+        load_w1_scales("sync", 0, PASSES)
         load_x(2, 1, 0, T)
-        load_w1(1, 0, E + 1)
-        load_w1(2, 0, E + 1)
+        for e in (0, SHARED, 1):
+            load_w1_expert(e)
         load_rest()
 
         def copy(engine, dst, src):
@@ -159,7 +161,7 @@ def tile_moe_shr_mlp_relu_kernel(
             copy(
                 engine,
                 x_pairs[s][:, 2 * (T * u + first) : 2 * (T * u + end)].rearrange("p (t d) -> p t d", d=2),
-                x_raw[s, u][:, :, first:end].rearrange("p d t -> p t d"),
+                x_raw[s, u][:].rearrange("p (d t) -> p t d", d=2)[:, first:end],
             )
 
         def gather(s, u, first, end):
@@ -170,6 +172,10 @@ def tile_moe_shr_mlp_relu_kernel(
 
         def staged(kind, s, first, end):
             kind2, s2, first2 = staging(kind, s, first)
+            if kind2 == "raw":
+                return x_raw[s2 // 2, s2 % 2][:].bitcast(BF16)[:, 4 * first2 : 4 * (first2 + end - first)]
+            if kind2 == "sp":
+                return slot_pairs[s2][:, 4 * first2 : 4 * (first2 + end - first)]
             return quads[kind2, s2][:, 4 * first2 : 4 * (first2 + end - first)]
 
         def interleave(engine, kind, s, first, end):
@@ -205,7 +211,7 @@ def tile_moe_shr_mlp_relu_kernel(
                 out=sums[kind, block][:],
                 lhsT=codes[kind, s][:, columns].bitcast(FP8X4),
                 lhsT_scale=planes[kind, s][:, columns],
-                rhs=w1_codes[s][:, 2 * H * e : 2 * H * (e + 1)].bitcast(FP4X4),
+                rhs=w1_codes[e][:, 2 * H * s : 2 * H * (s + 1)].bitcast(FP4X4),
                 rhs_scale=w1_planes[:, e * PASSES + s, :],
                 start=(s == 0),
                 stop=(s == PASSES - 1),
@@ -250,9 +256,15 @@ def tile_moe_shr_mlp_relu_kernel(
 
         def second_layer(kind, unit):
             e = expert_of(kind, 2 * unit)
-            y[kind, unit] = psum.tile([P, UNIT], F32, tag=f"bank{y_bank(kind, unit)}", bufs=1, name="y")
+            if (kind, unit) == ("token", 1) and y_bank(kind, 0) == y_bank(kind, 1):
+                y[kind, unit] = y["pair"][:, UNIT:]
+            elif (kind, unit) == ("token", 0):
+                y["pair"] = psum.tile([P, 2 * UNIT], F32, tag=f"bank{y_bank(kind, unit)}", bufs=1, name="y")
+                y[kind, unit] = y["pair"][:, :UNIT]
+            else:
+                y[kind, unit] = psum.tile([P, UNIT], F32, tag=f"bank{y_bank(kind, unit)}", bufs=1, name="y")[:]
             nc.tensor.matmul_mx(
-                out=y[kind, unit][:],
+                out=y[kind, unit],
                 lhsT=w2_codes[:, e, :].bitcast(FP4X4),
                 lhsT_scale=w2_planes[:, e, :],
                 rhs=h_codes[kind, unit][:].bitcast(FP8X4),
@@ -262,7 +274,7 @@ def tile_moe_shr_mlp_relu_kernel(
             )
 
         def take_y(engine, unit):
-            copy(engine, routed_y[:, unit_columns(unit)], y["slot", unit][:])
+            copy(engine, routed_y[:, unit_columns(unit)], y["slot", unit])
 
         def scatter(unit):
             columns = unit_columns(unit)
@@ -275,54 +287,28 @@ def tile_moe_shr_mlp_relu_kernel(
 
         def finish(unit):
             columns = unit_columns(unit)
-            nc.vector.tensor_tensor(result[:, columns], y["token", unit][:], routed[:, columns], ADD)
+            nc.vector.tensor_tensor(result[:, columns], y["token", unit], routed[:, columns], ADD)
             nc.sync.dma_start(out[:, columns], result[:, columns])
 
-        slots = [("slot", b) for b in range(4)]
-        tokens = [("token", b) for b in range(4)]
         last = PASSES - 1
-        round_x("scalar", 0, 0, 0, 256)
-        round_x("scalar", 0, 0, 256, 512)
-        round_x("vector", 0, 0, 512, T)
-        gather(0, 0, 0, S)
-        round_x("scalar", 0, 1, 0, 256)
-        round_x("vector", 0, 1, 256, T)
-        gather(0, 1, 0, S)
-        interleave("scalar", "token", 0, 0, 512)
-        round_x("scalar", 1, 0, 0, T)
-        gather(1, 0, 0, S)
-        round_x("scalar", 1, 1, 0, 512)
-        round_x("vector", 1, 1, 512, T)
-        gather(1, 1, 0, S)
-        interleave("vector", "slot", 0, 0, S)
-        quantise_x("slot", 0, 0, S)
-        quantise_x("token", 0, 0, 512)
-        for kind, block in slots + tokens:
-            first_layer(kind, block, 0)
-        round_x("scalar", 2, 0, 0, 256)
-        round_x("vector", 2, 0, 256, T)
-        gather(2, 0, 0, S)
-        interleave("scalar", "slot", 1, 0, S)
-        quantise_x("slot", 1, 0, S)
-        round_x("scalar", last, 1, 0, 512)
-        round_x("vector", last, 1, 512, T)
-        interleave("scalar", "token", 1, 0, 512)
-        quantise_x("token", 1, 0, 512)
-        for kind, block in slots + tokens:
-            first_layer(kind, block, 1)
+        for s in range(PASSES):
+            for u in range(2):
+                split = 256 if s == 0 else 512 if (s, u) == (last, 1) else T
+                round_x("scalar", s, u, 0, split)
+                if split < T:
+                    round_x("vector", s, u, split, T)
+                if u == 0:
+                    gather(s, 0, 0, S)
+            for e in range(E):
+                gather(s, 1, C * e, C * (e + 1))
+            for e in range(E):
+                interleave("vector", "slot", s, C * e, C * (e + 1))
+            for e in range(E):
+                quantise_x("slot", s, C * e, C * (e + 1))
         for e in range(E):
-            gather(last, 1, C * e, C * (e + 1))
-        interleave("scalar", "token", last, 0, 256)
-        quantise_x("token", last, 0, 256)
-        for e in range(E):
-            interleave("scalar", "slot", last, C * e, C * (e + 1))
-        for e in range(E):
-            quantise_x("slot", last, C * e, C * (e + 1))
-            first_layer("slot", 2 * e, last)
-            first_layer("slot", 2 * e + 1, last)
-        interleave("scalar", "token", last, 256, T)
-        for block in range(2):
-            first_layer("token", block, last)
+            for s in range(PASSES):
+                first_layer("slot", 2 * e, s)
+                first_layer("slot", 2 * e + 1, s)
         for e in range(E):
             relu("scalar", "slot", 2 * e)
             relu("vector", "slot", 2 * e + 1)
@@ -332,19 +318,16 @@ def tile_moe_shr_mlp_relu_kernel(
             quantise_h("slot", e)
             second_layer("slot", e)
             take_y("scalar", e)
-        for s in range(PASSES - 1):
-            interleave("scalar", "token", s, 512, T)
-        quantise_x("token", last, 256, T)
-        for block in range(2, 4):
-            first_layer("token", block, last)
-        for s in range(PASSES - 1):
-            quantise_x("token", s, 512, T)
-        for block in (4, 5):
-            for s in range(PASSES):
-                first_layer("token", block, s)
         for unit in range(3):
-            relu("vector" if unit == 0 else "scalar", "token", 2 * unit)
-            relu("vector" if unit == 0 else "scalar", "token", 2 * unit + 1)
+            for s in range(PASSES):
+                interleave("scalar", "token", s, UNIT * unit, UNIT * (unit + 1))
+                quantise_x("token", s, UNIT * unit, UNIT * (unit + 1))
+            for block in (2 * unit, 2 * unit + 1):
+                for s in range(PASSES):
+                    first_layer("token", block, s)
+        for unit in range(3):
+            relu("scalar", "token", 2 * unit)
+            relu("scalar", "token", 2 * unit + 1)
             turn("token", 2 * unit)
             turn("token", 2 * unit + 1)
         for unit in range(3):

@@ -28,7 +28,7 @@ RELU = mybir.ActivationFunctionType.Relu
 MULT = mybir.AluOpType.mult
 ADD = mybir.AluOpType.add
 
-BANK = {("slot", 0): 0, ("slot", 1): 1, ("slot", 2): 2, ("slot", 3): 3, ("token", 0): 4, ("token", 1): 5, ("token", 2): 6, ("token", 3): 7, ("token", 4): 1, ("token", 5): 3}
+BANK = {("slot", 0): 0, ("slot", 1): 1, ("slot", 2): 2, ("slot", 3): 3, ("token", 0): 4, ("token", 1): 5, ("token", 2): 6, ("token", 3): 7, ("token", 4): 0, ("token", 5): 2}
 
 
 def staging(kind, s, first):
@@ -40,12 +40,16 @@ def staging(kind, s, first):
 
 def y_bank(kind, unit):
     if kind == "token" and unit < 2:
-        return 3
-    return BANK[kind, 2 * unit]
+        return 0
+    return t_bank(kind, unit)
 
 
 def h_slot(kind, block):
     return kind, block
+
+
+def t_bank(kind, unit):
+    return BANK[kind, 2 * unit + 1]
 
 
 def tile_moe_shr_mlp_relu_kernel(
@@ -139,15 +143,18 @@ def tile_moe_shr_mlp_relu_kernel(
                 )
             nc.sync.dma_start(gate_sb[:], gate)
 
-        load_x(0, 0, 0, T)
+        load_x(0, 0, 0, 2 * UNIT)
+        load_x(0, 0, 2 * UNIT, T)
         load_offsets()
-        load_x(0, 1, 0, T)
+        load_x(0, 1, UNIT, T)
+        load_x(0, 1, 0, UNIT)
         load_x(1, 0, 0, T)
         load_x(1, 1, 0, T)
         load_x(2, 0, 0, T)
-        load_w1_scales("sync", 0, PASSES)
         load_x(2, 1, 0, T)
-        for e in (0, SHARED, 1):
+        load_w1_expert(0)
+        load_w1_scales("sync", 0, PASSES)
+        for e in (1, SHARED):
             load_w1_expert(e)
         load_rest()
 
@@ -230,7 +237,7 @@ def tile_moe_shr_mlp_relu_kernel(
         def turn(kind, block):
             unit, b = divmod(block, 2)
             if b == 0:
-                turned[kind, unit] = in_bank(kind, block, [P, 2, 2, P], "turned")
+                turned[kind, unit] = psum.tile([P, 2, 2, P], F32, tag=f"bank{t_bank(kind, unit)}", bufs=1, name="turned")
             words = h_rows[h_slot(kind, block)][:].bitcast(F32)
             for u in range(2):
                 nc.tensor.transpose(turned[kind, unit][:, b, u, :], words[:, P * u : P * (u + 1)], ident[:])
@@ -293,10 +300,15 @@ def tile_moe_shr_mlp_relu_kernel(
         last = PASSES - 1
         for s in range(PASSES):
             for u in range(2):
-                split = 256 if s == 0 else 512 if (s, u) == (last, 1) else T
-                round_x("scalar", s, u, 0, split)
-                if split < T:
-                    round_x("vector", s, u, split, T)
+                if (s, u) == (0, 0):
+                    round_x("scalar", s, u, 0, UNIT)
+                    round_x("vector", s, u, UNIT, 2 * UNIT)
+                    round_x("vector", s, u, 2 * UNIT, T)
+                elif s == 0:
+                    round_x("scalar", s, u, UNIT, T)
+                    round_x("vector", s, u, 0, UNIT)
+                else:
+                    round_x("scalar", s, u, 0, T)
                 if u == 0:
                     gather(s, 0, 0, S)
             for e in range(E):
@@ -306,12 +318,14 @@ def tile_moe_shr_mlp_relu_kernel(
             for e in range(E):
                 quantise_x("slot", s, C * e, C * (e + 1))
         for e in range(E):
-            for s in range(PASSES):
+            for s in range(last):
                 first_layer("slot", 2 * e, s)
                 first_layer("slot", 2 * e + 1, s)
+        for block in range(4):
+            first_layer("slot", block, last)
         for e in range(E):
             relu("scalar", "slot", 2 * e)
-            relu("vector", "slot", 2 * e + 1)
+            relu("scalar", "slot", 2 * e + 1)
             turn("slot", 2 * e)
             turn("slot", 2 * e + 1)
             spread("scalar", "slot", e)
@@ -320,18 +334,21 @@ def tile_moe_shr_mlp_relu_kernel(
             take_y("scalar", e)
         for unit in range(3):
             for s in range(PASSES):
-                interleave("scalar", "token", s, UNIT * unit, UNIT * (unit + 1))
-                quantise_x("token", s, UNIT * unit, UNIT * (unit + 1))
+                if (unit, s) == (1, 0):
+                    continue
+                end = 2 * UNIT if (unit, s) == (0, 0) else UNIT * (unit + 1)
+                interleave("scalar", "token", s, UNIT * unit, end)
+                quantise_x("token", s, UNIT * unit, end)
             for block in (2 * unit, 2 * unit + 1):
                 for s in range(PASSES):
                     first_layer("token", block, s)
         for unit in range(3):
-            relu("scalar", "token", 2 * unit)
-            relu("scalar", "token", 2 * unit + 1)
+            relu("vector" if unit == 0 else "scalar", "token", 2 * unit)
+            relu("vector" if unit == 0 else "scalar", "token", 2 * unit + 1)
             turn("token", 2 * unit)
             turn("token", 2 * unit + 1)
         for unit in range(3):
-            spread("scalar", "token", unit)
+            spread("vector" if unit == 1 else "scalar", "token", unit)
             quantise_h("token", unit)
         for unit in range(3):
             second_layer("token", unit)

@@ -143,11 +143,9 @@ def tile_moe_shr_mlp_relu_kernel(
                 )
             nc.sync.dma_start(gate_sb[:], gate)
 
-        load_x(0, 0, 0, 2 * UNIT)
-        load_x(0, 0, 2 * UNIT, T)
+        load_x(0, 0, 0, T)
         load_offsets()
-        load_x(0, 1, UNIT, T)
-        load_x(0, 1, 0, UNIT)
+        load_x(0, 1, 0, T)
         load_x(1, 0, 0, T)
         load_x(1, 1, 0, T)
         load_x(2, 0, 0, T)
@@ -222,6 +220,18 @@ def tile_moe_shr_mlp_relu_kernel(
                 rhs_scale=w1_planes[:, e * PASSES + s, :],
                 start=(s == 0),
                 stop=(s == PASSES - 1),
+            )
+
+        def warm_up():
+            unread = psum.tile([P, H], F32, tag=f"bank{BANK['token', 3]}", bufs=1, name="unread")
+            nc.tensor.matmul_mx(
+                out=unread[:],
+                lhsT=codes["slot", 0][:, :P].bitcast(FP8X4),
+                lhsT_scale=planes["slot", 0][:, :P],
+                rhs=w1_codes[0][:, : 2 * H].bitcast(FP4X4),
+                rhs_scale=planes["slot", 0][:],
+                start=True,
+                stop=True,
             )
 
         def relu(engine, kind, block):
@@ -300,13 +310,9 @@ def tile_moe_shr_mlp_relu_kernel(
         last = PASSES - 1
         for s in range(PASSES):
             for u in range(2):
-                if (s, u) == (0, 0):
+                if s == 0:
                     round_x("scalar", s, u, 0, UNIT)
-                    round_x("vector", s, u, UNIT, 2 * UNIT)
-                    round_x("vector", s, u, 2 * UNIT, T)
-                elif s == 0:
-                    round_x("scalar", s, u, UNIT, T)
-                    round_x("vector", s, u, 0, UNIT)
+                    round_x("vector", s, u, UNIT, T)
                 else:
                     round_x("scalar", s, u, 0, T)
                 if u == 0:
@@ -317,6 +323,8 @@ def tile_moe_shr_mlp_relu_kernel(
                 interleave("vector", "slot", s, C * e, C * (e + 1))
             for e in range(E):
                 quantise_x("slot", s, C * e, C * (e + 1))
+        for repeat in range(3):
+            warm_up()
         for e in range(E):
             for s in range(last):
                 first_layer("slot", 2 * e, s)

@@ -32,9 +32,8 @@ BANK = {("slot", 0): 0, ("slot", 1): 1, ("slot", 2): 2, ("slot", 3): 3, ("token"
 
 
 def staging(kind, s, first):
-    if kind == "token":
-        unit = first // 256
-        return (("token", s, 0), ("raw", 4, 256 * s), ("raw", 5, 256 * s))[unit]
+    if kind == "token" and (first, s) in ((256, 1), (512, 0), (512, 1)):
+        return "raw", 5, {(256, 1): 0, (512, 0): 256, (512, 1): 512}[first, s]
     return kind, s, first
 
 
@@ -77,8 +76,9 @@ def tile_moe_shr_mlp_relu_kernel(
                 x_raw[s, u] = keep.tile([P, 2 * T], F32, align_bytes=64, name=f"x_raw{s}{u}")
             x_pairs[s] = keep.tile([P, 2 * T * 2], BF16, align_bytes=64, name=f"x_pairs{s}")
             slot_pairs[s] = keep.tile([P, 2 * S * 2], BF16, align_bytes=64, name=f"slot_pairs{s}")
-        for e in range(E + 1):
-            w1_codes[e] = keep.tile([P, PASSES * 2 * H], U8, align_bytes=64, name=f"w1_codes{e}")
+        for s in range(PASSES):
+            w1_codes[s] = keep.tile([P, E * 2 * H], U8, align_bytes=64, name=f"w1_codes{s}")
+        w1_shared = keep.tile([P, PASSES * 2 * H], U8, align_bytes=64, name="w1_shared")
         h_rows, h_quads, h_codes, h_planes = {}, {}, {}, {}
         for kind, n in (("slot", S), ("token", T)):
             for s in range(PASSES):
@@ -111,9 +111,15 @@ def tile_moe_shr_mlp_relu_kernel(
         def load_offsets():
             nc.sync.dma_start(offsets[:], offs)
 
+        def load_w1(s, first, end):
+            nc.sync.dma_start(
+                w1_codes[s][:].bitcast(I32).rearrange("p (e b) -> p e b", e=E),
+                w1_words.bitcast(I32)[first:end, s].rearrange("e p b -> p e b"),
+            )
+
         def load_w1_expert(e):
             nc.sync.dma_start(
-                w1_codes[e][:].bitcast(I32).rearrange("p (s b) -> p s b", s=PASSES),
+                w1_shared[:].bitcast(I32).rearrange("p (s b) -> p s b", s=PASSES),
                 w1_words.bitcast(I32)[e].rearrange("s p b -> p s b"),
             )
 
@@ -149,11 +155,11 @@ def tile_moe_shr_mlp_relu_kernel(
         load_x(1, 0, 0, T)
         load_x(1, 1, 0, T)
         load_x(2, 0, 0, T)
-        load_x(2, 1, 0, T)
-        load_w1_expert(0)
         load_w1_scales("sync", 0, PASSES)
-        for e in (1, SHARED):
-            load_w1_expert(e)
+        load_x(2, 1, 0, T)
+        for s in range(PASSES):
+            load_w1(s, 0, E)
+        load_w1_expert(SHARED)
         load_rest()
 
         def copy(engine, dst, src):
@@ -216,22 +222,10 @@ def tile_moe_shr_mlp_relu_kernel(
                 out=sums[kind, block][:],
                 lhsT=codes[kind, s][:, columns].bitcast(FP8X4),
                 lhsT_scale=planes[kind, s][:, columns],
-                rhs=w1_codes[e][:, 2 * H * s : 2 * H * (s + 1)].bitcast(FP4X4),
+                rhs=(w1_shared[:, 2 * H * s : 2 * H * (s + 1)] if e == SHARED else w1_codes[s][:, 2 * H * e : 2 * H * (e + 1)]).bitcast(FP4X4),
                 rhs_scale=w1_planes[:, e * PASSES + s, :],
                 start=(s == 0),
                 stop=(s == PASSES - 1),
-            )
-
-        def warm_up():
-            unread = psum.tile([P, H], F32, tag=f"bank{BANK['token', 3]}", bufs=1, name="unread")
-            nc.tensor.matmul_mx(
-                out=unread[:],
-                lhsT=codes["slot", 0][:, :P].bitcast(FP8X4),
-                lhsT_scale=planes["slot", 0][:, :P],
-                rhs=w1_codes[0][:, : 2 * H].bitcast(FP4X4),
-                rhs_scale=planes["slot", 0][:],
-                start=True,
-                stop=True,
             )
 
         def relu(engine, kind, block):
@@ -308,8 +302,11 @@ def tile_moe_shr_mlp_relu_kernel(
             nc.sync.dma_start(out[:, columns], result[:, columns])
 
         last = PASSES - 1
+        EARLY = ((0, 1),)
         for s in range(PASSES):
             for u in range(2):
+                if (s, u) == (last, 1):
+                    interleave("scalar", "token", 1, 0, 1 * UNIT)
                 if s == 0:
                     round_x("scalar", s, u, 0, UNIT)
                     round_x("vector", s, u, UNIT, T)
@@ -323,14 +320,9 @@ def tile_moe_shr_mlp_relu_kernel(
                 interleave("vector", "slot", s, C * e, C * (e + 1))
             for e in range(E):
                 quantise_x("slot", s, C * e, C * (e + 1))
-        for repeat in range(3):
-            warm_up()
-        for e in range(E):
-            for s in range(last):
-                first_layer("slot", 2 * e, s)
-                first_layer("slot", 2 * e + 1, s)
-        for block in range(4):
-            first_layer("slot", block, last)
+        for s in range(PASSES):
+            for block in range(4):
+                first_layer("slot", block, s)
         for e in range(E):
             relu("scalar", "slot", 2 * e)
             relu("scalar", "slot", 2 * e + 1)
@@ -345,7 +337,8 @@ def tile_moe_shr_mlp_relu_kernel(
                 if (unit, s) == (1, 0):
                     continue
                 end = 2 * UNIT if (unit, s) == (0, 0) else UNIT * (unit + 1)
-                interleave("scalar", "token", s, UNIT * unit, end)
+                if (unit, s) not in EARLY:
+                    interleave("scalar", "token", s, UNIT * unit, end)
                 quantise_x("token", s, UNIT * unit, end)
             for block in (2 * unit, 2 * unit + 1):
                 for s in range(PASSES):
@@ -356,7 +349,7 @@ def tile_moe_shr_mlp_relu_kernel(
             turn("token", 2 * unit)
             turn("token", 2 * unit + 1)
         for unit in range(3):
-            spread("vector" if unit == 1 else "scalar", "token", unit)
+            spread("scalar", "token", unit)
             quantise_h("token", unit)
         for unit in range(3):
             second_layer("token", unit)

@@ -28,33 +28,17 @@ RELU = mybir.ActivationFunctionType.Relu
 MULT = mybir.AluOpType.mult
 ADD = mybir.AluOpType.add
 
+
+EARLY = 4 * P
 BANK = {("slot", 0): 0, ("slot", 1): 1, ("slot", 2): 2, ("slot", 3): 3, ("token", 0): 4, ("token", 1): 5, ("token", 2): 6, ("token", 3): 7, ("token", 4): 0, ("token", 5): 2}
-
-
-def staging(kind, s, first):
-    if kind == "token" and (first, s) in ((256, 1), (512, 0), (512, 1)):
-        return "raw", 5, {(256, 1): 0, (512, 0): 256, (512, 1): 512}[first, s]
-    return kind, s, first
-
-
-def y_bank(kind, unit):
-    if kind == "token" and unit < 2:
-        return 0
-    return t_bank(kind, unit)
-
-
-def h_slot(kind, block):
-    return kind, block
-
-
-def t_bank(kind, unit):
-    return BANK[kind, 2 * unit + 1]
+UNITS = {"e0": ("slot", 0, 2, 1, 1), "e1": ("slot", 2, 2, 3, 3), "t0": ("token", 0, 2, 5, 2), "t1": ("token", 2, 2, 7, 2), "t2": ("token", 4, 2, 2, 4)}
 
 
 def tile_moe_shr_mlp_relu_kernel(
     tc, xT, w1_words, w1_scales, w2_words, w2_scales, gate, offs, out
 ):
     nc = tc.nc
+    last = PASSES - 1
     with ExitStack() as ctx:
         keep = ctx.enter_context(tc.tile_pool(name="keep", bufs=1))
         psum = ctx.enter_context(tc.psum_pool(name="psum", bufs=1))
@@ -62,7 +46,8 @@ def tile_moe_shr_mlp_relu_kernel(
         offsets = keep.tile([P, S // 16], U16, name="offsets")
         gate_sb = keep.tile([P, S], F32, name="gate_sb")
         w2_codes = keep.tile([P, E + 1, 2 * N], U8, align_bytes=64, name="w2_codes")
-        w1_planes = keep.tile([P, (E + 1) * PASSES, H], U8, align_bytes=64, name="w1_planes")
+        shared_planes = keep.tile([P, PASSES * H], U8, align_bytes=64, name="shared_planes")
+        routed_planes = keep.tile([P, E * PASSES * H], U8, align_bytes=64, name="routed_planes")
         w2_planes = keep.tile([P, E + 1, N], U8, align_bytes=64, name="w2_planes")
         ident = keep.tile([P, P], F32, name="ident")
         routed = keep.tile([P, T], F32, name="routed")
@@ -76,66 +61,56 @@ def tile_moe_shr_mlp_relu_kernel(
                 x_raw[s, u] = keep.tile([P, 2 * T], F32, align_bytes=64, name=f"x_raw{s}{u}")
             x_pairs[s] = keep.tile([P, 2 * T * 2], BF16, align_bytes=64, name=f"x_pairs{s}")
             slot_pairs[s] = keep.tile([P, 2 * S * 2], BF16, align_bytes=64, name=f"slot_pairs{s}")
-        for s in range(PASSES):
             w1_codes[s] = keep.tile([P, E * 2 * H], U8, align_bytes=64, name=f"w1_codes{s}")
+        late_codes = keep.tile([P, 2 * UNIT], U32, align_bytes=64, name="late_codes")
         w1_shared = keep.tile([P, PASSES * 2 * H], U8, align_bytes=64, name="w1_shared")
         h_rows, h_quads, h_codes, h_planes = {}, {}, {}, {}
         for kind, n in (("slot", S), ("token", T)):
             for s in range(PASSES):
-                quads[kind, s] = keep.tile([P, n * 4], BF16, align_bytes=64, name=f"{kind}_quads{s}")
+                quads[kind, s] = keep.tile([P, S * 4], BF16, align_bytes=64, name=f"{kind}_quads{s}")
                 codes[kind, s] = keep.tile([P, n], U32, align_bytes=64, name=f"{kind}_codes{s}")
                 planes[kind, s] = keep.tile([P, n], U8, align_bytes=64, name=f"{kind}_planes{s}")
             for block in range(n // P):
-                if h_slot(kind, block) not in h_rows:
-                    h_rows[h_slot(kind, block)] = keep.tile([P, H], BF16, align_bytes=64, name=f"{kind}_h_rows{block}")
-            for unit in range(n // UNIT):
-                h_quads[kind, unit] = keep.tile([P, UNIT * 4], BF16, align_bytes=64, name=f"{kind}_h_quads{unit}")
-                h_codes[kind, unit] = keep.tile([P, UNIT], U32, align_bytes=64, name=f"{kind}_h_codes{unit}")
-                h_planes[kind, unit] = keep.tile([P, UNIT], U8, align_bytes=64, name=f"{kind}_h_planes{unit}")
+                h_rows[kind, block] = keep.tile([P, H], BF16, align_bytes=64, name=f"{kind}_h_rows{block}")
+        for unit, (kind, first, blocks, tb, yb) in UNITS.items():
+            h_quads[unit] = keep.tile([P, blocks * P * 4], BF16, align_bytes=64, name=f"h_quads{unit}")
+            h_codes[unit] = keep.tile([P, blocks * P], U32, align_bytes=64, name=f"h_codes{unit}")
+            h_planes[unit] = keep.tile([P, blocks * P], U8, align_bytes=64, name=f"h_planes{unit}")
 
+        shared_words = shared_planes[:].bitcast(I32)
+        routed_words = routed_planes[:].bitcast(I32)
+        w2_plane_words = w2_planes[:].rearrange("p a i -> p (a i)").bitcast(I32)
+        nc.vector.memset(shared_words, 0)
         warm = keep.tile([P, 1], F32, name="warm")
         nc.vector.memset(warm[:], 0.0)
         nc.scalar.activation(warm[:], warm[:], RELU)
-
-        w1_plane_words = w1_planes[:].rearrange("p a i -> p (a i)").bitcast(I32)
-        w2_plane_words = w2_planes[:].rearrange("p a i -> p (a i)").bitcast(I32)
         make_identity(nc, ident[:])
-        nc.vector.memset(w1_plane_words, 0)
+        nc.vector.memset(routed_words, 0)
         nc.vector.memset(w2_plane_words, 0)
         nc.vector.memset(routed[:], 0.0)
 
-        def load_x(s, u, first, end):
+        def load_x(s, u, first=0, end=T):
             rows = xT[K_PASS * s : K_PASS * (s + 1), :].rearrange("(p d) t -> p d t", d=4)
             nc.sync.dma_start(x_raw[s, u][:].rearrange("p (d t) -> p d t", d=2)[:, :, first:end], rows[:, 2 * u : 2 * u + 2, first:end])
 
-        def load_offsets():
-            nc.sync.dma_start(offsets[:], offs)
-
-        def load_w1(s, first, end):
+        def load_routed(s):
             nc.sync.dma_start(
                 w1_codes[s][:].bitcast(I32).rearrange("p (e b) -> p e b", e=E),
-                w1_words.bitcast(I32)[first:end, s].rearrange("e p b -> p e b"),
+                w1_words.bitcast(I32)[0:E, s].rearrange("e p b -> p e b"),
             )
 
-        def load_w1_expert(e):
+        def load_shared():
             nc.sync.dma_start(
                 w1_shared[:].bitcast(I32).rearrange("p (s b) -> p s b", s=PASSES),
-                w1_words.bitcast(I32)[e].rearrange("s p b -> p s b"),
+                w1_words.bitcast(I32)[SHARED].rearrange("s p b -> p s b"),
             )
 
-        def load_w1_scales(queue, first, end):
-            planes_of = w1_plane_words.rearrange("p (e s i) -> p e s i", s=PASSES, i=H // 4)
+        def load_w1_scales(words, first, end):
             for r in range(4):
-                if end - first == 1:
-                    nc.sync.dma_start(
-                        planes_of[r:P:32, :, first],
-                        w1_scales.bitcast(I32)[:, first, r:16:4, :].rearrange("e q i -> q e i"),
-                    )
-                else:
-                    nc.sync.dma_start(
-                        w1_plane_words.rearrange("p (a i) -> p a i", i=H // 4)[r:P:32],
-                        w1_scales.bitcast(I32)[:, :, r:16:4, :].rearrange("e s q i -> q (e s) i"),
-                    )
+                nc.sync.dma_start(
+                    words.rearrange("p (a i) -> p a i", i=H // 4)[r:P:32],
+                    w1_scales.bitcast(I32)[first:end, :, r:16:4, :].rearrange("e s q i -> q (e s) i"),
+                )
 
         def load_rest():
             nc.sync.dma_start(
@@ -149,17 +124,18 @@ def tile_moe_shr_mlp_relu_kernel(
                 )
             nc.sync.dma_start(gate_sb[:], gate)
 
-        load_x(0, 0, 0, T)
-        load_offsets()
-        load_x(0, 1, 0, T)
-        load_x(1, 0, 0, T)
-        load_x(1, 1, 0, T)
-        load_x(2, 0, 0, T)
-        load_w1_scales("sync", 0, PASSES)
-        load_x(2, 1, 0, T)
+        load_x(0, 0)
+        nc.sync.dma_start(offsets[:], offs)
+        load_x(0, 1)
+        load_x(1, 0)
+        load_x(1, 1)
+        load_x(2, 0)
+        load_w1_scales(shared_words, SHARED, SHARED + 1)
+        load_shared()
+        load_x(2, 1)
+        load_w1_scales(routed_words, 0, E)
         for s in range(PASSES):
-            load_w1(s, 0, E)
-        load_w1_expert(SHARED)
+            load_routed(s)
         load_rest()
 
         def copy(engine, dst, src):
@@ -182,12 +158,23 @@ def tile_moe_shr_mlp_relu_kernel(
             )
 
         def staged(kind, s, first, end):
-            kind2, s2, first2 = staging(kind, s, first)
-            if kind2 == "raw":
-                return x_raw[s2 // 2, s2 % 2][:].bitcast(BF16)[:, 4 * first2 : 4 * (first2 + end - first)]
-            if kind2 == "sp":
-                return slot_pairs[s2][:, 4 * first2 : 4 * (first2 + end - first)]
-            return quads[kind2, s2][:, 4 * first2 : 4 * (first2 + end - first)]
+            if kind == "token" and first >= EARLY:
+                return x_raw[last, 1][:].bitcast(BF16)[:, 4 * UNIT * s : 4 * UNIT * (s + 1)]
+            return quads[kind, s][:, 4 * first : 4 * end]
+
+        def plane_of(kind, s, first, end):
+            if (kind, s) == ("slot", 1):
+                return planes["token", last][:, first:end]
+            if kind == "token" and first >= EARLY and s < last:
+                return planes["slot", last][:, UNIT * s + first - EARLY : UNIT * s + end - EARLY]
+            return planes[kind, s][:, first:end]
+
+        def codes_of(kind, s, first, end):
+            if kind == "token" and first >= EARLY:
+                if s < last:
+                    return late_codes[:, UNIT * s + first - EARLY : UNIT * s + end - EARLY]
+                return codes["slot", last][:, C + first - EARLY : C + end - EARLY]
+            return codes[kind, s][:, first:end]
 
         def interleave(engine, kind, s, first, end):
             pairs = slot_pairs[s] if kind == "slot" else x_pairs[s]
@@ -200,36 +187,45 @@ def tile_moe_shr_mlp_relu_kernel(
 
         def quantise_x(kind, s, first, end):
             nc.vector.quantize_mx(
-                out=codes[kind, s][:, first:end].bitcast(FP8X4),
-                scales=planes[kind, s][:, first:end],
+                out=codes_of(kind, s, first, end).bitcast(FP8X4),
+                scales=plane_of(kind, s, first, end),
                 in_=staged(kind, s, first, end),
             )
 
+        def quantise_late():
+            nc.vector.quantize_mx(
+                out=late_codes[:].bitcast(FP8X4),
+                scales=planes["slot", last][:],
+                in_=x_raw[last, 1][:].bitcast(BF16)[:, : 8 * UNIT],
+            )
+            quantise_x("token", last, EARLY, T)
+
         def expert_of(kind, block):
             return block * P // C if kind == "slot" else SHARED
-
-        def in_bank(kind, block, shape, name):
-            return psum.tile(shape, F32, tag=f"bank{BANK[kind, block]}", bufs=1, name=name)
 
         sums = {}
 
         def first_layer(kind, block, s):
             if s == 0:
-                sums[kind, block] = in_bank(kind, block, [P, H], "sums")
+                sums[kind, block] = psum.tile([P, H], F32, tag=f"bank{BANK[kind, block]}", bufs=1, name="sums")
             e = expert_of(kind, block)
-            columns = slice(P * block, P * (block + 1))
+            if e == SHARED:
+                words, plane = w1_shared[:, 2 * H * s : 2 * H * (s + 1)], shared_planes[:, H * s : H * (s + 1)]
+            else:
+                a = PASSES * e + s
+                words, plane = w1_codes[s][:, 2 * H * e : 2 * H * (e + 1)], routed_planes[:, H * a : H * (a + 1)]
             nc.tensor.matmul_mx(
                 out=sums[kind, block][:],
-                lhsT=codes[kind, s][:, columns].bitcast(FP8X4),
-                lhsT_scale=planes[kind, s][:, columns],
-                rhs=(w1_shared[:, 2 * H * s : 2 * H * (s + 1)] if e == SHARED else w1_codes[s][:, 2 * H * e : 2 * H * (e + 1)]).bitcast(FP4X4),
-                rhs_scale=w1_planes[:, e * PASSES + s, :],
+                lhsT=codes_of(kind, s, P * block, P * (block + 1)).bitcast(FP8X4),
+                lhsT_scale=plane_of(kind, s, P * block, P * (block + 1)),
+                rhs=words.bitcast(FP4X4),
+                rhs_scale=plane,
                 start=(s == 0),
-                stop=(s == PASSES - 1),
+                stop=(s == last),
             )
 
         def relu(engine, kind, block):
-            dst = h_rows[h_slot(kind, block)][:].rearrange("c (u p d) -> c u p d", u=2, d=2)
+            dst = h_rows[kind, block][:].rearrange("c (u p d) -> c u p d", u=2, d=2)
             src = sums[kind, block][:].rearrange("c (p u d) -> c u p d", u=2, d=2)
             if engine == "vector":
                 nc.vector.tensor_scalar_max(dst, src, 0.0)
@@ -238,122 +234,114 @@ def tile_moe_shr_mlp_relu_kernel(
 
         turned = {}
 
-        def turn(kind, block):
-            unit, b = divmod(block, 2)
-            if b == 0:
-                turned[kind, unit] = psum.tile([P, 2, 2, P], F32, tag=f"bank{t_bank(kind, unit)}", bufs=1, name="turned")
-            words = h_rows[h_slot(kind, block)][:].bitcast(F32)
-            for u in range(2):
-                nc.tensor.transpose(turned[kind, unit][:, b, u, :], words[:, P * u : P * (u + 1)], ident[:])
+        def turn(unit):
+            kind, first, blocks, bank = UNITS[unit][:4]
+            turned[unit] = psum.tile([P, blocks, 2, P], F32, tag=f"bank{bank}", bufs=1, name="turned")
+            for b in range(blocks):
+                words = h_rows[kind, first + b][:].bitcast(F32)
+                for u in range(2):
+                    nc.tensor.transpose(turned[unit][:, b, u, :], words[:, P * u : P * (u + 1)], ident[:])
 
-        def unit_columns(unit):
-            return slice(UNIT * unit, UNIT * (unit + 1))
+        def columns_of(unit):
+            first, blocks = UNITS[unit][1:3]
+            return slice(P * first, P * (first + blocks))
 
-        def spread(engine, kind, unit):
+        def spread(engine, unit):
             copy(
                 engine,
-                h_quads[kind, unit][:].bitcast(F32).rearrange("p (b c u) -> p b c u", b=2, u=2),
-                turned[kind, unit][:].rearrange("p b u c -> p b c u"),
+                h_quads[unit][:].bitcast(F32).rearrange("p (b c u) -> p b c u", c=P, u=2),
+                turned[unit][:].rearrange("p b u c -> p b c u"),
             )
 
-        def quantise_h(kind, unit):
-            nc.vector.quantize_mx(
-                out=h_codes[kind, unit][:].bitcast(FP8X4),
-                scales=h_planes[kind, unit][:],
-                in_=h_quads[kind, unit][:],
-            )
+        def quantise_h(unit):
+            nc.vector.quantize_mx(out=h_codes[unit][:].bitcast(FP8X4), scales=h_planes[unit][:], in_=h_quads[unit][:])
 
         y = {}
 
-        def second_layer(kind, unit):
-            e = expert_of(kind, 2 * unit)
-            if (kind, unit) == ("token", 1) and y_bank(kind, 0) == y_bank(kind, 1):
-                y[kind, unit] = y["pair"][:, UNIT:]
-            elif (kind, unit) == ("token", 0):
-                y["pair"] = psum.tile([P, 2 * UNIT], F32, tag=f"bank{y_bank(kind, unit)}", bufs=1, name="y")
-                y[kind, unit] = y["pair"][:, :UNIT]
+        def second_layer(unit):
+            kind, first, blocks, tb, bank = UNITS[unit]
+            e = expert_of(kind, first)
+            if unit in ("t0","t1"):
+                if "pair" not in y:
+                    y["pair"] = psum.tile([P, 2 * UNIT], F32, tag=f"bank{bank}", bufs=1, name="y")
+                y[unit] = y["pair"][:, columns_of(unit)]
             else:
-                y[kind, unit] = psum.tile([P, UNIT], F32, tag=f"bank{y_bank(kind, unit)}", bufs=1, name="y")[:]
+                y[unit] = psum.tile([P, blocks * P], F32, tag=f"bank{bank}", bufs=1, name="y")[:]
             nc.tensor.matmul_mx(
-                out=y[kind, unit],
+                out=y[unit],
                 lhsT=w2_codes[:, e, :].bitcast(FP4X4),
                 lhsT_scale=w2_planes[:, e, :],
-                rhs=h_codes[kind, unit][:].bitcast(FP8X4),
-                rhs_scale=h_planes[kind, unit][:],
+                rhs=h_codes[unit][:].bitcast(FP8X4),
+                rhs_scale=h_planes[unit][:],
                 start=True,
                 stop=True,
             )
 
         def take_y(engine, unit):
-            copy(engine, routed_y[:, unit_columns(unit)], y["slot", unit])
+            copy(engine, routed_y[:, columns_of(unit)], y[unit])
 
-        def scatter(unit):
-            columns = unit_columns(unit)
+        def scatter(first, end):
             nc.vector.tensor_tensor(
-                routed[:].indirect(offsets[:, UNIT // 16 * unit : UNIT // 16 * (unit + 1)]),
-                routed_y[:, columns],
-                gate_sb[:, columns],
-                MULT,
+                routed[:].indirect(offsets[:, first // 16 : end // 16]), routed_y[:, first:end], gate_sb[:, first:end], MULT
             )
 
         def finish(unit):
-            columns = unit_columns(unit)
-            nc.vector.tensor_tensor(result[:, columns], y["token", unit], routed[:, columns], ADD)
+            columns = columns_of(unit)
+            nc.vector.tensor_tensor(result[:, columns], y[unit], routed[:, columns], ADD)
             nc.sync.dma_start(out[:, columns], result[:, columns])
 
-        last = PASSES - 1
-        EARLY = ((0, 1),)
         for s in range(PASSES):
             for u in range(2):
-                if (s, u) == (last, 1):
-                    interleave("scalar", "token", 1, 0, 1 * UNIT)
-                if s == 0:
-                    round_x("scalar", s, u, 0, UNIT)
-                    round_x("vector", s, u, UNIT, T)
-                else:
-                    round_x("scalar", s, u, 0, T)
-                if u == 0:
-                    gather(s, 0, 0, S)
-            for e in range(E):
-                gather(s, 1, C * e, C * (e + 1))
-            for e in range(E):
-                interleave("vector", "slot", s, C * e, C * (e + 1))
-            for e in range(E):
-                quantise_x("slot", s, C * e, C * (e + 1))
-        for s in range(PASSES):
+                split = UNIT if s == 0 else (T - 192 if (s, u) == (last, 1) else T)
+                round_x("scalar", s, u, 0, split)
+                if split < T:
+                    round_x("vector", s, u, split, T)
+                if (s, u) != (last, 1):
+                    gather(s, u, 0, S)
+            if s < last:
+                interleave("vector", "slot", s, 0, S)
+                quantise_x("slot", s, 0, S)
+                interleave("scalar", "token", s, 0, EARLY)
+                quantise_x("token", s, 0, EARLY)
+                for block in range(4):
+                    first_layer("token", block, s)
+        for e in range(E):
+            gather(last, 1, C * e, C * (e + 1))
+        for e in range(E):
+            interleave("vector", "slot", last, C * e, C * (e + 1))
+        for e in range(E):
+            quantise_x("slot", last, C * e, C * (e + 1))
+        for s in range(0, 3):
             for block in range(4):
                 first_layer("slot", block, s)
-        for e in range(E):
-            relu("scalar", "slot", 2 * e)
-            relu("scalar", "slot", 2 * e + 1)
-            turn("slot", 2 * e)
-            turn("slot", 2 * e + 1)
-            spread("scalar", "slot", e)
-            quantise_h("slot", e)
-            second_layer("slot", e)
-            take_y("scalar", e)
-        for unit in range(3):
+        for unit, (kind, first, blocks, tb, yb) in UNITS.items():
+            if kind == "slot":
+                for block in range(first, first + blocks):
+                    relu("vector" if block in (1,3) else "scalar", kind, block)
+                turn(unit)
+                spread("scalar", unit)
+                quantise_h(unit)
+                second_layer(unit)
+                take_y("scalar", unit)
+                scatter(P * first, P * (first + blocks))
+        interleave("scalar", "token", last, 0, EARLY)
+        quantise_x("token", last, 0, EARLY)
+        for block in range(4):
+            first_layer("token", block, last)
+        for s in range(PASSES):
+            interleave("scalar", "token", s, EARLY, T)
+        quantise_late()
+        for block in (4, 5):
             for s in range(PASSES):
-                if (unit, s) == (1, 0):
-                    continue
-                end = 2 * UNIT if (unit, s) == (0, 0) else UNIT * (unit + 1)
-                if (unit, s) not in EARLY:
-                    interleave("scalar", "token", s, UNIT * unit, end)
-                quantise_x("token", s, UNIT * unit, end)
-            for block in (2 * unit, 2 * unit + 1):
-                for s in range(PASSES):
-                    first_layer("token", block, s)
-        for unit in range(3):
-            relu("vector" if unit == 0 else "scalar", "token", 2 * unit)
-            relu("vector" if unit == 0 else "scalar", "token", 2 * unit + 1)
-            turn("token", 2 * unit)
-            turn("token", 2 * unit + 1)
-        for unit in range(3):
-            spread("scalar", "token", unit)
-            quantise_h("token", unit)
-        for unit in range(3):
-            second_layer("token", unit)
-        for e in range(E):
-            scatter(e)
-        for unit in range(3):
+                first_layer("token", block, s)
+        tokens = [unit for unit in UNITS if UNITS[unit][0] == "token"]
+        for unit in tokens:
+            for block in range(UNITS[unit][1], UNITS[unit][1] + UNITS[unit][2]):
+                relu("vector" if block in (1,3) else "scalar", "token", block)
+            turn(unit)
+            spread("vector" if unit in () else "scalar", unit)
+            quantise_h(unit)
+        for unit in tokens:
+            second_layer(unit)
+        for unit in tokens:
             finish(unit)

@@ -30,8 +30,8 @@ ADD = mybir.AluOpType.add
 
 
 EARLY = 4 * P
-BANK = {("slot", 0): 0, ("slot", 1): 1, ("slot", 2): 2, ("slot", 3): 3, ("token", 0): 4, ("token", 1): 5, ("token", 2): 6, ("token", 3): 7, ("token", 4): 0, ("token", 5): 2}
-UNITS = {"e0": ("slot", 0, 2, 1, 1), "e1": ("slot", 2, 2, 3, 3), "t0": ("token", 0, 2, 5, 2), "t1": ("token", 2, 2, 7, 2), "t2": ("token", 4, 2, 2, 4)}
+BANK = {("slot", 0): 0, ("slot", 1): 1, ("slot", 2): 2, ("slot", 3): 3, ("token", 0): 4, ("token", 1): 5, ("token", 2): 6, ("token", 3): 7, ("token", 4): 0, ("token", 5): 5}
+UNITS = {"e0": ("slot", 0, 2, 1, 1), "e1": ("slot", 2, 2, 3, 3), "t0": ("token", 0, 2, 2, 5), "t1": ("token", 2, 2, 7, 5), "t2": ("token", 4, 2, 5, 4)}
 
 
 def tile_moe_shr_mlp_relu_kernel(
@@ -62,7 +62,8 @@ def tile_moe_shr_mlp_relu_kernel(
             x_pairs[s] = keep.tile([P, 2 * T * 2], BF16, align_bytes=64, name=f"x_pairs{s}")
             slot_pairs[s] = keep.tile([P, 2 * S * 2], BF16, align_bytes=64, name=f"slot_pairs{s}")
             w1_codes[s] = keep.tile([P, E * 2 * H], U8, align_bytes=64, name=f"w1_codes{s}")
-        late_codes = keep.tile([P, 2 * UNIT], U32, align_bytes=64, name="late_codes")
+        late_codes = keep.tile([P, 4 * P], U32, align_bytes=64, name="late_codes")
+        late_planes = keep.tile([P, 2 * P], U8, align_bytes=64, name="late_planes")
         w1_shared = keep.tile([P, PASSES * 2 * H], U8, align_bytes=64, name="w1_shared")
         h_rows, h_quads, h_codes, h_planes = {}, {}, {}, {}
         for kind, n in (("slot", S), ("token", T)):
@@ -132,7 +133,8 @@ def tile_moe_shr_mlp_relu_kernel(
         load_x(2, 0)
         load_w1_scales(shared_words, SHARED, SHARED + 1)
         load_shared()
-        load_x(2, 1)
+        load_x(2, 1, 0, EARLY)
+        load_x(2, 1, EARLY, T)
         load_w1_scales(routed_words, 0, E)
         for s in range(PASSES):
             load_routed(s)
@@ -141,6 +143,8 @@ def tile_moe_shr_mlp_relu_kernel(
         def copy(engine, dst, src):
             if engine == "vector":
                 nc.vector.tensor_copy(dst, src)
+            elif engine == "gpsimd":
+                nc.gpsimd.tensor_copy(dst, src)
             else:
                 nc.scalar.copy(dst, src)
 
@@ -158,30 +162,34 @@ def tile_moe_shr_mlp_relu_kernel(
             )
 
         def staged(kind, s, first, end):
-            if kind == "token" and first >= EARLY:
-                return x_raw[last, 1][:].bitcast(BF16)[:, 4 * UNIT * s : 4 * UNIT * (s + 1)]
+
             return quads[kind, s][:, 4 * first : 4 * end]
 
         def plane_of(kind, s, first, end):
             if (kind, s) == ("slot", 1):
                 return planes["token", last][:, first:end]
-            if kind == "token" and first >= EARLY and s < last:
-                return planes["slot", last][:, UNIT * s + first - EARLY : UNIT * s + end - EARLY]
+            if kind == "token" and first >= EARLY:
+                place = PASSES * (first - EARLY) // P + s
+                if place < 4:
+                    return planes["slot", last][:, P * place : P * (place + 1)]
+                return late_planes[:, P * (place - 4) : P * (place - 3)]
             return planes[kind, s][:, first:end]
 
         def codes_of(kind, s, first, end):
             if kind == "token" and first >= EARLY:
-                if s < last:
-                    return late_codes[:, UNIT * s + first - EARLY : UNIT * s + end - EARLY]
-                return codes["slot", last][:, C + first - EARLY : C + end - EARLY]
+                place = PASSES * (first - EARLY) // P + s
+                if place < 4:
+                    return late_codes[:, P * place : P * (place + 1)]
+                return codes["slot", last][:, C:][:, P * (place - 4) : P * (place - 3)]
             return codes[kind, s][:, first:end]
 
         def interleave(engine, kind, s, first, end):
             pairs = slot_pairs[s] if kind == "slot" else x_pairs[s]
-            words = pairs[:].bitcast(F32).rearrange("p (u c) -> p c u", u=2)
+            word = I32 if engine == "gpsimd" else F32
+            words = pairs[:].bitcast(word).rearrange("p (u c) -> p c u", u=2)
             copy(
                 engine,
-                staged(kind, s, first, end).bitcast(F32).rearrange("p (c u) -> p c u", u=2),
+                staged(kind, s, first, end).bitcast(word).rearrange("p (c u) -> p c u", u=2),
                 words[:, first:end],
             )
 
@@ -192,13 +200,20 @@ def tile_moe_shr_mlp_relu_kernel(
                 in_=staged(kind, s, first, end),
             )
 
-        def quantise_late():
-            nc.vector.quantize_mx(
-                out=late_codes[:].bitcast(FP8X4),
-                scales=planes["slot", last][:],
-                in_=x_raw[last, 1][:].bitcast(BF16)[:, : 8 * UNIT],
+        late_quads = x_raw[last, 1][:].bitcast(BF16)
+
+        def interleave_late(engine, s):
+            copy(
+                engine,
+                x_raw[last, 1][:].rearrange("p (b s c u) -> p s b c u", b=2, s=PASSES, u=2)[:, s],
+                x_pairs[s][:].bitcast(F32).rearrange("p (u b c) -> p b c u", u=2, c=P)[:, EARLY // P :],
             )
-            quantise_x("token", last, EARLY, T)
+
+        def quantise_late(part):
+            if part == 0:
+                nc.vector.quantize_mx(out=late_codes[:].bitcast(FP8X4), scales=planes["slot", last][:], in_=late_quads[:, : 16 * P])
+            else:
+                nc.vector.quantize_mx(out=codes["slot", last][:, C:][:, : 2 * P].bitcast(FP8X4), scales=late_planes[:], in_=late_quads[:, 16 * P :])
 
         def expert_of(kind, block):
             return block * P // C if kind == "slot" else SHARED
@@ -237,7 +252,7 @@ def tile_moe_shr_mlp_relu_kernel(
         def turn(unit):
             kind, first, blocks, bank = UNITS[unit][:4]
             turned[unit] = psum.tile([P, blocks, 2, P], F32, tag=f"bank{bank}", bufs=1, name="turned")
-            for b in range(blocks):
+            for b in reversed(range(blocks)):
                 words = h_rows[kind, first + b][:].bitcast(F32)
                 for u in range(2):
                     nc.tensor.transpose(turned[unit][:, b, u, :], words[:, P * u : P * (u + 1)], ident[:])
@@ -292,55 +307,81 @@ def tile_moe_shr_mlp_relu_kernel(
 
         for s in range(PASSES):
             for u in range(2):
-                split = UNIT if s == 0 else (T - 192 if (s, u) == (last, 1) else T)
-                round_x("scalar", s, u, 0, split)
-                if split < T:
-                    round_x("vector", s, u, split, T)
-                if (s, u) != (last, 1):
+                if s == 0:
+                    round_x("scalar", s, u, 0, 192 if u else UNIT)
+                    round_x("vector", s, u, 192 if u else UNIT, T)
+                elif u == 1:
+                    round_x("scalar", s, u, 0, EARLY)
+                    round_x("scalar", s, u, EARLY, T)
+                else:
+                    round_x("scalar", s, u, 0, T)
+                if u == 0:
                     gather(s, u, 0, S)
+            for e in range(E):
+                gather(s, 1, C * e, C * (e + 1))
+            for e in range(E):
+                interleave("vector", "slot", s, C * e, C * (e + 1))
+            for e in range(E):
+                quantise_x("slot", s, C * e, C * (e + 1))
             if s < last:
-                interleave("vector", "slot", s, 0, S)
-                quantise_x("slot", s, 0, S)
-                interleave("scalar", "token", s, 0, EARLY)
+                if s == 0:
+                    interleave("scalar", "token", s, 0, 192)
+                    interleave("scalar", "token", s, 192, EARLY)
+                else:
+                    interleave("scalar", "token", s, 0, EARLY)
                 quantise_x("token", s, 0, EARLY)
                 for block in range(4):
                     first_layer("token", block, s)
-        for e in range(E):
-            gather(last, 1, C * e, C * (e + 1))
-        for e in range(E):
-            interleave("vector", "slot", last, C * e, C * (e + 1))
-        for e in range(E):
-            quantise_x("slot", last, C * e, C * (e + 1))
         for s in range(0, 3):
             for block in range(4):
                 first_layer("slot", block, s)
-        for unit, (kind, first, blocks, tb, yb) in UNITS.items():
-            if kind == "slot":
-                for block in range(first, first + blocks):
-                    relu("vector" if block in (1,3) else "scalar", kind, block)
-                turn(unit)
-                spread("scalar", unit)
-                quantise_h(unit)
+        def second_half(unit, b, bank):
+            first = UNITS[unit][1] + b
+            y[unit, b] = psum.tile([P, P], F32, tag=f"bank{bank}", bufs=1, name="y")
+            nc.tensor.matmul_mx(
+                out=y[unit, b][:],
+                lhsT=w2_codes[:, expert_of("slot", first), :].bitcast(FP4X4),
+                lhsT_scale=w2_planes[:, expert_of("slot", first), :],
+                rhs=h_codes[unit][:, P * b : P * (b + 1)].bitcast(FP8X4),
+                rhs_scale=h_planes[unit][:, P * b : P * (b + 1)],
+                start=True,
+                stop=True,
+            )
+            copy("scalar", routed_y[:, P * first : P * (first + 1)], y[unit, b][:])
+            scatter(P * first, P * (first + 1))
+
+        for unit in ("e0", "e1"):
+            first = UNITS[unit][1]
+            for block in (first, first + 1):
+                relu("vector" if block in (1,3) else "scalar", "slot", block)
+            turn(unit)
+            spread("scalar", unit)
+            quantise_h(unit)
+            if unit == "e0":
                 second_layer(unit)
-                take_y("scalar", unit)
-                scatter(P * first, P * (first + blocks))
+                take_y("vector", unit)
+                scatter(0, C)
+        second_half("e1", 0, 3)
         interleave("scalar", "token", last, 0, EARLY)
         quantise_x("token", last, 0, EARLY)
         for block in range(4):
             first_layer("token", block, last)
         for s in range(PASSES):
-            interleave("scalar", "token", s, EARLY, T)
-        quantise_late()
+            interleave_late("scalar", s)
+        quantise_late(0)
+        quantise_late(1)
         for block in (4, 5):
             for s in range(PASSES):
                 first_layer("token", block, s)
-        tokens = [unit for unit in UNITS if UNITS[unit][0] == "token"]
+        tokens = ("t0", "t1", "t2")
+        for block in range(T // P):
+            relu("vector" if block in (2,) else "scalar", "token", block)
         for unit in tokens:
-            for block in range(UNITS[unit][1], UNITS[unit][1] + UNITS[unit][2]):
-                relu("vector" if block in (1,3) else "scalar", "token", block)
             turn(unit)
-            spread("vector" if unit in () else "scalar", unit)
+            spread("scalar", unit)
             quantise_h(unit)
+            if unit == "t0":
+                second_half("e1", 1, 2)
         for unit in tokens:
             second_layer(unit)
         for unit in tokens:

@@ -30,8 +30,8 @@ ADD = mybir.AluOpType.add
 
 
 EARLY = 4 * P
-BANK = {("slot", 0): 0, ("slot", 1): 1, ("slot", 2): 2, ("slot", 3): 3, ("token", 0): 4, ("token", 1): 5, ("token", 2): 6, ("token", 3): 7, ("token", 4): 0, ("token", 5): 5}
-UNITS = {"e0": ("slot", 0, 2, 1, 1), "e1": ("slot", 2, 2, 3, 3), "t0": ("token", 0, 2, 2, 5), "t1": ("token", 2, 2, 7, 5), "t2": ("token", 4, 2, 5, 4)}
+BANK = {("slot", 0): 0, ("slot", 1): 1, ("slot", 2): 2, ("slot", 3): 3, ("token", 0): 4, ("token", 1): 5, ("token", 2): 6, ("token", 3): 7, ("token", 4): 0, ("token", 5): 4}
+UNITS = {"e0": ("slot", 0, 2, 1, 1), "e1": ("slot", 2, 2, 3, 3), "t0": ("token", 0, 2, 5, 7), "t1": ("token", 2, 2, 7, 7), "t2": ("token", 4, 2, 4, 6)}
 
 
 def tile_moe_shr_mlp_relu_kernel(
@@ -100,10 +100,10 @@ def tile_moe_shr_mlp_relu_kernel(
                 w1_words.bitcast(I32)[0:E, s].rearrange("e p b -> p e b"),
             )
 
-        def load_shared():
+        def load_shared(first, end):
             nc.sync.dma_start(
-                w1_shared[:].bitcast(I32).rearrange("p (s b) -> p s b", s=PASSES),
-                w1_words.bitcast(I32)[SHARED].rearrange("s p b -> p s b"),
+                w1_shared[:].bitcast(I32).rearrange("p (s b) -> p s b", s=PASSES)[:, first:end],
+                w1_words.bitcast(I32)[SHARED, first:end].rearrange("s p b -> p s b"),
             )
 
         def load_w1_scales(words, first, end):
@@ -132,12 +132,13 @@ def tile_moe_shr_mlp_relu_kernel(
         load_x(1, 1)
         load_x(2, 0)
         load_w1_scales(shared_words, SHARED, SHARED + 1)
-        load_shared()
+        load_shared(0, last)
         load_x(2, 1, 0, EARLY)
         load_x(2, 1, EARLY, T)
         load_w1_scales(routed_words, 0, E)
         for s in range(PASSES):
             load_routed(s)
+        load_shared(last, PASSES)
         load_rest()
 
         def copy(engine, dst, src):
@@ -166,7 +167,7 @@ def tile_moe_shr_mlp_relu_kernel(
             return quads[kind, s][:, 4 * first : 4 * end]
 
         def plane_of(kind, s, first, end):
-            if (kind, s) == ("slot", 1):
+            if (kind, s) == ("slot", 0):
                 return planes["token", last][:, first:end]
             if kind == "token" and first >= EARLY:
                 place = PASSES * (first - EARLY) // P + s
@@ -332,36 +333,28 @@ def tile_moe_shr_mlp_relu_kernel(
                 quantise_x("token", s, 0, EARLY)
                 for block in range(4):
                     first_layer("token", block, s)
-        for s in range(0, 3):
-            for block in range(4):
-                first_layer("slot", block, s)
-        def second_half(unit, b, bank):
-            first = UNITS[unit][1] + b
-            y[unit, b] = psum.tile([P, P], F32, tag=f"bank{bank}", bufs=1, name="y")
-            nc.tensor.matmul_mx(
-                out=y[unit, b][:],
-                lhsT=w2_codes[:, expert_of("slot", first), :].bitcast(FP4X4),
-                lhsT_scale=w2_planes[:, expert_of("slot", first), :],
-                rhs=h_codes[unit][:, P * b : P * (b + 1)].bitcast(FP8X4),
-                rhs_scale=h_planes[unit][:, P * b : P * (b + 1)],
-                start=True,
-                stop=True,
-            )
-            copy("scalar", routed_y[:, P * first : P * (first + 1)], y[unit, b][:])
-            scatter(P * first, P * (first + 1))
-
+        for block in range(4):
+            first_layer("slot", block, 0)
+        for e in range(E):
+            for s in range(1, PASSES):
+                for block in (2 * e, 2 * e + 1):
+                    first_layer("slot", block, s)
         for unit in ("e0", "e1"):
             first = UNITS[unit][1]
             for block in (first, first + 1):
-                relu("vector" if block in (1,3) else "scalar", "slot", block)
+                relu("vector" if block % 2 else "scalar", "slot", block)
             turn(unit)
             spread("scalar", unit)
             quantise_h(unit)
+            second_layer(unit)
             if unit == "e0":
-                second_layer(unit)
                 take_y("vector", unit)
                 scatter(0, C)
-        second_half("e1", 0, 3)
+
+        def put_back(block):
+            copy("scalar", routed_y[:, P * block : P * (block + 1)], y["e1"][:, P * (block - 2) : P * (block - 1)])
+            scatter(P * block, P * (block + 1))
+
         interleave("scalar", "token", last, 0, EARLY)
         quantise_x("token", last, 0, EARLY)
         for block in range(4):
@@ -375,13 +368,14 @@ def tile_moe_shr_mlp_relu_kernel(
                 first_layer("token", block, s)
         tokens = ("t0", "t1", "t2")
         for block in range(T // P):
-            relu("vector" if block in (2,) else "scalar", "token", block)
+            relu("vector" if block in (1,) else "scalar", "token", block)
+        put_back(2)
         for unit in tokens:
             turn(unit)
             spread("scalar", unit)
             quantise_h(unit)
-            if unit == "t0":
-                second_half("e1", 1, 2)
+            if unit == "t1":
+                put_back(3)
         for unit in tokens:
             second_layer(unit)
         for unit in tokens:

@@ -9,9 +9,13 @@ P = 128
 S = E * C
 K_PASS = 512
 PASSES = K // K_PASS
-QUADRANTS = 4
+LAST = PASSES - 1
+SCALE_ROWS = 4
 SHARED = E
 UNIT = 2 * P
+EARLY = 2 * UNIT
+SCALAR_ROUNDS = T // 3
+SCALAR_QUADS = P
 
 FLOPS = 2 * (S + T) * (K * H + H * N)
 
@@ -29,354 +33,290 @@ MULT = mybir.AluOpType.mult
 ADD = mybir.AluOpType.add
 
 
-EARLY = 4 * P
-BANK = {("slot", 0): 0, ("slot", 1): 1, ("slot", 2): 2, ("slot", 3): 3, ("token", 0): 4, ("token", 1): 5, ("token", 2): 6, ("token", 3): 7, ("token", 4): 0, ("token", 5): 4}
-UNITS = {"e0": ("slot", 0, 2, 1, 1), "e1": ("slot", 2, 2, 3, 3), "t0": ("token", 0, 2, 5, 7), "t1": ("token", 2, 2, 7, 7), "t2": ("token", 4, 2, 4, 6)}
+def sum_bank(kind, block):
+    return block if kind == "slot" else 4 + block % 4
 
 
 def tile_moe_shr_mlp_relu_kernel(
     tc, xT, w1_words, w1_scales, w2_words, w2_scales, gate, offs, out
 ):
     nc = tc.nc
-    last = PASSES - 1
     with ExitStack() as ctx:
         keep = ctx.enter_context(tc.tile_pool(name="keep", bufs=1))
         psum = ctx.enter_context(tc.psum_pool(name="psum", bufs=1))
 
-        offsets = keep.tile([P, S // 16], U16, name="offsets")
-        gate_sb = keep.tile([P, S], F32, name="gate_sb")
-        w2_codes = keep.tile([P, E + 1, 2 * N], U8, align_bytes=64, name="w2_codes")
-        shared_planes = keep.tile([P, PASSES * H], U8, align_bytes=64, name="shared_planes")
-        routed_planes = keep.tile([P, E * PASSES * H], U8, align_bytes=64, name="routed_planes")
-        w2_planes = keep.tile([P, E + 1, N], U8, align_bytes=64, name="w2_planes")
-        ident = keep.tile([P, P], F32, name="ident")
-        routed = keep.tile([P, T], F32, name="routed")
-        routed_y = keep.tile([P, S], F32, name="routed_y")
-        result = keep.tile([P, T], F32, name="result")
+        def sbuf(columns, dtype, name):
+            return keep.tile([P, columns], dtype, align_bytes=64, name=name)
 
-        x_raw, w1_codes, x_pairs, slot_pairs = {}, {}, {}, {}
-        quads, codes, planes = {}, {}, {}
+        def in_bank(bank, shape, name):
+            return psum.tile(shape, F32, tag=f"bank{bank}", bufs=1, name=name)
+
+        offsets = sbuf(S // 16, U16, "offsets")
+        gate_sb = sbuf(S, F32, "gate_sb")
+        ident = sbuf(P, F32, "ident")
+        w1_shared = sbuf(PASSES * 2 * H, U8, "w1_shared")
+        w1_routed = [sbuf(E * 2 * H, U8, f"w1_routed{s}") for s in range(PASSES)]
+        w1_shared_planes = sbuf(PASSES * H, U8, "w1_shared_planes")
+        w1_routed_planes = sbuf(E * PASSES * H, U8, "w1_routed_planes")
+        w2_codes = sbuf((E + 1) * 2 * N, U8, "w2_codes")
+        w2_planes = sbuf((E + 1) * N, U8, "w2_planes")
+        routed_y = sbuf(S, F32, "routed_y")
+        routed = sbuf(T, F32, "routed")
+        result = sbuf(T, F32, "result")
+
+        x_raw, x_pairs, slot_pairs, quads, codes, planes = {}, {}, {}, {}, {}, {}
         for s in range(PASSES):
             for u in range(2):
-                x_raw[s, u] = keep.tile([P, 2 * T], F32, align_bytes=64, name=f"x_raw{s}{u}")
-            x_pairs[s] = keep.tile([P, 2 * T * 2], BF16, align_bytes=64, name=f"x_pairs{s}")
-            slot_pairs[s] = keep.tile([P, 2 * S * 2], BF16, align_bytes=64, name=f"slot_pairs{s}")
-            w1_codes[s] = keep.tile([P, E * 2 * H], U8, align_bytes=64, name=f"w1_codes{s}")
-        late_codes = keep.tile([P, 4 * P], U32, align_bytes=64, name="late_codes")
-        late_planes = keep.tile([P, 2 * P], U8, align_bytes=64, name="late_planes")
-        w1_shared = keep.tile([P, PASSES * 2 * H], U8, align_bytes=64, name="w1_shared")
-        h_rows, h_quads, h_codes, h_planes = {}, {}, {}, {}
-        for kind, n in (("slot", S), ("token", T)):
-            for s in range(PASSES):
-                quads[kind, s] = keep.tile([P, S * 4], BF16, align_bytes=64, name=f"{kind}_quads{s}")
-                codes[kind, s] = keep.tile([P, n], U32, align_bytes=64, name=f"{kind}_codes{s}")
-                planes[kind, s] = keep.tile([P, n], U8, align_bytes=64, name=f"{kind}_planes{s}")
-            for block in range(n // P):
-                h_rows[kind, block] = keep.tile([P, H], BF16, align_bytes=64, name=f"{kind}_h_rows{block}")
-        for unit, (kind, first, blocks, tb, yb) in UNITS.items():
-            h_quads[unit] = keep.tile([P, blocks * P * 4], BF16, align_bytes=64, name=f"h_quads{unit}")
-            h_codes[unit] = keep.tile([P, blocks * P], U32, align_bytes=64, name=f"h_codes{unit}")
-            h_planes[unit] = keep.tile([P, blocks * P], U8, align_bytes=64, name=f"h_planes{unit}")
-
-        shared_words = shared_planes[:].bitcast(I32)
-        routed_words = routed_planes[:].bitcast(I32)
-        w2_plane_words = w2_planes[:].rearrange("p a i -> p (a i)").bitcast(I32)
-        nc.vector.memset(shared_words, 0)
-        warm = keep.tile([P, 1], F32, name="warm")
-        nc.vector.memset(warm[:], 0.0)
-        nc.scalar.activation(warm[:], warm[:], RELU)
-        make_identity(nc, ident[:])
-        nc.vector.memset(routed_words, 0)
-        nc.vector.memset(w2_plane_words, 0)
-        nc.vector.memset(routed[:], 0.0)
-
-        def load_x(s, u, first=0, end=T):
-            rows = xT[K_PASS * s : K_PASS * (s + 1), :].rearrange("(p d) t -> p d t", d=4)
-            nc.sync.dma_start(x_raw[s, u][:].rearrange("p (d t) -> p d t", d=2)[:, :, first:end], rows[:, 2 * u : 2 * u + 2, first:end])
-
-        def load_routed(s):
-            nc.sync.dma_start(
-                w1_codes[s][:].bitcast(I32).rearrange("p (e b) -> p e b", e=E),
-                w1_words.bitcast(I32)[0:E, s].rearrange("e p b -> p e b"),
-            )
-
-        def load_shared(first, end):
-            nc.sync.dma_start(
-                w1_shared[:].bitcast(I32).rearrange("p (s b) -> p s b", s=PASSES)[:, first:end],
-                w1_words.bitcast(I32)[SHARED, first:end].rearrange("s p b -> p s b"),
-            )
-
-        def load_w1_scales(words, first, end):
-            for r in range(4):
-                nc.sync.dma_start(
-                    words.rearrange("p (a i) -> p a i", i=H // 4)[r:P:32],
-                    w1_scales.bitcast(I32)[first:end, :, r:16:4, :].rearrange("e s q i -> q (e s) i"),
-                )
-
-        def load_rest():
-            nc.sync.dma_start(
-                w2_codes[:].rearrange("p e b -> p (e b)").bitcast(I32).rearrange("p (e b) -> p e b", e=E + 1),
-                w2_words.bitcast(I32)[:, 0].rearrange("e p b -> p e b"),
-            )
-            for r in range(4):
-                nc.sync.dma_start(
-                    w2_plane_words.rearrange("p (a i) -> p a i", i=N // 4)[r:P:32],
-                    w2_scales.bitcast(I32)[:, 0, r:16:4, :].rearrange("e q i -> q e i"),
-                )
-            nc.sync.dma_start(gate_sb[:], gate)
-
-        load_x(0, 0)
-        nc.sync.dma_start(offsets[:], offs)
-        load_x(0, 1)
-        load_x(1, 0)
-        load_x(1, 1)
-        load_x(2, 0)
-        load_w1_scales(shared_words, SHARED, SHARED + 1)
-        load_shared(0, last)
-        load_x(2, 1, 0, EARLY)
-        load_x(2, 1, EARLY, T)
-        load_w1_scales(routed_words, 0, E)
+                x_raw[s, u] = sbuf(2 * T, F32, f"x_raw{s}{u}")
+            x_pairs[s] = sbuf(2 * T, U32, f"x_pairs{s}")
+            for kind in ("slot", "token"):
+                quads[kind, s] = sbuf(2 * EARLY, U32, f"{kind}_quads{s}")
+                codes[kind, s] = sbuf(EARLY, U32, f"{kind}_codes{s}")
+        for s in range(LAST):
+            slot_pairs[s] = sbuf(2 * S, U32, f"slot_pairs{s}")
+            planes["token", s] = sbuf(EARLY, U8, f"token_plane{s}")
         for s in range(PASSES):
-            load_routed(s)
-        load_shared(last, PASSES)
-        load_rest()
+            planes["slot", s] = sbuf(S, U8, f"slot_plane{s}")
+        slot_pairs[LAST] = quads["token", LAST - 1]
+        planes["token", LAST] = planes["slot", 0]
+        late_quads = x_raw[LAST, 1][:].bitcast(U32)
+        late_codes = [sbuf(4 * P, U32, "late_codes")[:], codes["slot", LAST][:, C:]]
+        late_planes = [planes["slot", LAST][:], sbuf(2 * P, U8, "late_plane")[:]]
+
+        h_rows, h_quads, h_codes, h_planes = {}, {}, {}, {}
+        for kind, columns in (("slot", S), ("token", T)):
+            for block in range(columns // P):
+                h_rows[kind, block] = sbuf(H, BF16, f"{kind}_h_rows{block}")
+            for unit in range(columns // UNIT):
+                h_quads[kind, unit] = sbuf(2 * UNIT, F32, f"{kind}_h_quads{unit}")
+                h_codes[kind, unit] = sbuf(UNIT, U32, f"{kind}_h_codes{unit}")
+                h_planes[kind, unit] = sbuf(UNIT, U8, f"{kind}_h_plane{unit}")
+
+        for tile in (w1_routed_planes, w1_shared_planes, w2_planes):
+            nc.vector.memset(tile[:].bitcast(I32), 0)
+        nc.scalar.activation(routed[:], w1_routed_planes[:].bitcast(F32), RELU)
+        make_identity(nc, ident[:])
+
+        def load_x(s, u, first, end):
+            rows = xT[K_PASS * s : K_PASS * (s + 1), :].rearrange("(p d) t -> p d t", d=4)
+            nc.sync.dma_start(
+                x_raw[s, u][:].rearrange("p (d t) -> p d t", d=2)[:, :, first:end],
+                rows[:, 2 * u : 2 * u + 2, first:end],
+            )
+
+        def load_planes(tile, scales, width):
+            for r in range(SCALE_ROWS):
+                nc.sync.dma_start(
+                    tile[:].bitcast(I32).rearrange("p (a i) -> p a i", i=width // 4)[r:P:32],
+                    scales.bitcast(I32)[:, :, r:16:SCALE_ROWS, :].rearrange("e s q i -> q (e s) i"),
+                )
+
+        def load_words(dst, words):
+            nc.sync.dma_start(
+                dst.bitcast(I32).rearrange("p (a b) -> p a b", a=words.shape[0]),
+                words.bitcast(I32).rearrange("a p b -> p a b"),
+            )
+
+        load_x(0, 0, 0, T)
+        nc.sync.dma_start(offsets[:], offs)
+        load_x(0, 1, 0, T)
+        load_x(1, 0, 0, T)
+        load_x(1, 1, 0, T)
+        load_x(LAST, 0, 0, T)
+        load_planes(w1_shared_planes, w1_scales[SHARED:], H)
+        load_words(w1_shared[:, : LAST * 2 * H], w1_words[SHARED, :LAST])
+        load_x(LAST, 1, 0, EARLY)
+        load_x(LAST, 1, EARLY, T)
+        load_planes(w1_routed_planes, w1_scales[:E], H)
+        for s in range(PASSES):
+            load_words(w1_routed[s][:], w1_words[:E, s])
+        load_words(w1_shared[:, LAST * 2 * H :], w1_words[SHARED, LAST:])
+        load_words(w2_codes[:], w2_words[:, 0])
+        load_planes(w2_planes, w2_scales, N)
+        nc.sync.dma_start(gate_sb[:], gate)
 
         def copy(engine, dst, src):
-            if engine == "vector":
-                nc.vector.tensor_copy(dst, src)
-            elif engine == "gpsimd":
-                nc.gpsimd.tensor_copy(dst, src)
-            else:
+            if engine is nc.scalar:
                 nc.scalar.copy(dst, src)
+            else:
+                engine.tensor_copy(dst, src)
 
         def round_x(engine, s, u, first, end):
             copy(
                 engine,
-                x_pairs[s][:, 2 * (T * u + first) : 2 * (T * u + end)].rearrange("p (t d) -> p t d", d=2),
+                x_pairs[s][:, T * u + first : T * u + end].bitcast(BF16).rearrange("p (t d) -> p t d", d=2),
                 x_raw[s, u][:].rearrange("p (d t) -> p t d", d=2)[:, first:end],
             )
 
         def gather(s, u, first, end):
             nc.vector.tensor_copy(
-                slot_pairs[s][:, 2 * (S * u + first) : 2 * (S * u + end)].bitcast(U32),
-                x_pairs[s][:, 2 * T * u : 2 * T * (u + 1)].bitcast(U32).indirect(offsets[:, first // 16 : end // 16]),
+                slot_pairs[s][:, S * u + first : S * u + end],
+                x_pairs[s][:, T * u : T * (u + 1)].indirect(offsets[:, first // 16 : end // 16]),
             )
 
-        def staged(kind, s, first, end):
-
-            return quads[kind, s][:, 4 * first : 4 * end]
-
-        def plane_of(kind, s, first, end):
-            if (kind, s) == ("slot", 0):
-                return planes["token", last][:, first:end]
-            if kind == "token" and first >= EARLY:
-                place = PASSES * (first - EARLY) // P + s
-                if place < 4:
-                    return planes["slot", last][:, P * place : P * (place + 1)]
-                return late_planes[:, P * (place - 4) : P * (place - 3)]
-            return planes[kind, s][:, first:end]
-
-        def codes_of(kind, s, first, end):
-            if kind == "token" and first >= EARLY:
-                place = PASSES * (first - EARLY) // P + s
-                if place < 4:
-                    return late_codes[:, P * place : P * (place + 1)]
-                return codes["slot", last][:, C:][:, P * (place - 4) : P * (place - 3)]
-            return codes[kind, s][:, first:end]
-
-        def interleave(engine, kind, s, first, end):
+        def make_quads(engine, kind, s, first, end):
+            word = I32 if engine is nc.gpsimd else F32
             pairs = slot_pairs[s] if kind == "slot" else x_pairs[s]
-            word = I32 if engine == "gpsimd" else F32
-            words = pairs[:].bitcast(word).rearrange("p (u c) -> p c u", u=2)
             copy(
                 engine,
-                staged(kind, s, first, end).bitcast(word).rearrange("p (c u) -> p c u", u=2),
-                words[:, first:end],
+                quads[kind, s][:].bitcast(word).rearrange("p (c u) -> p c u", u=2)[:, first:end],
+                pairs[:].bitcast(word).rearrange("p (u c) -> p c u", u=2)[:, first:end],
             )
 
-        def quantise_x(kind, s, first, end):
-            nc.vector.quantize_mx(
-                out=codes_of(kind, s, first, end).bitcast(FP8X4),
-                scales=plane_of(kind, s, first, end),
-                in_=staged(kind, s, first, end),
-            )
-
-        late_quads = x_raw[last, 1][:].bitcast(BF16)
-
-        def interleave_late(engine, s):
-            copy(
-                engine,
-                x_raw[last, 1][:].rearrange("p (b s c u) -> p s b c u", b=2, s=PASSES, u=2)[:, s],
+        def make_late_quads(s):
+            nc.scalar.copy(
+                late_quads.bitcast(F32).rearrange("p (b s c u) -> p s b c u", b=2, s=PASSES, u=2)[:, s],
                 x_pairs[s][:].bitcast(F32).rearrange("p (u b c) -> p b c u", u=2, c=P)[:, EARLY // P :],
             )
 
-        def quantise_late(part):
-            if part == 0:
-                nc.vector.quantize_mx(out=late_codes[:].bitcast(FP8X4), scales=planes["slot", last][:], in_=late_quads[:, : 16 * P])
-            else:
-                nc.vector.quantize_mx(out=codes["slot", last][:, C:][:, : 2 * P].bitcast(FP8X4), scales=late_planes[:], in_=late_quads[:, 16 * P :])
+        def quantise(words, code, plane):
+            nc.vector.quantize_mx(out=code.bitcast(FP8X4), scales=plane, in_=words.bitcast(BF16))
 
-        def expert_of(kind, block):
-            return block * P // C if kind == "slot" else SHARED
+        def quantise_x(kind, s, first, end):
+            quantise(quads[kind, s][:, 2 * first : 2 * end], codes[kind, s][:, first:end], planes[kind, s][:, first:end])
 
-        sums = {}
+        sums, y = {}, {}
 
-        def first_layer(kind, block, s):
+        def first_product(kind, block, s):
             if s == 0:
-                sums[kind, block] = psum.tile([P, H], F32, tag=f"bank{BANK[kind, block]}", bufs=1, name="sums")
-            e = expert_of(kind, block)
-            if e == SHARED:
-                words, plane = w1_shared[:, 2 * H * s : 2 * H * (s + 1)], shared_planes[:, H * s : H * (s + 1)]
+                sums[kind, block] = in_bank(sum_bank(kind, block), [P, H], "sums")
+            if block * P < EARLY:
+                code, plane, place = codes[kind, s], planes[kind, s], block
             else:
+                call, place = divmod(PASSES * (block - EARLY // P) + s, 4)
+                code, plane = late_codes[call], late_planes[call]
+            if kind == "token":
+                w1, w1_plane = w1_shared[:, 2 * H * s : 2 * H * (s + 1)], w1_shared_planes[:, H * s : H * (s + 1)]
+            else:
+                e = block * P // C
                 a = PASSES * e + s
-                words, plane = w1_codes[s][:, 2 * H * e : 2 * H * (e + 1)], routed_planes[:, H * a : H * (a + 1)]
+                w1, w1_plane = w1_routed[s][:, 2 * H * e : 2 * H * (e + 1)], w1_routed_planes[:, H * a : H * (a + 1)]
             nc.tensor.matmul_mx(
                 out=sums[kind, block][:],
-                lhsT=codes_of(kind, s, P * block, P * (block + 1)).bitcast(FP8X4),
-                lhsT_scale=plane_of(kind, s, P * block, P * (block + 1)),
-                rhs=words.bitcast(FP4X4),
-                rhs_scale=plane,
+                lhsT=code[:, P * place : P * (place + 1)].bitcast(FP8X4),
+                lhsT_scale=plane[:, P * place : P * (place + 1)],
+                rhs=w1.bitcast(FP4X4),
+                rhs_scale=w1_plane,
                 start=(s == 0),
-                stop=(s == last),
+                stop=(s == LAST),
             )
 
         def relu(engine, kind, block):
             dst = h_rows[kind, block][:].rearrange("c (u p d) -> c u p d", u=2, d=2)
             src = sums[kind, block][:].rearrange("c (p u d) -> c u p d", u=2, d=2)
-            if engine == "vector":
-                nc.vector.tensor_scalar_max(dst, src, 0.0)
-            else:
+            if engine is nc.scalar:
                 nc.scalar.activation(dst, src, RELU)
+            else:
+                nc.vector.tensor_scalar_max(dst, src, 0.0)
 
-        turned = {}
-
-        def turn(unit):
-            kind, first, blocks, bank = UNITS[unit][:4]
-            turned[unit] = psum.tile([P, blocks, 2, P], F32, tag=f"bank{bank}", bufs=1, name="turned")
-            for b in reversed(range(blocks)):
+        def turn(kind, first, end, bank):
+            turned = in_bank(bank, [P, end - first, 2, P], "turned")
+            for b in reversed(range(end - first)):
                 words = h_rows[kind, first + b][:].bitcast(F32)
                 for u in range(2):
-                    nc.tensor.transpose(turned[unit][:, b, u, :], words[:, P * u : P * (u + 1)], ident[:])
-
-        def columns_of(unit):
-            first, blocks = UNITS[unit][1:3]
-            return slice(P * first, P * (first + blocks))
-
-        def spread(engine, unit):
-            copy(
-                engine,
-                h_quads[unit][:].bitcast(F32).rearrange("p (b c u) -> p b c u", c=P, u=2),
-                turned[unit][:].rearrange("p b u c -> p b c u"),
+                    nc.tensor.transpose(turned[:, b, u, :], words[:, P * u : P * (u + 1)], ident[:])
+            nc.scalar.copy(
+                h_quads[kind, first // 2][:].rearrange("p (b c u) -> p b c u", c=P, u=2)[:, first % 2 : first % 2 + end - first],
+                turned[:].rearrange("p b u c -> p b c u"),
             )
 
-        def quantise_h(unit):
-            nc.vector.quantize_mx(out=h_codes[unit][:].bitcast(FP8X4), scales=h_planes[unit][:], in_=h_quads[unit][:])
+        def quantise_h(kind, unit):
+            quantise(h_quads[kind, unit][:], h_codes[kind, unit][:], h_planes[kind, unit][:])
 
-        y = {}
-
-        def second_layer(unit):
-            kind, first, blocks, tb, bank = UNITS[unit]
-            e = expert_of(kind, first)
-            if unit in ("t0","t1"):
-                if "pair" not in y:
-                    y["pair"] = psum.tile([P, 2 * UNIT], F32, tag=f"bank{bank}", bufs=1, name="y")
-                y[unit] = y["pair"][:, columns_of(unit)]
-            else:
-                y[unit] = psum.tile([P, blocks * P], F32, tag=f"bank{bank}", bufs=1, name="y")[:]
+        def second_product(kind, unit, dst):
+            e = unit if kind == "slot" else SHARED
+            y[kind, unit] = dst
             nc.tensor.matmul_mx(
-                out=y[unit],
-                lhsT=w2_codes[:, e, :].bitcast(FP4X4),
-                lhsT_scale=w2_planes[:, e, :],
-                rhs=h_codes[unit][:].bitcast(FP8X4),
-                rhs_scale=h_planes[unit][:],
+                out=dst,
+                lhsT=w2_codes[:, 2 * N * e : 2 * N * (e + 1)].bitcast(FP4X4),
+                lhsT_scale=w2_planes[:, N * e : N * (e + 1)],
+                rhs=h_codes[kind, unit][:].bitcast(FP8X4),
+                rhs_scale=h_planes[kind, unit][:],
                 start=True,
                 stop=True,
             )
 
-        def take_y(engine, unit):
-            copy(engine, routed_y[:, columns_of(unit)], y[unit])
-
-        def scatter(first, end):
+        def put_back(engine, first, end):
+            copy(engine, routed_y[:, first:end], y["slot", first // C][:, first % C : first % C + end - first])
             nc.vector.tensor_tensor(
-                routed[:].indirect(offsets[:, first // 16 : end // 16]), routed_y[:, first:end], gate_sb[:, first:end], MULT
+                routed[:].indirect(offsets[:, first // 16 : end // 16]),
+                routed_y[:, first:end],
+                gate_sb[:, first:end],
+                MULT,
             )
-
-        def finish(unit):
-            columns = columns_of(unit)
-            nc.vector.tensor_tensor(result[:, columns], y[unit], routed[:, columns], ADD)
-            nc.sync.dma_start(out[:, columns], result[:, columns])
 
         for s in range(PASSES):
             for u in range(2):
                 if s == 0:
-                    round_x("scalar", s, u, 0, 192 if u else UNIT)
-                    round_x("vector", s, u, 192 if u else UNIT, T)
-                elif u == 1:
-                    round_x("scalar", s, u, 0, EARLY)
-                    round_x("scalar", s, u, EARLY, T)
+                    round_x(nc.scalar, s, u, 0, SCALAR_ROUNDS)
+                    round_x(nc.vector, s, u, SCALAR_ROUNDS, T)
+                elif (s, u) == (LAST, 1):
+                    round_x(nc.scalar, s, u, 0, EARLY)
+                    round_x(nc.scalar, s, u, EARLY, T)
                 else:
-                    round_x("scalar", s, u, 0, T)
+                    round_x(nc.scalar, s, u, 0, T)
                 if u == 0:
                     gather(s, u, 0, S)
             for e in range(E):
                 gather(s, 1, C * e, C * (e + 1))
             for e in range(E):
-                interleave("vector", "slot", s, C * e, C * (e + 1))
+                make_quads(nc.vector, "slot", s, C * e, C * (e + 1))
             for e in range(E):
                 quantise_x("slot", s, C * e, C * (e + 1))
-            if s < last:
-                if s == 0:
-                    interleave("scalar", "token", s, 0, 192)
-                    interleave("scalar", "token", s, 192, EARLY)
-                else:
-                    interleave("scalar", "token", s, 0, EARLY)
+            if s < LAST:
+                make_quads(nc.scalar, "token", s, 0, SCALAR_QUADS)
+                make_quads(nc.gpsimd, "token", s, SCALAR_QUADS, EARLY)
                 quantise_x("token", s, 0, EARLY)
-                for block in range(4):
-                    first_layer("token", block, s)
-        for block in range(4):
-            first_layer("slot", block, 0)
+                for block in range(EARLY // P):
+                    first_product("token", block, s)
+
+        for block in range(S // P):
+            first_product("slot", block, 0)
         for e in range(E):
             for s in range(1, PASSES):
                 for block in (2 * e, 2 * e + 1):
-                    first_layer("slot", block, s)
-        for unit in ("e0", "e1"):
-            first = UNITS[unit][1]
-            for block in (first, first + 1):
-                relu("vector" if block % 2 else "scalar", "slot", block)
-            turn(unit)
-            spread("scalar", unit)
-            quantise_h(unit)
-            second_layer(unit)
-            if unit == "e0":
-                take_y("vector", unit)
-                scatter(0, C)
+                    first_product("slot", block, s)
+        for e in range(E):
+            relu(nc.scalar, "slot", 2 * e)
+            relu(nc.vector, "slot", 2 * e + 1)
+            if e == 0:
+                for block in (0, 1):
+                    turn("slot", block, block + 1, sum_bank("slot", block))
+            else:
+                turn("slot", 2, 4, sum_bank("slot", 3))
+            quantise_h("slot", e)
+            second_product("slot", e, in_bank(sum_bank("slot", 2 * e + 1), [P, UNIT], "y")[:])
+            if e == 0:
+                put_back(nc.vector, 0, C)
 
-        def put_back(block):
-            copy("scalar", routed_y[:, P * block : P * (block + 1)], y["e1"][:, P * (block - 2) : P * (block - 1)])
-            scatter(P * block, P * (block + 1))
-
-        interleave("scalar", "token", last, 0, EARLY)
-        quantise_x("token", last, 0, EARLY)
-        for block in range(4):
-            first_layer("token", block, last)
+        make_quads(nc.scalar, "token", LAST, 0, EARLY)
+        quantise_x("token", LAST, 0, EARLY)
+        for block in range(EARLY // P):
+            first_product("token", block, LAST)
         for s in range(PASSES):
-            interleave_late("scalar", s)
-        quantise_late(0)
-        quantise_late(1)
-        for block in (4, 5):
+            make_late_quads(s)
+        quantise(late_quads[:, : 8 * P], late_codes[0], late_planes[0])
+        quantise(late_quads[:, 8 * P :], late_codes[1], late_planes[1])
+        for block in range(EARLY // P, T // P):
             for s in range(PASSES):
-                first_layer("token", block, s)
-        tokens = ("t0", "t1", "t2")
+                first_product("token", block, s)
         for block in range(T // P):
-            relu("vector" if block in (1,) else "scalar", "token", block)
-        put_back(2)
-        for unit in tokens:
-            turn(unit)
-            spread("scalar", unit)
-            quantise_h(unit)
-            if unit == "t1":
-                put_back(3)
-        for unit in tokens:
-            second_layer(unit)
-        for unit in tokens:
-            finish(unit)
+            relu(nc.vector if block == 1 else nc.scalar, "token", block)
+
+        put_back(nc.scalar, C, C + P)
+        turn("token", 0, 2, sum_bank("token", 3))
+        quantise_h("token", 0)
+        turn("token", 2, 4, sum_bank("token", 2))
+        quantise_h("token", 1)
+        put_back(nc.scalar, C + P, S)
+        turn("token", 4, 6, sum_bank("token", 5))
+        quantise_h("token", 2)
+
+        early_y = in_bank(sum_bank("token", 2), [P, EARLY], "y")
+        second_product("token", 0, early_y[:, :UNIT])
+        second_product("token", 1, early_y[:, UNIT:])
+        second_product("token", 2, in_bank(sum_bank("slot", 0), [P, UNIT], "y")[:])
+        for unit in range(T // UNIT):
+            columns = slice(UNIT * unit, UNIT * (unit + 1))
+            nc.vector.tensor_tensor(result[:, columns], y["token", unit], routed[:, columns], ADD)
+            nc.sync.dma_start(out[:, columns], result[:, columns])

@@ -14,7 +14,7 @@ SCALE_ROWS = 4
 SHARED = E
 UNIT = 2 * P
 EARLY = 2 * UNIT
-SCALAR_ROUNDS = T // 3
+SCALAR_ROUNDS = (T // 3, T // 2)
 SCALAR_QUADS = P
 
 FLOPS = 2 * (S + T) * (K * H + H * N)
@@ -78,6 +78,7 @@ def tile_moe_shr_mlp_relu_kernel(
         for s in range(PASSES):
             planes["slot", s] = sbuf(S, U8, f"slot_plane{s}")
         slot_pairs[LAST] = quads["token", LAST - 1]
+        handed_quads = x_raw[LAST, 0][:, : 2 * C].bitcast(U32)
         planes["token", LAST] = planes["slot", 0]
         late_quads = x_raw[LAST, 1][:].bitcast(U32)
         late_codes = [sbuf(4 * P, U32, "late_codes")[:], codes["slot", LAST][:, C:]]
@@ -154,12 +155,17 @@ def tile_moe_shr_mlp_relu_kernel(
                 x_pairs[s][:, T * u : T * (u + 1)].indirect(offsets[:, first // 16 : end // 16]),
             )
 
+        def quads_of(kind, s, first, end):
+            if (kind, s, first) == ("slot", LAST - 1, C):
+                return handed_quads
+            return quads[kind, s][:, 2 * first : 2 * end]
+
         def make_quads(engine, kind, s, first, end):
             word = I32 if engine is nc.gpsimd else F32
             pairs = slot_pairs[s] if kind == "slot" else x_pairs[s]
             copy(
                 engine,
-                quads[kind, s][:].bitcast(word).rearrange("p (c u) -> p c u", u=2)[:, first:end],
+                quads_of(kind, s, first, end).bitcast(word).rearrange("p (c u) -> p c u", u=2),
                 pairs[:].bitcast(word).rearrange("p (u c) -> p c u", u=2)[:, first:end],
             )
 
@@ -173,7 +179,7 @@ def tile_moe_shr_mlp_relu_kernel(
             nc.vector.quantize_mx(out=code.bitcast(FP8X4), scales=plane, in_=words.bitcast(BF16))
 
         def quantise_x(kind, s, first, end):
-            quantise(quads[kind, s][:, 2 * first : 2 * end], codes[kind, s][:, first:end], planes[kind, s][:, first:end])
+            quantise(quads_of(kind, s, first, end), codes[kind, s][:, first:end], planes[kind, s][:, first:end])
 
         sums, y = {}, {}
 
@@ -245,30 +251,53 @@ def tile_moe_shr_mlp_relu_kernel(
                 MULT,
             )
 
-        for s in range(PASSES):
-            for u in range(2):
-                if s == 0:
-                    round_x(nc.scalar, s, u, 0, SCALAR_ROUNDS)
-                    round_x(nc.vector, s, u, SCALAR_ROUNDS, T)
-                elif (s, u) == (LAST, 1):
-                    round_x(nc.scalar, s, u, 0, EARLY)
-                    round_x(nc.scalar, s, u, EARLY, T)
-                else:
-                    round_x(nc.scalar, s, u, 0, T)
-                if u == 0:
-                    gather(s, u, 0, S)
+        def round_in_two(s, u):
+            round_x(nc.scalar, s, u, 0, EARLY)
+            round_x(nc.scalar, s, u, EARLY, T)
+
+        def gather_by_expert(s):
             for e in range(E):
                 gather(s, 1, C * e, C * (e + 1))
-            for e in range(E):
-                make_quads(nc.vector, "slot", s, C * e, C * (e + 1))
-            for e in range(E):
-                quantise_x("slot", s, C * e, C * (e + 1))
-            if s < LAST:
-                make_quads(nc.scalar, "token", s, 0, SCALAR_QUADS)
-                make_quads(nc.gpsimd, "token", s, SCALAR_QUADS, EARLY)
-                quantise_x("token", s, 0, EARLY)
-                for block in range(EARLY // P):
-                    first_product("token", block, s)
+
+        def early_products(s):
+            for block in range(EARLY // P):
+                first_product("token", block, s)
+
+        for u in range(2):
+            round_x(nc.scalar, 0, u, 0, SCALAR_ROUNDS[u])
+            round_x(nc.vector, 0, u, SCALAR_ROUNDS[u], T)
+            if u == 0:
+                gather(0, 0, 0, S)
+        gather_by_expert(0)
+        make_quads(nc.vector, "slot", 0, 0, C)
+        make_quads(nc.vector, "slot", 0, C, S)
+        quantise_x("slot", 0, 0, C)
+        make_quads(nc.scalar, "token", 0, 0, SCALAR_QUADS)
+        make_quads(nc.gpsimd, "token", 0, SCALAR_QUADS, EARLY)
+        quantise_x("token", 0, 0, EARLY)
+        quantise_x("slot", 0, C, S)
+        early_products(0)
+
+        round_x(nc.scalar, 1, 0, 0, T)
+        gather(1, 0, 0, S)
+        round_in_two(1, 1)
+        gather_by_expert(1)
+        make_quads(nc.vector, "slot", 1, 0, C)
+        quantise_x("slot", 1, 0, C)
+        make_quads(nc.gpsimd, "token", 1, 0, EARLY)
+        quantise_x("token", 1, 0, EARLY)
+        early_products(1)
+
+        round_in_two(LAST, 0)
+        gather(LAST, 0, 0, S)
+        make_quads(nc.scalar, "slot", 1, C, S)
+        quantise_x("slot", 1, C, S)
+        round_in_two(LAST, 1)
+        gather_by_expert(LAST)
+        make_quads(nc.vector, "slot", LAST, 0, C)
+        make_quads(nc.vector, "slot", LAST, C, S)
+        quantise_x("slot", LAST, 0, C)
+        quantise_x("slot", LAST, C, S)
 
         for block in range(S // P):
             first_product("slot", block, 0)
@@ -300,10 +329,11 @@ def tile_moe_shr_mlp_relu_kernel(
         for block in range(EARLY // P, T // P):
             for s in range(PASSES):
                 first_product("token", block, s)
-        for block in range(T // P):
+        for block in range(T // P - 1):
             relu(nc.vector if block == 1 else nc.scalar, "token", block)
 
         put_back(nc.scalar, C, C + P)
+        relu(nc.scalar, "token", T // P - 1)
         turn("token", 0, 2, sum_bank("token", 3))
         quantise_h("token", 0)
         turn("token", 2, 4, sum_bank("token", 2))

@@ -67,20 +67,22 @@ def tile_moe_shr_mlp_relu_kernel(
         x_raw, x_pairs, slot_pairs, quads, codes, planes = {}, {}, {}, {}, {}, {}
         for s in range(PASSES):
             for u in range(2):
-                x_raw[s, u] = sbuf(2 * T, F32, f"x_raw{s}{u}")
+                spare = 2 * C if (s, u) == (LAST, 1) else 0
+                x_raw[s, u] = sbuf(2 * T + spare, F32, f"x_raw{s}{u}")
             x_pairs[s] = sbuf(2 * T, U32, f"x_pairs{s}")
             for kind in ("slot", "token"):
                 quads[kind, s] = sbuf(2 * EARLY, U32, f"{kind}_quads{s}")
-                codes[kind, s] = sbuf(EARLY, U32, f"{kind}_codes{s}")
+                if (kind, s) != ("slot", 1):
+                    codes[kind, s] = sbuf(EARLY, U32, f"{kind}_codes{s}")
         for s in range(LAST):
-            slot_pairs[s] = sbuf(2 * S, U32, f"slot_pairs{s}")
             planes["token", s] = sbuf(EARLY, U8, f"token_plane{s}")
         for s in range(PASSES):
+            slot_pairs[s] = sbuf(2 * S, U32, f"slot_pairs{s}")
             planes["slot", s] = sbuf(S, U8, f"slot_plane{s}")
-        slot_pairs[LAST] = quads["token", LAST - 1]
-        handed_quads = x_raw[LAST, 0][:, : 2 * C].bitcast(U32)
+        codes["slot", 1] = codes["token", 0]
         planes["token", LAST] = planes["slot", 0]
-        late_quads = x_raw[LAST, 1][:].bitcast(U32)
+        handed_quads = x_raw[LAST, 1][:, : 2 * C].bitcast(U32)
+        late_quads = x_raw[LAST, 1][:, 2 * C :].bitcast(U32)
         late_codes = [sbuf(4 * P, U32, "late_codes")[:], codes["slot", LAST][:, C:]]
         late_planes = [planes["slot", LAST][:], sbuf(2 * P, U8, "late_plane")[:]]
 
@@ -101,7 +103,7 @@ def tile_moe_shr_mlp_relu_kernel(
         def load_x(s, u, first, end):
             rows = xT[K_PASS * s : K_PASS * (s + 1), :].rearrange("(p d) t -> p d t", d=4)
             nc.sync.dma_start(
-                x_raw[s, u][:].rearrange("p (d t) -> p d t", d=2)[:, :, first:end],
+                x_raw[s, u][:, : 2 * T].rearrange("p (d t) -> p d t", d=2)[:, :, first:end],
                 rows[:, 2 * u : 2 * u + 2, first:end],
             )
 
@@ -146,7 +148,7 @@ def tile_moe_shr_mlp_relu_kernel(
             copy(
                 engine,
                 x_pairs[s][:, T * u + first : T * u + end].bitcast(BF16).rearrange("p (t d) -> p t d", d=2),
-                x_raw[s, u][:].rearrange("p (d t) -> p t d", d=2)[:, first:end],
+                x_raw[s, u][:, : 2 * T].rearrange("p (d t) -> p t d", d=2)[:, first:end],
             )
 
         def gather(s, u, first, end):
@@ -156,7 +158,7 @@ def tile_moe_shr_mlp_relu_kernel(
             )
 
         def quads_of(kind, s, first, end):
-            if (kind, s, first) == ("slot", LAST - 1, C):
+            if (kind, s, first) == ("slot", 1, C):
                 return handed_quads
             return quads[kind, s][:, 2 * first : 2 * end]
 
@@ -221,8 +223,9 @@ def tile_moe_shr_mlp_relu_kernel(
                 words = h_rows[kind, first + b][:].bitcast(F32)
                 for u in range(2):
                     nc.tensor.transpose(turned[:, b, u, :], words[:, P * u : P * (u + 1)], ident[:])
+            unit_quads = h_quads[kind, first // 2][:].rearrange("p (b c u) -> p b c u", c=P, u=2)
             nc.scalar.copy(
-                h_quads[kind, first // 2][:].rearrange("p (b c u) -> p b c u", c=P, u=2)[:, first % 2 : first % 2 + end - first],
+                unit_quads[:, first % 2 : first % 2 + end - first],
                 turned[:].rearrange("p b u c -> p b c u"),
             )
 
@@ -288,15 +291,15 @@ def tile_moe_shr_mlp_relu_kernel(
         quantise_x("token", 1, 0, EARLY)
         early_products(1)
 
-        round_in_two(LAST, 0)
+        round_x(nc.scalar, LAST, 0, 0, T)
         gather(LAST, 0, 0, S)
-        make_quads(nc.scalar, "slot", 1, C, S)
-        quantise_x("slot", 1, C, S)
         round_in_two(LAST, 1)
+        make_quads(nc.scalar, "slot", 1, C, S)
         gather_by_expert(LAST)
         make_quads(nc.vector, "slot", LAST, 0, C)
         make_quads(nc.vector, "slot", LAST, C, S)
         quantise_x("slot", LAST, 0, C)
+        quantise_x("slot", 1, C, S)
         quantise_x("slot", LAST, C, S)
 
         for block in range(S // P):

@@ -34,7 +34,7 @@ ADD = mybir.AluOpType.add
 
 
 def sum_bank(kind, block):
-    return block if kind == "slot" else 4 + block % 4
+    return block if kind == "slot" else 4 + block if block < 4 else 1 + block
 
 
 def tile_moe_shr_mlp_relu_kernel(
@@ -60,19 +60,19 @@ def tile_moe_shr_mlp_relu_kernel(
         w1_routed_planes = sbuf(E * PASSES * H, U8, "w1_routed_planes")
         w2_codes = sbuf((E + 1) * 2 * N, U8, "w2_codes")
         w2_planes = sbuf((E + 1) * N, U8, "w2_planes")
-        routed_y = sbuf(S, F32, "routed_y")
         routed = sbuf(T, F32, "routed")
         result = sbuf(T, F32, "result")
 
         x_raw, x_pairs, slot_pairs, quads, codes, planes = {}, {}, {}, {}, {}, {}
         for s in range(PASSES):
             for u in range(2):
-                spare = 2 * C if (s, u) == (LAST, 1) else 0
-                x_raw[s, u] = sbuf(2 * T + spare, F32, f"x_raw{s}{u}")
+                if s < LAST:
+                    x_raw[s, u] = sbuf(2 * T, F32, f"x_raw{s}{u}")
             x_pairs[s] = sbuf(2 * T, U32, f"x_pairs{s}")
             for kind in ("slot", "token"):
-                quads[kind, s] = sbuf(2 * EARLY, U32, f"{kind}_quads{s}")
-                if (kind, s) != ("slot", 1):
+                if s == 0 or (kind, s) == ("slot", LAST):
+                    quads[kind, s] = sbuf(2 * EARLY, U32, f"{kind}_quads{s}")
+                if (kind, s) not in (("slot", 1), ("token", LAST)):
                     codes[kind, s] = sbuf(EARLY, U32, f"{kind}_codes{s}")
         for s in range(LAST):
             planes["token", s] = sbuf(EARLY, U8, f"token_plane{s}")
@@ -80,11 +80,20 @@ def tile_moe_shr_mlp_relu_kernel(
             slot_pairs[s] = sbuf(2 * S, U32, f"slot_pairs{s}")
             planes["slot", s] = sbuf(S, U8, f"slot_plane{s}")
         codes["slot", 1] = codes["token", 0]
-        planes["token", LAST] = planes["slot", 0]
-        handed_quads = x_raw[LAST, 1][:, : 2 * C].bitcast(U32)
-        late_quads = x_raw[LAST, 1][:, 2 * C :].bitcast(U32)
-        late_codes = [sbuf(4 * P, U32, "late_codes")[:], codes["slot", LAST][:, C:]]
-        late_planes = [planes["slot", LAST][:], sbuf(2 * P, U8, "late_plane")[:]]
+        stage = sbuf(2 * EARLY + 4 * T, U32, "stage")
+        quads["token", 1] = stage[:, : 2 * EARLY]
+        x_raw[LAST, 1] = stage[:, 2 * EARLY : 2 * EARLY + 2 * T].bitcast(F32)
+        x_raw[LAST, 0] = stage[:, 2 * EARLY + 2 * T :].bitcast(F32)
+        slot1_quads = [stage[:, 2 * EARLY : 3 * EARLY], stage[:, EARLY : 2 * EARLY]]
+        late_quads = stage[:, 2 * EARLY + 2 * T : 2 * EARLY + 2 * T + 4 * UNIT]
+        late_codes = sbuf(4 * P, U32, "late_codes")[:]
+        late_planes = planes["slot", LAST][:]
+        quads["token", LAST] = sbuf(2 * T, U32, "token_quads2")
+        codes["token", LAST] = sbuf(T, U32, "token_codes2")
+        last_plane = sbuf(2 * S, U8, "last_plane")
+        planes["token", LAST] = last_plane[:, :T]
+        planes["slot", 0] = last_plane[:, :S]
+        plane1 = [sbuf(C, U8, "slot_plane10")[:], last_plane[:, S : S + C]]
 
         h_rows, h_quads, h_codes, h_planes = {}, {}, {}, {}
         for kind, columns in (("slot", S), ("token", T)):
@@ -94,6 +103,8 @@ def tile_moe_shr_mlp_relu_kernel(
                 h_quads[kind, unit] = sbuf(2 * UNIT, F32, f"{kind}_h_quads{unit}")
                 h_codes[kind, unit] = sbuf(UNIT, U32, f"{kind}_h_codes{unit}")
                 h_planes[kind, unit] = sbuf(UNIT, U8, f"{kind}_h_plane{unit}")
+
+        routed_y = [h_rows["slot", 3][:].bitcast(F32), h_rows["token", 1][:].bitcast(F32)]
 
         for tile in (w1_routed_planes, w1_shared_planes, w2_planes):
             nc.vector.memset(tile[:].bitcast(I32), 0)
@@ -128,8 +139,7 @@ def tile_moe_shr_mlp_relu_kernel(
         load_x(LAST, 0, 0, T)
         load_planes(w1_shared_planes, w1_scales[SHARED:], H)
         load_words(w1_shared[:, : LAST * 2 * H], w1_words[SHARED, :LAST])
-        load_x(LAST, 1, 0, EARLY)
-        load_x(LAST, 1, EARLY, T)
+        load_x(LAST, 1, 0, T)
         load_planes(w1_routed_planes, w1_scales[:E], H)
         for s in range(PASSES):
             load_words(w1_routed[s][:], w1_words[:E, s])
@@ -158,8 +168,10 @@ def tile_moe_shr_mlp_relu_kernel(
             )
 
         def quads_of(kind, s, first, end):
-            if (kind, s, first) == ("slot", 1, C):
-                return handed_quads
+            if (kind, s) == ("slot", 1):
+                return slot1_quads[first // C]
+            if (kind, s, first) == ("token", LAST, EARLY):
+                return slot_pairs[LAST][:, C : C + 2 * UNIT]
             return quads[kind, s][:, 2 * first : 2 * end]
 
         def make_quads(engine, kind, s, first, end):
@@ -173,26 +185,36 @@ def tile_moe_shr_mlp_relu_kernel(
 
         def make_late_quads(s):
             nc.scalar.copy(
-                late_quads.bitcast(F32).rearrange("p (b s c u) -> p s b c u", b=2, s=PASSES, u=2)[:, s],
-                x_pairs[s][:].bitcast(F32).rearrange("p (u b c) -> p b c u", u=2, c=P)[:, EARLY // P :],
+                late_quads.bitcast(F32).rearrange("p (a c u) -> p a c u", c=UNIT, u=2)[:, s],
+                x_pairs[s][:].bitcast(F32).rearrange("p (u c) -> p c u", u=2)[:, EARLY:],
             )
 
         def quantise(words, code, plane):
             nc.vector.quantize_mx(out=code.bitcast(FP8X4), scales=plane, in_=words.bitcast(BF16))
 
+        def codes_of(kind, s, first, end):
+            if kind == "slot" and s > 0 and first >= C:
+                return codes[kind, 0][:, (s - 2) * C + first : (s - 2) * C + end]
+            return codes[kind, s][:, first:end]
+
+        def plane_of(kind, s, first, end):
+            if (kind, s) == ("slot", 1):
+                return plane1[first // C][:, first % C : first % C + end - first]
+            return planes[kind, s][:, first:end]
+
         def quantise_x(kind, s, first, end):
-            quantise(quads_of(kind, s, first, end), codes[kind, s][:, first:end], planes[kind, s][:, first:end])
+            quantise(quads_of(kind, s, first, end), codes_of(kind, s, first, end), plane_of(kind, s, first, end))
 
         sums, y = {}, {}
 
         def first_product(kind, block, s):
             if s == 0:
                 sums[kind, block] = in_bank(sum_bank(kind, block), [P, H], "sums")
-            if block * P < EARLY:
-                code, plane, place = codes[kind, s], planes[kind, s], block
+            if block * P < EARLY or s == LAST:
+                code, plane, place = codes_of(kind, s, P * block, P * (block + 1)), plane_of(kind, s, P * block, P * (block + 1)), 0
             else:
-                call, place = divmod(PASSES * (block - EARLY // P) + s, 4)
-                code, plane = late_codes[call], late_planes[call]
+                code, plane, place = None, late_planes, block - EARLY // P + 2 * s
+                code = late_codes[:, P * place : P * (place + 1)]
             if kind == "token":
                 w1, w1_plane = w1_shared[:, 2 * H * s : 2 * H * (s + 1)], w1_shared_planes[:, H * s : H * (s + 1)]
             else:
@@ -201,7 +223,7 @@ def tile_moe_shr_mlp_relu_kernel(
                 w1, w1_plane = w1_routed[s][:, 2 * H * e : 2 * H * (e + 1)], w1_routed_planes[:, H * a : H * (a + 1)]
             nc.tensor.matmul_mx(
                 out=sums[kind, block][:],
-                lhsT=code[:, P * place : P * (place + 1)].bitcast(FP8X4),
+                lhsT=code.bitcast(FP8X4),
                 lhsT_scale=plane[:, P * place : P * (place + 1)],
                 rhs=w1.bitcast(FP4X4),
                 rhs_scale=w1_plane,
@@ -217,14 +239,15 @@ def tile_moe_shr_mlp_relu_kernel(
             else:
                 nc.vector.tensor_scalar_max(dst, src, 0.0)
 
-        def turn(kind, first, end, bank):
+        def turn(kind, first, end, bank, engine=nc.scalar):
             turned = in_bank(bank, [P, end - first, 2, P], "turned")
             for b in reversed(range(end - first)):
                 words = h_rows[kind, first + b][:].bitcast(F32)
                 for u in range(2):
                     nc.tensor.transpose(turned[:, b, u, :], words[:, P * u : P * (u + 1)], ident[:])
             unit_quads = h_quads[kind, first // 2][:].rearrange("p (b c u) -> p b c u", c=P, u=2)
-            nc.scalar.copy(
+            copy(
+                engine,
                 unit_quads[:, first % 2 : first % 2 + end - first],
                 turned[:].rearrange("p b u c -> p b c u"),
             )
@@ -245,11 +268,39 @@ def tile_moe_shr_mlp_relu_kernel(
                 stop=True,
             )
 
-        def put_back(engine, first, end):
-            copy(engine, routed_y[:, first:end], y["slot", first // C][:, first % C : first % C + end - first])
+        def block_chain(block, bank):
+            cols = slice(P * (block % 2), P * (block % 2 + 1))
+            unit = block // 2
+            quantise(h_quads["slot", unit][:, 2 * cols.start : 2 * cols.stop], h_codes["slot", unit][:, cols], h_planes["slot", unit][:, cols])
+            dst = in_bank(bank, [P, P], "y")[:]
+            nc.tensor.matmul_mx(
+                out=dst,
+                lhsT=w2_codes[:, 2 * N * unit : 2 * N * (unit + 1)].bitcast(FP4X4),
+                lhsT_scale=w2_planes[:, N * unit : N * (unit + 1)],
+                rhs=h_codes["slot", unit][:, cols].bitcast(FP8X4),
+                rhs_scale=h_planes["slot", unit][:, cols],
+                start=True,
+                stop=True,
+            )
+            return dst
+
+        def leave(engine, src, first, end):
+            copy(engine, routed_y[:, first:end], src)
+
+        def scatter(first, end):
             nc.vector.tensor_tensor(
                 routed[:].indirect(offsets[:, first // 16 : end // 16]),
                 routed_y[:, first:end],
+                gate_sb[:, first:end],
+                MULT,
+            )
+
+        def put_back(engine, first, end):
+            values = routed_y[first // C][:, first % C : first % C + end - first]
+            copy(engine, values, y["slot", first // C][:, first % C : first % C + end - first])
+            nc.vector.tensor_tensor(
+                routed[:].indirect(offsets[:, first // 16 : end // 16]),
+                values,
                 gate_sb[:, first:end],
                 MULT,
             )
@@ -285,71 +336,71 @@ def tile_moe_shr_mlp_relu_kernel(
         gather(1, 0, 0, S)
         round_in_two(1, 1)
         gather_by_expert(1)
-        make_quads(nc.vector, "slot", 1, 0, C)
-        quantise_x("slot", 1, 0, C)
         make_quads(nc.gpsimd, "token", 1, 0, EARLY)
         quantise_x("token", 1, 0, EARLY)
         early_products(1)
 
-        round_x(nc.scalar, LAST, 0, 0, T)
+        V, A, G = nc.vector, nc.scalar, nc.gpsimd
+        round_x(A, LAST, 0, 0, T)
         gather(LAST, 0, 0, S)
-        round_in_two(LAST, 1)
-        make_quads(nc.scalar, "slot", 1, C, S)
+        make_quads(G, "slot", 1, C, S)
+        make_late_quads(0)
+        make_late_quads(1)
+        round_x(A, LAST, 1, 0, UNIT)
+        round_x(V, LAST, 1, UNIT, T)
         gather_by_expert(LAST)
-        make_quads(nc.vector, "slot", LAST, 0, C)
-        make_quads(nc.vector, "slot", LAST, C, S)
+        make_quads(A, "slot", 1, 0, C)
+        quantise_x("slot", 1, 0, C)
+        make_quads(G, "token", LAST, 0, T // 2)
+        make_quads(A, "token", LAST, T // 2, EARLY)
+        for e in range(E):
+            make_quads(A, "slot", LAST, C * e, C * (e + 1))
+        make_quads(A, "token", LAST, EARLY, T)
         quantise_x("slot", LAST, 0, C)
-        quantise_x("slot", 1, C, S)
-        quantise_x("slot", LAST, C, S)
-
         for block in range(S // P):
             first_product("slot", block, 0)
+        quantise_x("slot", 1, C, S)
+        quantise_x("slot", LAST, C, S)
         for e in range(E):
             for s in range(1, PASSES):
                 for block in (2 * e, 2 * e + 1):
                     first_product("slot", block, s)
-        for e in range(E):
-            relu(nc.scalar, "slot", 2 * e)
-            relu(nc.vector, "slot", 2 * e + 1)
-            if e == 0:
-                for block in (0, 1):
-                    turn("slot", block, block + 1, sum_bank("slot", block))
-            else:
-                turn("slot", 2, 4, sum_bank("slot", 3))
-            quantise_h("slot", e)
-            second_product("slot", e, in_bank(sum_bank("slot", 2 * e + 1), [P, UNIT], "y")[:])
-            if e == 0:
-                put_back(nc.vector, 0, C)
-
-        make_quads(nc.scalar, "token", LAST, 0, EARLY)
+        relu(A, "slot", 0)
+        relu(V, "slot", 1)
+        for block in (0, 1):
+            turn("slot", block, block + 1, block)
+        quantise_h("slot", 0)
+        second_product("slot", 0, in_bank(1, [P, UNIT], "y")[:])
+        relu(A, "slot", 2)
+        relu(V, "slot", 3)
+        turn("slot", 2, 4, 3, V)
+        put_back(V, 0, C)
+        quantise_h("slot", 1)
+        second_product("slot", 1, in_bank(3, [P, UNIT], "y")[:])
         quantise_x("token", LAST, 0, EARLY)
+        quantise_x("token", LAST, EARLY, T)
         for block in range(EARLY // P):
             first_product("token", block, LAST)
-        for s in range(PASSES):
-            make_late_quads(s)
-        quantise(late_quads[:, : 8 * P], late_codes[0], late_planes[0])
-        quantise(late_quads[:, 8 * P :], late_codes[1], late_planes[1])
+        quantise(late_quads, late_codes, late_planes)
+        relu(A, "token", 0)
+        relu(A, "token", 1)
+        turn("token", 0, 2, 0)
+        quantise_h("token", 0)
+        put_back(A, C, S)
         for block in range(EARLY // P, T // P):
             for s in range(PASSES):
                 first_product("token", block, s)
-        for block in range(T // P - 1):
-            relu(nc.vector if block == 1 else nc.scalar, "token", block)
-
-        put_back(nc.scalar, C, C + P)
-        relu(nc.scalar, "token", T // P - 1)
-        turn("token", 0, 2, sum_bank("token", 3))
-        quantise_h("token", 0)
-        turn("token", 2, 4, sum_bank("token", 2))
+        for block in range(2, T // P):
+            relu(A, "token", block)
+        turn("token", 2, 4, 7)
         quantise_h("token", 1)
-        put_back(nc.scalar, C + P, S)
-        turn("token", 4, 6, sum_bank("token", 5))
+        turn("token", 4, 5, 5)
+        turn("token", 5, 6, 6)
         quantise_h("token", 2)
-
-        early_y = in_bank(sum_bank("token", 2), [P, EARLY], "y")
-        second_product("token", 0, early_y[:, :UNIT])
-        second_product("token", 1, early_y[:, UNIT:])
-        second_product("token", 2, in_bank(sum_bank("slot", 0), [P, UNIT], "y")[:])
+        for unit, bank in enumerate((7, 5, 2)):
+            second_product("token", unit, in_bank(bank, [P, UNIT], "y")[:])
         for unit in range(T // UNIT):
             columns = slice(UNIT * unit, UNIT * (unit + 1))
-            nc.vector.tensor_tensor(result[:, columns], y["token", unit], routed[:, columns], ADD)
-            nc.sync.dma_start(out[:, columns], result[:, columns])
+            dst = h_quads["token", 2][:, columns] if unit < 2 else result[:, columns]
+            nc.vector.tensor_tensor(dst, y["token", unit], routed[:, columns], ADD)
+            nc.sync.dma_start(out[:, columns], dst)

@@ -15,7 +15,7 @@ SHARED = E
 UNIT = 2 * P
 EARLY = 2 * UNIT
 SCALAR_ROUNDS = (T // 3, T // 2)
-SCALAR_QUADS = P
+SCALAR_QUADS = 2 * P
 
 FLOPS = 2 * (S + T) * (K * H + H * N)
 
@@ -66,11 +66,11 @@ def tile_moe_shr_mlp_relu_kernel(
         x_raw, x_pairs, slot_pairs, quads, codes, planes = {}, {}, {}, {}, {}, {}
         for s in range(PASSES):
             for u in range(2):
-                if s < LAST:
+                if True:
                     x_raw[s, u] = sbuf(2 * T, F32, f"x_raw{s}{u}")
             x_pairs[s] = sbuf(2 * T, U32, f"x_pairs{s}")
             for kind in ("slot", "token"):
-                if s == 0 or (kind, s) == ("slot", LAST):
+                if (kind, s) in (("token", 0), ("slot", LAST)):
                     quads[kind, s] = sbuf(2 * EARLY, U32, f"{kind}_quads{s}")
                 if (kind, s) not in (("slot", 1), ("token", LAST)):
                     codes[kind, s] = sbuf(EARLY, U32, f"{kind}_codes{s}")
@@ -80,12 +80,11 @@ def tile_moe_shr_mlp_relu_kernel(
             slot_pairs[s] = sbuf(2 * S, U32, f"slot_pairs{s}")
             planes["slot", s] = sbuf(S, U8, f"slot_plane{s}")
         codes["slot", 1] = codes["token", 0]
-        stage = sbuf(2 * EARLY + 4 * T, U32, "stage")
-        quads["token", 1] = stage[:, : 2 * EARLY]
-        x_raw[LAST, 1] = stage[:, 2 * EARLY : 2 * EARLY + 2 * T].bitcast(F32)
-        x_raw[LAST, 0] = stage[:, 2 * EARLY + 2 * T :].bitcast(F32)
-        slot1_quads = [stage[:, 2 * EARLY : 3 * EARLY], stage[:, EARLY : 2 * EARLY]]
-        late_quads = stage[:, 2 * EARLY + 2 * T : 2 * EARLY + 2 * T + 4 * UNIT]
+        first_quads = sbuf(2 * C + 2 * EARLY, U32, "first_quads")
+        quads["slot", 0] = first_quads[:, : 2 * S]
+        quads["token", 1] = first_quads[:, 2 * C :]
+        slot1_quads = [x_raw[LAST, 1][:, : 2 * C].bitcast(U32), sbuf(2 * C, U32, "slot_quads11")[:]]
+        late_quads = x_raw[LAST, 0][:, : 4 * UNIT].bitcast(U32)
         late_codes = sbuf(4 * P, U32, "late_codes")[:]
         late_planes = planes["slot", LAST][:]
         quads["token", LAST] = sbuf(2 * T, U32, "token_quads2")
@@ -334,9 +333,11 @@ def tile_moe_shr_mlp_relu_kernel(
 
         round_x(nc.scalar, 1, 0, 0, T)
         gather(1, 0, 0, S)
-        round_in_two(1, 1)
-        gather_by_expert(1)
-        make_quads(nc.gpsimd, "token", 1, 0, EARLY)
+        for unit in range(T // UNIT):
+            round_x(nc.scalar, 1, 1, UNIT * unit, UNIT * (unit + 1))
+        gather(1, 1, 0, S)
+        for unit in range(EARLY // UNIT):
+            make_quads(nc.gpsimd, "token", 1, UNIT * unit, UNIT * (unit + 1))
         quantise_x("token", 1, 0, EARLY)
         early_products(1)
 

@@ -63,12 +63,13 @@ def tile_moe_shr_mlp_relu_kernel(
         routed = sbuf(T, F32, "routed")
         result = sbuf(T, F32, "result")
 
+        both_pairs = sbuf(4 * T, U32, "both_pairs")
         x_raw, x_pairs, slot_pairs, quads, codes, planes = {}, {}, {}, {}, {}, {}
         for s in range(PASSES):
             for u in range(2):
-                if True:
+                if s < LAST:
                     x_raw[s, u] = sbuf(2 * T, F32, f"x_raw{s}{u}")
-            x_pairs[s] = sbuf(2 * T, U32, f"x_pairs{s}")
+            x_pairs[s] = both_pairs[:, 2 * T * s : 2 * T * (s + 1)] if s < LAST else sbuf(2 * T, U32, f"x_pairs{s}")
             for kind in ("slot", "token"):
                 if (kind, s) in (("token", 0), ("slot", LAST)):
                     quads[kind, s] = sbuf(2 * EARLY, U32, f"{kind}_quads{s}")
@@ -77,22 +78,35 @@ def tile_moe_shr_mlp_relu_kernel(
         for s in range(LAST):
             planes["token", s] = sbuf(EARLY, U8, f"token_plane{s}")
         for s in range(PASSES):
-            slot_pairs[s] = sbuf(2 * S, U32, f"slot_pairs{s}")
+            if s < LAST:
+                slot_pairs[s] = sbuf(2 * S, U32, f"slot_pairs{s}")
             planes["slot", s] = sbuf(S, U8, f"slot_plane{s}")
         codes["slot", 1] = codes["token", 0]
         first_quads = sbuf(2 * C + 2 * EARLY, U32, "first_quads")
         quads["slot", 0] = first_quads[:, : 2 * S]
         quads["token", 1] = first_quads[:, 2 * C :]
-        slot1_quads = [x_raw[LAST, 1][:, : 2 * C].bitcast(U32), sbuf(2 * C, U32, "slot_quads11")[:]]
-        late_quads = x_raw[LAST, 0][:, : 4 * UNIT].bitcast(U32)
+        last_load = sbuf(2 * C - P + 2 * T, F32, "last_load")
+        x_raw[LAST, 1] = last_load[:, 2 * C - P :]
+        slot1_quads = [last_load[:, : 2 * C].bitcast(U32), sbuf(2 * C, U32, "slot_quads11")[:]]
+        fifth_load = sbuf(3 * UNIT + 2 * T, F32, "fifth_load")
+        x_raw[LAST, 0] = fifth_load[:, 3 * UNIT :]
+        late_quads = fifth_load[:, : 4 * UNIT].bitcast(U32)
+        last_pairs = sbuf(2 * UNIT + 2 * S, U32, "last_pairs")
+        slot_pairs[LAST] = last_pairs[:, 2 * UNIT :]
         late_codes = sbuf(4 * P, U32, "late_codes")[:]
-        late_planes = planes["slot", LAST][:]
-        quads["token", LAST] = sbuf(2 * T, U32, "token_quads2")
-        codes["token", LAST] = sbuf(T, U32, "token_codes2")
-        last_plane = sbuf(2 * S, U8, "last_plane")
-        planes["token", LAST] = last_plane[:, :T]
-        planes["slot", 0] = last_plane[:, :S]
-        plane1 = [sbuf(C, U8, "slot_plane10")[:], last_plane[:, S : S + C]]
+        late_planes = sbuf(4 * P, U8, "late_planes")[:]
+        plane1 = [sbuf(C, U8, "slot_plane10")[:], late_planes[:, :C]]
+        last_plane = sbuf(S + P, U8, "last_plane")
+        planes["slot", LAST] = last_plane[:, :S]
+        joint_quads = sbuf(6 * P, U32, "joint_quads")
+        joint_codes = sbuf(3 * P, U32, "joint_codes")
+        joint_plane = sbuf(3 * P, U8, "joint_plane")
+        last_calls = [
+            (sbuf(2 * UNIT, U32, "token_quads2")[:], sbuf(UNIT, U32, "token_codes2")[:], planes["slot", 0][:, C:]),
+            (last_pairs[:, : 6 * P], sbuf(3 * P, U32, "token_codes3")[:], last_plane[:, C:]),
+            (joint_quads[:], joint_codes[:], joint_plane[:]),
+        ]
+        last_place = ((0, 0), (0, 1), (1, 0), (2, 2), (1, 1), (1, 2))
 
         h_rows, h_quads, h_codes, h_planes = {}, {}, {}, {}
         for kind, columns in (("slot", S), ("token", T)):
@@ -103,6 +117,9 @@ def tile_moe_shr_mlp_relu_kernel(
                 h_codes[kind, unit] = sbuf(UNIT, U32, f"{kind}_h_codes{unit}")
                 h_planes[kind, unit] = sbuf(UNIT, U8, f"{kind}_h_plane{unit}")
 
+        h_quads["slot", 0] = joint_quads[:, : 2 * UNIT].bitcast(F32)
+        h_codes["slot", 0] = joint_codes[:, :UNIT]
+        h_planes["slot", 0] = joint_plane[:, :UNIT]
         routed_y = [h_rows["slot", 3][:].bitcast(F32), h_rows["token", 1][:].bitcast(F32)]
 
         for tile in (w1_routed_planes, w1_shared_planes, w2_planes):
@@ -169,8 +186,9 @@ def tile_moe_shr_mlp_relu_kernel(
         def quads_of(kind, s, first, end):
             if (kind, s) == ("slot", 1):
                 return slot1_quads[first // C]
-            if (kind, s, first) == ("token", LAST, EARLY):
-                return slot_pairs[LAST][:, C : C + 2 * UNIT]
+            if (kind, s) == ("token", LAST):
+                call, place = last_place[first // P]
+                return last_calls[call][0][:, 2 * P * place : 2 * P * place + 2 * (end - first)]
             return quads[kind, s][:, 2 * first : 2 * end]
 
         def make_quads(engine, kind, s, first, end):
@@ -184,8 +202,8 @@ def tile_moe_shr_mlp_relu_kernel(
 
         def make_late_quads(s):
             nc.scalar.copy(
-                late_quads.bitcast(F32).rearrange("p (a c u) -> p a c u", c=UNIT, u=2)[:, s],
-                x_pairs[s][:].bitcast(F32).rearrange("p (u c) -> p c u", u=2)[:, EARLY:],
+                late_quads.bitcast(F32).rearrange("p (a c u) -> p a c u", c=UNIT, u=2),
+                both_pairs[:].bitcast(F32).rearrange("p (a u c) -> p a c u", a=2, u=2)[:, :, EARLY:],
             )
 
         def quantise(words, code, plane):
@@ -194,11 +212,17 @@ def tile_moe_shr_mlp_relu_kernel(
         def codes_of(kind, s, first, end):
             if kind == "slot" and s > 0 and first >= C:
                 return codes[kind, 0][:, (s - 2) * C + first : (s - 2) * C + end]
+            if (kind, s) == ("token", LAST):
+                call, place = last_place[first // P]
+                return last_calls[call][1][:, P * place : P * (place + 1)]
             return codes[kind, s][:, first:end]
 
         def plane_of(kind, s, first, end):
             if (kind, s) == ("slot", 1):
                 return plane1[first // C][:, first % C : first % C + end - first]
+            if (kind, s) == ("token", LAST):
+                call, place = last_place[first // P]
+                return last_calls[call][2][:, P * place : P * (place + 1)]
             return planes[kind, s][:, first:end]
 
         def quantise_x(kind, s, first, end):
@@ -342,18 +366,20 @@ def tile_moe_shr_mlp_relu_kernel(
         early_products(1)
 
         V, A, G = nc.vector, nc.scalar, nc.gpsimd
-        round_x(A, LAST, 0, 0, T)
+        round_x(A, LAST, 0, 0, UNIT)
+        round_x(A, LAST, 0, UNIT, T)
         gather(LAST, 0, 0, S)
         make_quads(G, "slot", 1, C, S)
-        make_late_quads(0)
-        make_late_quads(1)
-        round_x(A, LAST, 1, 0, UNIT)
-        round_x(V, LAST, 1, UNIT, T)
+        make_late_quads(None)
+        round_x(A, LAST, 1, 0, P)
+        round_x(A, LAST, 1, P, 352)
+        round_x(V, LAST, 1, 352, T)
         gather_by_expert(LAST)
         make_quads(A, "slot", 1, 0, C)
         quantise_x("slot", 1, 0, C)
-        make_quads(G, "token", LAST, 0, T // 2)
-        make_quads(A, "token", LAST, T // 2, EARLY)
+        make_quads(G, "token", LAST, 0, UNIT)
+        make_quads(A, "token", LAST, 2 * P, 3 * P)
+        make_quads(A, "token", LAST, 3 * P, 4 * P)
         for e in range(E):
             make_quads(A, "slot", LAST, C * e, C * (e + 1))
         make_quads(A, "token", LAST, EARLY, T)
@@ -370,7 +396,7 @@ def tile_moe_shr_mlp_relu_kernel(
         relu(V, "slot", 1)
         for block in (0, 1):
             turn("slot", block, block + 1, block)
-        quantise_h("slot", 0)
+        quantise(*last_calls[2])
         second_product("slot", 0, in_bank(1, [P, UNIT], "y")[:])
         relu(A, "slot", 2)
         relu(V, "slot", 3)
@@ -378,11 +404,11 @@ def tile_moe_shr_mlp_relu_kernel(
         put_back(V, 0, C)
         quantise_h("slot", 1)
         second_product("slot", 1, in_bank(3, [P, UNIT], "y")[:])
-        quantise_x("token", LAST, 0, EARLY)
-        quantise_x("token", LAST, EARLY, T)
+        quantise(*last_calls[0])
+        quantise(late_quads, late_codes, late_planes)
+        quantise(*last_calls[1])
         for block in range(EARLY // P):
             first_product("token", block, LAST)
-        quantise(late_quads, late_codes, late_planes)
         relu(A, "token", 0)
         relu(A, "token", 1)
         turn("token", 0, 2, 0)
@@ -398,10 +424,10 @@ def tile_moe_shr_mlp_relu_kernel(
         turn("token", 4, 5, 5)
         turn("token", 5, 6, 6)
         quantise_h("token", 2)
-        for unit, bank in enumerate((7, 5, 2)):
+        for unit, bank in enumerate((5, 6, 2)):
             second_product("token", unit, in_bank(bank, [P, UNIT], "y")[:])
         for unit in range(T // UNIT):
             columns = slice(UNIT * unit, UNIT * (unit + 1))
-            dst = h_quads["token", 2][:, columns] if unit < 2 else result[:, columns]
+            dst = result[:, columns]
             nc.vector.tensor_tensor(dst, y["token", unit], routed[:, columns], ADD)
             nc.sync.dma_start(out[:, columns], dst)

@@ -372,8 +372,8 @@ def tile_moe_shr_mlp_relu_kernel(
         make_quads(G, "slot", 1, C, S)
         make_late_quads(None)
         round_x(A, LAST, 1, 0, P)
-        round_x(A, LAST, 1, P, 352)
-        round_x(V, LAST, 1, 352, T)
+        round_x(A, LAST, 1, P, 544)
+        round_x(V, LAST, 1, 544, T)
         gather_by_expert(LAST)
         make_quads(A, "slot", 1, 0, C)
         quantise_x("slot", 1, 0, C)

@@ -14,8 +14,9 @@ SCALE_ROWS = 4
 SHARED = E
 UNIT = 2 * P
 EARLY = 2 * UNIT
+LATE_BLOCKS = range(EARLY // P, T // P)
 SCALAR_ROUNDS = (T // 3, T // 2)
-SCALAR_QUADS = 2 * P
+LAST_ROUNDS = T // 2
 
 FLOPS = 2 * (S + T) * (K * H + H * N)
 
@@ -34,7 +35,9 @@ ADD = mybir.AluOpType.add
 
 
 def sum_bank(kind, block):
-    return block if kind == "slot" else 4 + block if block < 4 else 1 + block
+    if kind == "slot":
+        return block
+    return 1 + block if block in LATE_BLOCKS else 4 + block
 
 
 def tile_moe_shr_mlp_relu_kernel(
@@ -63,63 +66,66 @@ def tile_moe_shr_mlp_relu_kernel(
         routed = sbuf(T, F32, "routed")
         result = sbuf(T, F32, "result")
 
-        both_pairs = sbuf(4 * T, U32, "both_pairs")
-        x_raw, x_pairs, slot_pairs, quads, codes, planes = {}, {}, {}, {}, {}, {}
-        for s in range(PASSES):
-            for u in range(2):
-                if s < LAST:
-                    x_raw[s, u] = sbuf(2 * T, F32, f"x_raw{s}{u}")
-            x_pairs[s] = both_pairs[:, 2 * T * s : 2 * T * (s + 1)] if s < LAST else sbuf(2 * T, U32, f"x_pairs{s}")
-            for kind in ("slot", "token"):
-                if (kind, s) in (("token", 0), ("slot", LAST)):
-                    quads[kind, s] = sbuf(2 * EARLY, U32, f"{kind}_quads{s}")
-                if (kind, s) not in (("slot", 1), ("token", LAST)):
-                    codes[kind, s] = sbuf(EARLY, U32, f"{kind}_codes{s}")
-        for s in range(LAST):
-            planes["token", s] = sbuf(EARLY, U8, f"token_plane{s}")
-        for s in range(PASSES):
-            if s < LAST:
-                slot_pairs[s] = sbuf(2 * S, U32, f"slot_pairs{s}")
-            planes["slot", s] = sbuf(S, U8, f"slot_plane{s}")
-        codes["slot", 1] = codes["token", 0]
-        first_quads = sbuf(2 * C + 2 * EARLY, U32, "first_quads")
-        quads["slot", 0] = first_quads[:, : 2 * S]
-        quads["token", 1] = first_quads[:, 2 * C :]
-        last_load = sbuf(2 * C - P + 2 * T, F32, "last_load")
-        x_raw[LAST, 1] = last_load[:, 2 * C - P :]
-        slot1_quads = [last_load[:, : 2 * C].bitcast(U32), sbuf(2 * C, U32, "slot_quads11")[:]]
-        fifth_load = sbuf(3 * UNIT + 2 * T, F32, "fifth_load")
-        x_raw[LAST, 0] = fifth_load[:, 3 * UNIT :]
-        late_quads = fifth_load[:, : 4 * UNIT].bitcast(U32)
-        last_pairs = sbuf(2 * UNIT + 2 * S, U32, "last_pairs")
-        slot_pairs[LAST] = last_pairs[:, 2 * UNIT :]
-        late_codes = sbuf(4 * P, U32, "late_codes")[:]
-        late_planes = sbuf(4 * P, U8, "late_planes")[:]
-        plane1 = [sbuf(C, U8, "slot_plane10")[:], late_planes[:, :C]]
-        last_plane = sbuf(S + P, U8, "last_plane")
-        planes["slot", LAST] = last_plane[:, :S]
-        joint_quads = sbuf(6 * P, U32, "joint_quads")
-        joint_codes = sbuf(3 * P, U32, "joint_codes")
-        joint_plane = sbuf(3 * P, U8, "joint_plane")
-        last_calls = [
-            (sbuf(2 * UNIT, U32, "token_quads2")[:], sbuf(UNIT, U32, "token_codes2")[:], planes["slot", 0][:, C:]),
-            (last_pairs[:, : 6 * P], sbuf(3 * P, U32, "token_codes3")[:], last_plane[:, C:]),
-            (joint_quads[:], joint_codes[:], joint_plane[:]),
-        ]
-        last_place = ((0, 0), (0, 1), (1, 0), (2, 2), (1, 1), (1, 2))
+        x_raw = {(s, u): sbuf(2 * T, F32, f"x_raw{s}{u}")[:] for s in range(LAST) for u in range(2)}
+        first_pairs = sbuf(LAST * 2 * T, U32, "first_pairs")
+        x_pairs = [first_pairs[:, 2 * T * s : 2 * T * (s + 1)] for s in range(LAST)] + [sbuf(2 * T, U32, "x_pairs")[:]]
+        slot_pairs = [sbuf(2 * S, U32, f"slot_pairs{s}")[:] for s in range(LAST)]
 
-        h_rows, h_quads, h_codes, h_planes = {}, {}, {}, {}
+        quads_01 = sbuf(2 * C + 2 * EARLY, U32, "quads_01")
+        late_01 = sbuf(3 * UNIT + 2 * T, U32, "late_01")
+        x_raw[LAST, 0] = late_01[:, 3 * UNIT :].bitcast(F32)
+        joint = sbuf(2 * C + 3 * P + 2 * T, U32, "joint")
+        expert0_1 = joint[:, 2 * C :]
+        x_raw[LAST, 1] = expert0_1[:, 3 * P :].bitcast(F32)
+        rest_2 = sbuf(EARLY + 2 * S, U32, "rest_2")
+        slot_pairs.append(rest_2[:, EARLY:])
+        slot_quads_2 = sbuf(2 * S, U32, "slot_quads_2")
+
+        token_codes_0 = sbuf(EARLY, U32, "token_codes_0")
+        slot_codes_0 = sbuf(S, U32, "slot_codes_0")
+        slot_plane_0 = sbuf(S, U8, "slot_plane_0")
+        late_plane = sbuf(2 * UNIT, U8, "late_plane")
+        slot_plane_2 = sbuf(S + P, U8, "slot_plane_2")
+
+        calls, place = {}, {}
+
+        def add_call(name, pieces, quads=None, codes=None, plane=None):
+            columns = P * len(pieces)
+            calls[name] = (
+                sbuf(2 * columns, U32, f"{name}_quads")[:] if quads is None else quads,
+                sbuf(columns, U32, f"{name}_codes")[:] if codes is None else codes,
+                sbuf(columns, U8, f"{name}_plane")[:] if plane is None else plane,
+            )
+            place.update({piece: (name, i) for i, piece in enumerate(pieces)})
+
+        def blocks(kind, s, numbers):
+            return [(kind, s, block) for block in numbers]
+
+        for e in range(E):
+            part, words = slice(C * e, C * (e + 1)), slice(2 * C * e, 2 * C * (e + 1))
+            own = (2 * e, 2 * e + 1)
+            first = (quads_01[:, words], slot_codes_0[:, part], slot_plane_0[:, part])
+            add_call(f"expert{e}_0", blocks("slot", 0, own), *first)
+            codes_2 = slot_codes_0[:, part] if e == 1 else None
+            add_call(f"expert{e}_2", blocks("slot", LAST, own), slot_quads_2[:, words], codes_2, slot_plane_2[:, part])
+        add_call("expert0_1", blocks("slot", 1, (0, 1)), quads=expert0_1[:, : 2 * C], codes=token_codes_0[:, :C])
+        add_call("expert1_1", blocks("slot", 1, (2, 3)), codes=slot_codes_0[:, :C], plane=late_plane[:, :C])
+        add_call("early_0", blocks("token", 0, range(EARLY // P)), codes=token_codes_0[:])
+        add_call("early_1", blocks("token", 1, range(EARLY // P)), quads=quads_01[:, 2 * C :])
+        late_pieces = blocks("token", 0, LATE_BLOCKS) + blocks("token", 1, LATE_BLOCKS)
+        add_call("late_01", late_pieces, quads=late_01[:, : 4 * UNIT], plane=late_plane[:])
+        add_call("unit0_2", blocks("token", LAST, (0, 1)), plane=slot_plane_0[:, C:])
+        rest_pieces = blocks("token", LAST, (2, *LATE_BLOCKS))
+        add_call("rest_2", rest_pieces, quads=rest_2[:, : 6 * P], plane=slot_plane_2[:, C:])
+        add_call("slot_h0", blocks("slot", "h", (0, 1)) + blocks("token", LAST, (3,)), quads=joint[:, : 6 * P])
+        add_call("slot_h1", blocks("slot", "h", (2, 3)))
+        for unit in range(T // UNIT):
+            add_call(f"token_h{unit}", blocks("token", "h", (2 * unit, 2 * unit + 1)))
+
+        h_rows = {}
         for kind, columns in (("slot", S), ("token", T)):
             for block in range(columns // P):
                 h_rows[kind, block] = sbuf(H, BF16, f"{kind}_h_rows{block}")
-            for unit in range(columns // UNIT):
-                h_quads[kind, unit] = sbuf(2 * UNIT, F32, f"{kind}_h_quads{unit}")
-                h_codes[kind, unit] = sbuf(UNIT, U32, f"{kind}_h_codes{unit}")
-                h_planes[kind, unit] = sbuf(UNIT, U8, f"{kind}_h_plane{unit}")
-
-        h_quads["slot", 0] = joint_quads[:, : 2 * UNIT].bitcast(F32)
-        h_codes["slot", 0] = joint_codes[:, :UNIT]
-        h_planes["slot", 0] = joint_plane[:, :UNIT]
         routed_y = [h_rows["slot", 3][:].bitcast(F32), h_rows["token", 1][:].bitcast(F32)]
 
         for tile in (w1_routed_planes, w1_shared_planes, w2_planes):
@@ -127,11 +133,11 @@ def tile_moe_shr_mlp_relu_kernel(
         nc.scalar.activation(routed[:], w1_routed_planes[:].bitcast(F32), RELU)
         make_identity(nc, ident[:])
 
-        def load_x(s, u, first, end):
+        def load_x(s, u):
             rows = xT[K_PASS * s : K_PASS * (s + 1), :].rearrange("(p d) t -> p d t", d=4)
             nc.sync.dma_start(
-                x_raw[s, u][:, : 2 * T].rearrange("p (d t) -> p d t", d=2)[:, :, first:end],
-                rows[:, 2 * u : 2 * u + 2, first:end],
+                x_raw[s, u].rearrange("p (d t) -> p d t", d=2),
+                rows[:, 2 * u : 2 * u + 2, :],
             )
 
         def load_planes(tile, scales, width):
@@ -147,15 +153,15 @@ def tile_moe_shr_mlp_relu_kernel(
                 words.bitcast(I32).rearrange("a p b -> p a b"),
             )
 
-        load_x(0, 0, 0, T)
+        load_x(0, 0)
         nc.sync.dma_start(offsets[:], offs)
-        load_x(0, 1, 0, T)
-        load_x(1, 0, 0, T)
-        load_x(1, 1, 0, T)
-        load_x(LAST, 0, 0, T)
+        load_x(0, 1)
+        load_x(1, 0)
+        load_x(1, 1)
+        load_x(LAST, 0)
         load_planes(w1_shared_planes, w1_scales[SHARED:], H)
         load_words(w1_shared[:, : LAST * 2 * H], w1_words[SHARED, :LAST])
-        load_x(LAST, 1, 0, T)
+        load_x(LAST, 1)
         load_planes(w1_routed_planes, w1_scales[:E], H)
         for s in range(PASSES):
             load_words(w1_routed[s][:], w1_words[:E, s])
@@ -174,7 +180,7 @@ def tile_moe_shr_mlp_relu_kernel(
             copy(
                 engine,
                 x_pairs[s][:, T * u + first : T * u + end].bitcast(BF16).rearrange("p (t d) -> p t d", d=2),
-                x_raw[s, u][:, : 2 * T].rearrange("p (d t) -> p t d", d=2)[:, first:end],
+                x_raw[s, u].rearrange("p (d t) -> p t d", d=2)[:, first:end],
             )
 
         def gather(s, u, first, end):
@@ -183,61 +189,31 @@ def tile_moe_shr_mlp_relu_kernel(
                 x_pairs[s][:, T * u : T * (u + 1)].indirect(offsets[:, first // 16 : end // 16]),
             )
 
-        def quads_of(kind, s, first, end):
-            if (kind, s) == ("slot", 1):
-                return slot1_quads[first // C]
-            if (kind, s) == ("token", LAST):
-                call, place = last_place[first // P]
-                return last_calls[call][0][:, 2 * P * place : 2 * P * place + 2 * (end - first)]
-            return quads[kind, s][:, 2 * first : 2 * end]
+        def operands(kind, s, block, count):
+            name, first = place[kind, s, block]
+            quads, codes, plane = calls[name]
+            columns = slice(P * first, P * (first + count))
+            return quads[:, 2 * columns.start : 2 * columns.stop], codes[:, columns], plane[:, columns]
 
-        def make_quads(engine, kind, s, first, end):
+        def make_quads(engine, kind, s, block, count):
             word = I32 if engine is nc.gpsimd else F32
             pairs = slot_pairs[s] if kind == "slot" else x_pairs[s]
             copy(
                 engine,
-                quads_of(kind, s, first, end).bitcast(word).rearrange("p (c u) -> p c u", u=2),
-                pairs[:].bitcast(word).rearrange("p (u c) -> p c u", u=2)[:, first:end],
+                operands(kind, s, block, count)[0].bitcast(word).rearrange("p (c u) -> p c u", u=2),
+                pairs.bitcast(word).rearrange("p (u c) -> p c u", u=2)[:, P * block : P * (block + count)],
             )
 
-        def make_late_quads(s):
-            nc.scalar.copy(
-                late_quads.bitcast(F32).rearrange("p (a c u) -> p a c u", c=UNIT, u=2),
-                both_pairs[:].bitcast(F32).rearrange("p (a u c) -> p a c u", a=2, u=2)[:, :, EARLY:],
-            )
-
-        def quantise(words, code, plane):
-            nc.vector.quantize_mx(out=code.bitcast(FP8X4), scales=plane, in_=words.bitcast(BF16))
-
-        def codes_of(kind, s, first, end):
-            if kind == "slot" and s > 0 and first >= C:
-                return codes[kind, 0][:, (s - 2) * C + first : (s - 2) * C + end]
-            if (kind, s) == ("token", LAST):
-                call, place = last_place[first // P]
-                return last_calls[call][1][:, P * place : P * (place + 1)]
-            return codes[kind, s][:, first:end]
-
-        def plane_of(kind, s, first, end):
-            if (kind, s) == ("slot", 1):
-                return plane1[first // C][:, first % C : first % C + end - first]
-            if (kind, s) == ("token", LAST):
-                call, place = last_place[first // P]
-                return last_calls[call][2][:, P * place : P * (place + 1)]
-            return planes[kind, s][:, first:end]
-
-        def quantise_x(kind, s, first, end):
-            quantise(quads_of(kind, s, first, end), codes_of(kind, s, first, end), plane_of(kind, s, first, end))
+        def quantise(name):
+            quads, codes, plane = calls[name]
+            nc.vector.quantize_mx(out=codes.bitcast(FP8X4), scales=plane, in_=quads.bitcast(BF16))
 
         sums, y = {}, {}
 
         def first_product(kind, block, s):
             if s == 0:
                 sums[kind, block] = in_bank(sum_bank(kind, block), [P, H], "sums")
-            if block * P < EARLY or s == LAST:
-                code, plane, place = codes_of(kind, s, P * block, P * (block + 1)), plane_of(kind, s, P * block, P * (block + 1)), 0
-            else:
-                code, plane, place = None, late_planes, block - EARLY // P + 2 * s
-                code = late_codes[:, P * place : P * (place + 1)]
+            _, codes, plane = operands(kind, s, block, 1)
             if kind == "token":
                 w1, w1_plane = w1_shared[:, 2 * H * s : 2 * H * (s + 1)], w1_shared_planes[:, H * s : H * (s + 1)]
             else:
@@ -246,8 +222,8 @@ def tile_moe_shr_mlp_relu_kernel(
                 w1, w1_plane = w1_routed[s][:, 2 * H * e : 2 * H * (e + 1)], w1_routed_planes[:, H * a : H * (a + 1)]
             nc.tensor.matmul_mx(
                 out=sums[kind, block][:],
-                lhsT=code.bitcast(FP8X4),
-                lhsT_scale=plane[:, P * place : P * (place + 1)],
+                lhsT=codes.bitcast(FP8X4),
+                lhsT_scale=plane,
                 rhs=w1.bitcast(FP4X4),
                 rhs_scale=w1_plane,
                 start=(s == 0),
@@ -262,75 +238,40 @@ def tile_moe_shr_mlp_relu_kernel(
             else:
                 nc.vector.tensor_scalar_max(dst, src, 0.0)
 
-        def turn(kind, first, end, bank, engine=nc.scalar):
-            turned = in_bank(bank, [P, end - first, 2, P], "turned")
-            for b in reversed(range(end - first)):
-                words = h_rows[kind, first + b][:].bitcast(F32)
+        def turn(engine, kind, block, count, bank):
+            turned = in_bank(bank, [P, count, 2, P], "turned")
+            for b in reversed(range(count)):
+                words = h_rows[kind, block + b][:].bitcast(F32)
                 for u in range(2):
                     nc.tensor.transpose(turned[:, b, u, :], words[:, P * u : P * (u + 1)], ident[:])
-            unit_quads = h_quads[kind, first // 2][:].rearrange("p (b c u) -> p b c u", c=P, u=2)
             copy(
                 engine,
-                unit_quads[:, first % 2 : first % 2 + end - first],
+                operands(kind, "h", block, count)[0].bitcast(F32).rearrange("p (b c u) -> p b c u", c=P, u=2),
                 turned[:].rearrange("p b u c -> p b c u"),
             )
 
-        def quantise_h(kind, unit):
-            quantise(h_quads[kind, unit][:], h_codes[kind, unit][:], h_planes[kind, unit][:])
-
-        def second_product(kind, unit, dst):
+        def second_product(kind, unit, bank):
             e = unit if kind == "slot" else SHARED
-            y[kind, unit] = dst
+            _, codes, plane = operands(kind, "h", 2 * unit, 2)
+            y[kind, unit] = in_bank(bank, [P, UNIT], "y")
             nc.tensor.matmul_mx(
-                out=dst,
+                out=y[kind, unit][:],
                 lhsT=w2_codes[:, 2 * N * e : 2 * N * (e + 1)].bitcast(FP4X4),
                 lhsT_scale=w2_planes[:, N * e : N * (e + 1)],
-                rhs=h_codes[kind, unit][:].bitcast(FP8X4),
-                rhs_scale=h_planes[kind, unit][:],
+                rhs=codes.bitcast(FP8X4),
+                rhs_scale=plane,
                 start=True,
                 stop=True,
             )
 
-        def block_chain(block, bank):
-            cols = slice(P * (block % 2), P * (block % 2 + 1))
-            unit = block // 2
-            quantise(h_quads["slot", unit][:, 2 * cols.start : 2 * cols.stop], h_codes["slot", unit][:, cols], h_planes["slot", unit][:, cols])
-            dst = in_bank(bank, [P, P], "y")[:]
-            nc.tensor.matmul_mx(
-                out=dst,
-                lhsT=w2_codes[:, 2 * N * unit : 2 * N * (unit + 1)].bitcast(FP4X4),
-                lhsT_scale=w2_planes[:, N * unit : N * (unit + 1)],
-                rhs=h_codes["slot", unit][:, cols].bitcast(FP8X4),
-                rhs_scale=h_planes["slot", unit][:, cols],
-                start=True,
-                stop=True,
-            )
-            return dst
-
-        def leave(engine, src, first, end):
-            copy(engine, routed_y[:, first:end], src)
-
-        def scatter(first, end):
+        def put_back(engine, e):
+            copy(engine, routed_y[e], y["slot", e][:])
             nc.vector.tensor_tensor(
-                routed[:].indirect(offsets[:, first // 16 : end // 16]),
-                routed_y[:, first:end],
-                gate_sb[:, first:end],
+                routed[:].indirect(offsets[:, C * e // 16 : C * (e + 1) // 16]),
+                routed_y[e],
+                gate_sb[:, C * e : C * (e + 1)],
                 MULT,
             )
-
-        def put_back(engine, first, end):
-            values = routed_y[first // C][:, first % C : first % C + end - first]
-            copy(engine, values, y["slot", first // C][:, first % C : first % C + end - first])
-            nc.vector.tensor_tensor(
-                routed[:].indirect(offsets[:, first // 16 : end // 16]),
-                values,
-                gate_sb[:, first:end],
-                MULT,
-            )
-
-        def round_in_two(s, u):
-            round_x(nc.scalar, s, u, 0, EARLY)
-            round_x(nc.scalar, s, u, EARLY, T)
 
         def gather_by_expert(s):
             for e in range(E):
@@ -346,13 +287,13 @@ def tile_moe_shr_mlp_relu_kernel(
             if u == 0:
                 gather(0, 0, 0, S)
         gather_by_expert(0)
-        make_quads(nc.vector, "slot", 0, 0, C)
-        make_quads(nc.vector, "slot", 0, C, S)
-        quantise_x("slot", 0, 0, C)
-        make_quads(nc.scalar, "token", 0, 0, SCALAR_QUADS)
-        make_quads(nc.gpsimd, "token", 0, SCALAR_QUADS, EARLY)
-        quantise_x("token", 0, 0, EARLY)
-        quantise_x("slot", 0, C, S)
+        make_quads(nc.vector, "slot", 0, 0, 2)
+        make_quads(nc.vector, "slot", 0, 2, 2)
+        quantise("expert0_0")
+        make_quads(nc.scalar, "token", 0, 0, 2)
+        make_quads(nc.gpsimd, "token", 0, 2, 2)
+        quantise("early_0")
+        quantise("expert1_0")
         early_products(0)
 
         round_x(nc.scalar, 1, 0, 0, T)
@@ -361,73 +302,75 @@ def tile_moe_shr_mlp_relu_kernel(
             round_x(nc.scalar, 1, 1, UNIT * unit, UNIT * (unit + 1))
         gather(1, 1, 0, S)
         for unit in range(EARLY // UNIT):
-            make_quads(nc.gpsimd, "token", 1, UNIT * unit, UNIT * (unit + 1))
-        quantise_x("token", 1, 0, EARLY)
+            make_quads(nc.gpsimd, "token", 1, 2 * unit, 2)
+        quantise("early_1")
         early_products(1)
 
-        V, A, G = nc.vector, nc.scalar, nc.gpsimd
-        round_x(A, LAST, 0, 0, UNIT)
-        round_x(A, LAST, 0, UNIT, T)
+        round_x(nc.scalar, LAST, 0, 0, UNIT)
+        round_x(nc.scalar, LAST, 0, UNIT, T)
         gather(LAST, 0, 0, S)
-        make_quads(G, "slot", 1, C, S)
-        make_late_quads(None)
-        round_x(A, LAST, 1, 0, P)
-        round_x(A, LAST, 1, P, 544)
-        round_x(V, LAST, 1, 544, T)
+        make_quads(nc.gpsimd, "slot", 1, 2, 2)
+        nc.scalar.copy(
+            calls["late_01"][0].bitcast(F32).rearrange("p (s c u) -> p s c u", s=LAST, u=2),
+            first_pairs[:].bitcast(F32).rearrange("p (s u c) -> p s c u", s=LAST, u=2)[:, :, EARLY:],
+        )
+        round_x(nc.scalar, LAST, 1, 0, P)
+        round_x(nc.scalar, LAST, 1, P, LAST_ROUNDS)
+        round_x(nc.vector, LAST, 1, LAST_ROUNDS, T)
         gather_by_expert(LAST)
-        make_quads(A, "slot", 1, 0, C)
-        quantise_x("slot", 1, 0, C)
-        make_quads(G, "token", LAST, 0, UNIT)
-        make_quads(A, "token", LAST, 2 * P, 3 * P)
-        make_quads(A, "token", LAST, 3 * P, 4 * P)
+        make_quads(nc.scalar, "slot", 1, 0, 2)
+        quantise("expert0_1")
+        make_quads(nc.gpsimd, "token", LAST, 0, 2)
+        make_quads(nc.scalar, "token", LAST, 2, 1)
         for e in range(E):
-            make_quads(A, "slot", LAST, C * e, C * (e + 1))
-        make_quads(A, "token", LAST, EARLY, T)
-        quantise_x("slot", LAST, 0, C)
+            make_quads(nc.scalar, "slot", LAST, 2 * e, 2)
+        make_quads(nc.scalar, "token", LAST, 3, 1)
+        make_quads(nc.scalar, "token", LAST, LATE_BLOCKS[0], 2)
+        quantise("expert0_2")
+
         for block in range(S // P):
             first_product("slot", block, 0)
-        quantise_x("slot", 1, C, S)
-        quantise_x("slot", LAST, C, S)
+        quantise("expert1_1")
+        quantise("expert1_2")
         for e in range(E):
             for s in range(1, PASSES):
                 for block in (2 * e, 2 * e + 1):
                     first_product("slot", block, s)
-        relu(A, "slot", 0)
-        relu(V, "slot", 1)
+        relu(nc.scalar, "slot", 0)
+        relu(nc.vector, "slot", 1)
         for block in (0, 1):
-            turn("slot", block, block + 1, block)
-        quantise(*last_calls[2])
-        second_product("slot", 0, in_bank(1, [P, UNIT], "y")[:])
-        relu(A, "slot", 2)
-        relu(V, "slot", 3)
-        turn("slot", 2, 4, 3, V)
-        put_back(V, 0, C)
-        quantise_h("slot", 1)
-        second_product("slot", 1, in_bank(3, [P, UNIT], "y")[:])
-        quantise(*last_calls[0])
-        quantise(late_quads, late_codes, late_planes)
-        quantise(*last_calls[1])
-        for block in range(EARLY // P):
-            first_product("token", block, LAST)
-        relu(A, "token", 0)
-        relu(A, "token", 1)
-        turn("token", 0, 2, 0)
-        quantise_h("token", 0)
-        put_back(A, C, S)
-        for block in range(EARLY // P, T // P):
+            turn(nc.scalar, "slot", block, 1, bank=block)
+        quantise("slot_h0")
+        second_product("slot", 0, bank=1)
+        relu(nc.scalar, "slot", 2)
+        relu(nc.vector, "slot", 3)
+        turn(nc.vector, "slot", 2, 2, bank=3)
+        put_back(nc.vector, 0)
+        quantise("slot_h1")
+        second_product("slot", 1, bank=3)
+
+        quantise("unit0_2")
+        quantise("late_01")
+        quantise("rest_2")
+        early_products(LAST)
+        relu(nc.scalar, "token", 0)
+        relu(nc.scalar, "token", 1)
+        turn(nc.scalar, "token", 0, 2, bank=0)
+        quantise("token_h0")
+        put_back(nc.scalar, 1)
+        for block in LATE_BLOCKS:
             for s in range(PASSES):
                 first_product("token", block, s)
         for block in range(2, T // P):
-            relu(A, "token", block)
-        turn("token", 2, 4, 7)
-        quantise_h("token", 1)
-        turn("token", 4, 5, 5)
-        turn("token", 5, 6, 6)
-        quantise_h("token", 2)
-        for unit, bank in enumerate((5, 6, 2)):
-            second_product("token", unit, in_bank(bank, [P, UNIT], "y")[:])
+            relu(nc.scalar, "token", block)
+        turn(nc.scalar, "token", 2, 2, bank=sum_bank("token", 3))
+        quantise("token_h1")
+        for block in LATE_BLOCKS:
+            turn(nc.scalar, "token", block, 1, bank=sum_bank("token", block))
+        quantise("token_h2")
+        for unit, bank in enumerate((*(sum_bank("token", block) for block in LATE_BLOCKS), 2)):
+            second_product("token", unit, bank)
         for unit in range(T // UNIT):
             columns = slice(UNIT * unit, UNIT * (unit + 1))
-            dst = result[:, columns]
-            nc.vector.tensor_tensor(dst, y["token", unit], routed[:, columns], ADD)
-            nc.sync.dma_start(out[:, columns], dst)
+            nc.vector.tensor_tensor(result[:, columns], y["token", unit][:], routed[:, columns], ADD)
+            nc.sync.dma_start(out[:, columns], result[:, columns])

@@ -49,7 +49,7 @@ def tile_moe_shr_mlp_relu_kernel(
         psum = ctx.enter_context(tc.psum_pool(name="psum", bufs=1))
 
         def sbuf(columns, dtype, name):
-            return keep.tile([P, columns], dtype, align_bytes=64, name=name)
+            return keep.tile([P, columns], dtype, align_bytes=256, name=name)
 
         def in_bank(bank, shape, name):
             return psum.tile(shape, F32, tag=f"bank{bank}", bufs=1, name=name)

@@ -57,8 +57,13 @@ def tile_moe_shr_mlp_relu_kernel(
         offsets = sbuf(S // 16, U16, "offsets")
         gate_sb = sbuf(S, F32, "gate_sb")
         ident = sbuf(P, F32, "ident")
-        w1_shared = sbuf(PASSES * 2 * H, U8, "w1_shared")
-        w1_routed = [sbuf(E * 2 * H, U8, f"w1_routed{s}") for s in range(PASSES)]
+        word_loads = [[(SHARED, 0)], [(SHARED, 1)], [(0, 0)], [(0, 1), (1, 0)], [(0, 2), (1, 1)], [(1, 2), (SHARED, 2)]]
+        word_tiles = [sbuf(len(load) * 2 * H, U8, f"w1_words{i}") for i, load in enumerate(word_loads)]
+        w1_words_sb = {
+            matrix: tile[:, 2 * H * j : 2 * H * (j + 1)]
+            for load, tile in zip(word_loads, word_tiles)
+            for j, matrix in enumerate(load)
+        }
         w1_shared_planes = sbuf(PASSES * H, U8, "w1_shared_planes")
         w1_routed_planes = sbuf(E * PASSES * H, U8, "w1_routed_planes")
         w2_codes = sbuf((E + 1) * 2 * N, U8, "w2_codes")
@@ -153,6 +158,11 @@ def tile_moe_shr_mlp_relu_kernel(
                 words.bitcast(I32).rearrange("a p b -> p a b"),
             )
 
+        def load_w1(i):
+            first, last = (PASSES * e + s for e, s in (word_loads[i][0], word_loads[i][-1]))
+            matrices = w1_words.rearrange("e s p b -> (e s) p b")
+            load_words(word_tiles[i][:], matrices[first : last + 1 : max(last - first, 1)])
+
         load_x(0, 0)
         nc.sync.dma_start(offsets[:], offs)
         load_x(0, 1)
@@ -160,12 +170,12 @@ def tile_moe_shr_mlp_relu_kernel(
         load_x(1, 1)
         load_x(LAST, 0)
         load_planes(w1_shared_planes, w1_scales[SHARED:], H)
-        load_words(w1_shared[:, : LAST * 2 * H], w1_words[SHARED, :LAST])
+        load_w1(0)
         load_x(LAST, 1)
+        load_w1(1)
         load_planes(w1_routed_planes, w1_scales[:E], H)
-        for s in range(PASSES):
-            load_words(w1_routed[s][:], w1_words[:E, s])
-        load_words(w1_shared[:, LAST * 2 * H :], w1_words[SHARED, LAST:])
+        for i in range(2, len(word_loads)):
+            load_w1(i)
         load_words(w2_codes[:], w2_words[:, 0])
         load_planes(w2_planes, w2_scales, N)
         nc.sync.dma_start(gate_sb[:], gate)
@@ -215,11 +225,11 @@ def tile_moe_shr_mlp_relu_kernel(
                 sums[kind, block] = in_bank(sum_bank(kind, block), [P, H], "sums")
             _, codes, plane = operands(kind, s, block, 1)
             if kind == "token":
-                w1, w1_plane = w1_shared[:, 2 * H * s : 2 * H * (s + 1)], w1_shared_planes[:, H * s : H * (s + 1)]
+                w1, w1_plane = w1_words_sb[SHARED, s], w1_shared_planes[:, H * s : H * (s + 1)]
             else:
                 e = block * P // C
                 a = PASSES * e + s
-                w1, w1_plane = w1_routed[s][:, 2 * H * e : 2 * H * (e + 1)], w1_routed_planes[:, H * a : H * (a + 1)]
+                w1, w1_plane = w1_words_sb[e, s], w1_routed_planes[:, H * a : H * (a + 1)]
             nc.tensor.matmul_mx(
                 out=sums[kind, block][:],
                 lhsT=codes.bitcast(FP8X4),

@@ -16,7 +16,7 @@ UNIT = 2 * P
 EARLY = 2 * UNIT
 LATE_BLOCKS = range(EARLY // P, T // P)
 SCALAR_ROUNDS = (T // 3, T // 2)
-LAST_ROUNDS = T // 2
+LAST_ROUNDS = T // 4
 
 FLOPS = 2 * (S + T) * (K * H + H * N)
 
@@ -64,8 +64,8 @@ def tile_moe_shr_mlp_relu_kernel(
             for load, tile in zip(word_loads, word_tiles)
             for j, matrix in enumerate(load)
         }
-        w1_shared_planes = sbuf(PASSES * H, U8, "w1_shared_planes")
-        w1_routed_planes = sbuf(E * PASSES * H, U8, "w1_routed_planes")
+        w1_shared_planes = sbuf(P + PASSES * H, U8, "w1_shared_planes")[:, P:]
+        w1_routed_planes = sbuf(P + E * PASSES * H, U8, "w1_routed_planes")[:, P:]
         w2_codes = sbuf((E + 1) * 2 * N, U8, "w2_codes")
         w2_planes = sbuf((E + 1) * N, U8, "w2_planes")
         routed = sbuf(T, F32, "routed")
@@ -291,11 +291,13 @@ def tile_moe_shr_mlp_relu_kernel(
             for block in range(EARLY // P):
                 first_product("token", block, s)
 
-        for u in range(2):
-            round_x(nc.scalar, 0, u, 0, SCALAR_ROUNDS[u])
-            round_x(nc.vector, 0, u, SCALAR_ROUNDS[u], T)
-            if u == 0:
-                gather(0, 0, 0, S)
+        round_x(nc.scalar, 0, 0, 0, SCALAR_ROUNDS[0])
+        round_x(nc.vector, 0, 0, SCALAR_ROUNDS[0], T)
+        gather(0, 0, 0, S)
+        round_x(nc.scalar, 0, 1, 0, SCALAR_ROUNDS[1])
+        round_x(nc.vector, 0, 1, EARLY, T)
+        round_x(nc.vector, 0, 1, SCALAR_ROUNDS[1], EARLY)
+        make_quads(nc.vector, "token", 0, LATE_BLOCKS[0], 2)
         gather_by_expert(0)
         make_quads(nc.vector, "slot", 0, 0, 2)
         make_quads(nc.vector, "slot", 0, 2, 2)
@@ -320,13 +322,10 @@ def tile_moe_shr_mlp_relu_kernel(
         round_x(nc.scalar, LAST, 0, UNIT, T)
         gather(LAST, 0, 0, S)
         make_quads(nc.gpsimd, "slot", 1, 2, 2)
-        nc.scalar.copy(
-            calls["late_01"][0].bitcast(F32).rearrange("p (s c u) -> p s c u", s=LAST, u=2),
-            first_pairs[:].bitcast(F32).rearrange("p (s u c) -> p s c u", s=LAST, u=2)[:, :, EARLY:],
-        )
+        make_quads(nc.scalar, "token", 1, LATE_BLOCKS[0], 2)
         round_x(nc.scalar, LAST, 1, 0, P)
-        round_x(nc.scalar, LAST, 1, P, LAST_ROUNDS)
-        round_x(nc.vector, LAST, 1, LAST_ROUNDS, T)
+        round_x(nc.scalar, LAST, 1, P + LAST_ROUNDS, T)
+        round_x(nc.vector, LAST, 1, P, P + LAST_ROUNDS)
         gather_by_expert(LAST)
         make_quads(nc.scalar, "slot", 1, 0, 2)
         quantise("expert0_1")

from contextlib import ExitStack

import concourse.mybir as mybir
from concourse.masks import make_identity

K, T, E, C, H, N = 1536, 768, 2, 256, 512, 128

P = 128
S = E * C
K_PASS = 512
PASSES = K // K_PASS
LAST = PASSES - 1
SCALE_ROWS = 4
SHARED = E
UNIT = 2 * P
EARLY = 2 * UNIT
LATE_BLOCKS = range(EARLY // P, T // P)
SCALAR_ROUNDS = (T // 3, T // 2)
LAST_ROUNDS = T // 4

FLOPS = 2 * (S + T) * (K * H + H * N)

F32 = mybir.dt.float32
BF16 = mybir.dt.bfloat16
I32 = mybir.dt.int32
U32 = mybir.dt.uint32
U16 = mybir.dt.uint16
U8 = mybir.dt.uint8
FP8X4 = mybir.dt.float8_e4m3fn_x4
FP4X4 = mybir.dt.float4_e2m1fn_x4

RELU = mybir.ActivationFunctionType.Relu
MULT = mybir.AluOpType.mult
ADD = mybir.AluOpType.add


def sum_bank(kind, block):
    if kind == "slot":
        return block
    return 1 + block if block in LATE_BLOCKS else 4 + block


def tile_moe_shr_mlp_relu_kernel(
    tc, xT, w1_words, w1_scales, w2_words, w2_scales, gate, offs, out
):
    nc = tc.nc
    with ExitStack() as ctx:
        keep = ctx.enter_context(tc.tile_pool(name="keep", bufs=1))
        psum = ctx.enter_context(tc.psum_pool(name="psum", bufs=1))

        def sbuf(columns, dtype, name):
            return keep.tile([P, columns], dtype, align_bytes=256, name=name)

        def in_bank(bank, shape, name):
            return psum.tile(shape, F32, tag=f"bank{bank}", bufs=1, name=name)

        offsets = sbuf(S // 16, U16, "offsets")
        gate_sb = sbuf(S, F32, "gate_sb")
        ident = sbuf(P, F32, "ident")
        word_loads = [[(SHARED, 0)], [(SHARED, 1)], [(0, 0)], [(0, 1), (1, 0)], [(0, 2), (1, 1)], [(1, 2), (SHARED, 2)]]
        word_tiles = [sbuf(len(load) * 2 * H, U8, f"w1_words{i}") for i, load in enumerate(word_loads)]
        w1_words_sb = {
            matrix: tile[:, 2 * H * j : 2 * H * (j + 1)]
            for load, tile in zip(word_loads, word_tiles)
            for j, matrix in enumerate(load)
        }
        w1_shared_planes = sbuf(P + PASSES * H, U8, "w1_shared_planes")[:, P:]
        w1_routed_planes = sbuf(P + E * PASSES * H, U8, "w1_routed_planes")[:, P:]
        w2_codes = sbuf((E + 1) * 2 * N, U8, "w2_codes")
        w2_planes = sbuf((E + 1) * N, U8, "w2_planes")
        routed = sbuf(T, F32, "routed")
        result = sbuf(T, F32, "result")

        x_raw = {(s, u): sbuf(2 * T, F32, f"x_raw{s}{u}")[:] for s in range(LAST) for u in range(2)}
        first_pairs = sbuf(LAST * 2 * T, U32, "first_pairs")
        x_pairs = [first_pairs[:, 2 * T * s : 2 * T * (s + 1)] for s in range(LAST)] + [sbuf(2 * T, U32, "x_pairs")[:]]
        slot_pairs = [sbuf(2 * S, U32, f"slot_pairs{s}")[:] for s in range(LAST)]

        quads_01 = sbuf(2 * C + 2 * EARLY, U32, "quads_01")
        late_01 = sbuf(3 * UNIT + 2 * T, U32, "late_01")
        x_raw[LAST, 0] = late_01[:, 3 * UNIT :].bitcast(F32)
        joint = sbuf(2 * C + 3 * P + 2 * T, U32, "joint")
        expert0_1 = joint[:, 2 * C :]
        x_raw[LAST, 1] = expert0_1[:, 3 * P :].bitcast(F32)
        rest_2 = sbuf(EARLY + 2 * S, U32, "rest_2")
        slot_pairs.append(rest_2[:, EARLY:])
        slot_quads_2 = sbuf(2 * S, U32, "slot_quads_2")

        token_codes_0 = sbuf(EARLY, U32, "token_codes_0")
        slot_codes_0 = sbuf(S, U32, "slot_codes_0")
        slot_plane_0 = sbuf(S, U8, "slot_plane_0")
        late_plane = sbuf(2 * UNIT, U8, "late_plane")
        slot_plane_2 = sbuf(S + P, U8, "slot_plane_2")

        calls, place = {}, {}

        def add_call(name, pieces, quads=None, codes=None, plane=None):
            columns = P * len(pieces)
            calls[name] = (
                sbuf(2 * columns, U32, f"{name}_quads")[:] if quads is None else quads,
                sbuf(columns, U32, f"{name}_codes")[:] if codes is None else codes,
                sbuf(columns, U8, f"{name}_plane")[:] if plane is None else plane,
            )
            place.update({piece: (name, i) for i, piece in enumerate(pieces)})

        def blocks(kind, s, numbers):
            return [(kind, s, block) for block in numbers]

        for e in range(E):
            part, words = slice(C * e, C * (e + 1)), slice(2 * C * e, 2 * C * (e + 1))
            own = (2 * e, 2 * e + 1)
            first = (quads_01[:, words], slot_codes_0[:, part], slot_plane_0[:, part])
            add_call(f"expert{e}_0", blocks("slot", 0, own), *first)
            codes_2 = slot_codes_0[:, part] if e == 1 else None
            add_call(f"expert{e}_2", blocks("slot", LAST, own), slot_quads_2[:, words], codes_2, slot_plane_2[:, part])
        add_call("expert0_1", blocks("slot", 1, (0, 1)), quads=expert0_1[:, : 2 * C], codes=token_codes_0[:, :C])
        add_call("expert1_1", blocks("slot", 1, (2, 3)), codes=slot_codes_0[:, :C], plane=late_plane[:, :C])
        add_call("early_0", blocks("token", 0, range(EARLY // P)), codes=token_codes_0[:])
        add_call("early_1", blocks("token", 1, range(EARLY // P)), quads=quads_01[:, 2 * C :])
        late_pieces = blocks("token", 0, LATE_BLOCKS) + blocks("token", 1, LATE_BLOCKS)
        add_call("late_01", late_pieces, quads=late_01[:, : 4 * UNIT], plane=late_plane[:])
        add_call("unit0_2", blocks("token", LAST, (0, 1)), plane=slot_plane_0[:, C:])
        rest_pieces = blocks("token", LAST, (2, *LATE_BLOCKS))
        add_call("rest_2", rest_pieces, quads=rest_2[:, : 6 * P], plane=slot_plane_2[:, C:])
        add_call("slot_h0", blocks("slot", "h", (0, 1)) + blocks("token", LAST, (3,)), quads=joint[:, : 6 * P])
        add_call("slot_h1", blocks("slot", "h", (2, 3)))
        for unit in range(T // UNIT):
            add_call(f"token_h{unit}", blocks("token", "h", (2 * unit, 2 * unit + 1)))

        h_rows = {}
        for kind, columns in (("slot", S), ("token", T)):
            for block in range(columns // P):
                h_rows[kind, block] = sbuf(H, BF16, f"{kind}_h_rows{block}")
        routed_y = [h_rows["slot", 3][:].bitcast(F32), h_rows["token", 1][:].bitcast(F32)]

        for tile in (w1_routed_planes, w1_shared_planes, w2_planes):
            nc.vector.memset(tile[:].bitcast(I32), 0)
        nc.scalar.activation(routed[:], w1_routed_planes[:].bitcast(F32), RELU)
        make_identity(nc, ident[:])

        def load_x(s, u):
            rows = xT[K_PASS * s : K_PASS * (s + 1), :].rearrange("(p d) t -> p d t", d=4)
            nc.sync.dma_start(
                x_raw[s, u].rearrange("p (d t) -> p d t", d=2),
                rows[:, 2 * u : 2 * u + 2, :],
            )

        def load_planes(tile, scales, width):
            for r in range(SCALE_ROWS):
                nc.sync.dma_start(
                    tile[:].bitcast(I32).rearrange("p (a i) -> p a i", i=width // 4)[r:P:32],
                    scales.bitcast(I32)[:, :, r:16:SCALE_ROWS, :].rearrange("e s q i -> q (e s) i"),
                )

        def load_words(dst, words):
            nc.sync.dma_start(
                dst.bitcast(I32).rearrange("p (a b) -> p a b", a=words.shape[0]),
                words.bitcast(I32).rearrange("a p b -> p a b"),
            )

        def load_w1(i):
            first, last = (PASSES * e + s for e, s in (word_loads[i][0], word_loads[i][-1]))
            matrices = w1_words.rearrange("e s p b -> (e s) p b")
            load_words(word_tiles[i][:], matrices[first : last + 1 : max(last - first, 1)])

        load_x(0, 0)
        nc.sync.dma_start(offsets[:], offs)
        load_x(0, 1)
        load_x(1, 0)
        load_x(1, 1)
        load_x(LAST, 0)
        load_planes(w1_shared_planes, w1_scales[SHARED:], H)
        load_w1(0)
        load_x(LAST, 1)
        load_w1(1)
        load_planes(w1_routed_planes, w1_scales[:E], H)
        for i in range(2, len(word_loads)):
            load_w1(i)
        load_words(w2_codes[:], w2_words[:, 0])
        load_planes(w2_planes, w2_scales, N)
        nc.sync.dma_start(gate_sb[:], gate)

        def copy(engine, dst, src):
            if engine is nc.scalar:
                nc.scalar.copy(dst, src)
            else:
                engine.tensor_copy(dst, src)

        def round_x(engine, s, u, first, end):
            copy(
                engine,
                x_pairs[s][:, T * u + first : T * u + end].bitcast(BF16).rearrange("p (t d) -> p t d", d=2),
                x_raw[s, u].rearrange("p (d t) -> p t d", d=2)[:, first:end],
            )

        def gather(s, u, first, end):
            nc.vector.tensor_copy(
                slot_pairs[s][:, S * u + first : S * u + end],
                x_pairs[s][:, T * u : T * (u + 1)].indirect(offsets[:, first // 16 : end // 16]),
            )

        def operands(kind, s, block, count):
            name, first = place[kind, s, block]
            quads, codes, plane = calls[name]
            columns = slice(P * first, P * (first + count))
            return quads[:, 2 * columns.start : 2 * columns.stop], codes[:, columns], plane[:, columns]

        def make_quads(engine, kind, s, block, count):
            word = I32 if engine is nc.gpsimd else F32
            pairs = slot_pairs[s] if kind == "slot" else x_pairs[s]
            copy(
                engine,
                operands(kind, s, block, count)[0].bitcast(word).rearrange("p (c u) -> p c u", u=2),
                pairs.bitcast(word).rearrange("p (u c) -> p c u", u=2)[:, P * block : P * (block + count)],
            )

        def quantise(name):
            quads, codes, plane = calls[name]
            nc.vector.quantize_mx(out=codes.bitcast(FP8X4), scales=plane, in_=quads.bitcast(BF16))

        sums, y = {}, {}

        def first_product(kind, block, s):
            if s == 0:
                sums[kind, block] = in_bank(sum_bank(kind, block), [P, H], "sums")
            _, codes, plane = operands(kind, s, block, 1)
            if kind == "token":
                w1, w1_plane = w1_words_sb[SHARED, s], w1_shared_planes[:, H * s : H * (s + 1)]
            else:
                e = block * P // C
                a = PASSES * e + s
                w1, w1_plane = w1_words_sb[e, s], w1_routed_planes[:, H * a : H * (a + 1)]
            nc.tensor.matmul_mx(
                out=sums[kind, block][:],
                lhsT=codes.bitcast(FP8X4),
                lhsT_scale=plane,
                rhs=w1.bitcast(FP4X4),
                rhs_scale=w1_plane,
                start=(s == 0),
                stop=(s == LAST),
            )

        def relu(engine, kind, block):
            dst = h_rows[kind, block][:].rearrange("c (u p d) -> c u p d", u=2, d=2)
            src = sums[kind, block][:].rearrange("c (p u d) -> c u p d", u=2, d=2)
            if engine is nc.scalar:
                nc.scalar.activation(dst, src, RELU)
            else:
                nc.vector.tensor_scalar_max(dst, src, 0.0)

        def turn(engine, kind, block, count, bank):
            turned = in_bank(bank, [P, count, 2, P], "turned")
            for b in reversed(range(count)):
                words = h_rows[kind, block + b][:].bitcast(F32)
                for u in range(2):
                    nc.tensor.transpose(turned[:, b, u, :], words[:, P * u : P * (u + 1)], ident[:])
            copy(
                engine,
                operands(kind, "h", block, count)[0].bitcast(F32).rearrange("p (b c u) -> p b c u", c=P, u=2),
                turned[:].rearrange("p b u c -> p b c u"),
            )

        def second_product(kind, unit, bank):
            e = unit if kind == "slot" else SHARED
            _, codes, plane = operands(kind, "h", 2 * unit, 2)
            y[kind, unit] = in_bank(bank, [P, UNIT], "y")
            nc.tensor.matmul_mx(
                out=y[kind, unit][:],
                lhsT=w2_codes[:, 2 * N * e : 2 * N * (e + 1)].bitcast(FP4X4),
                lhsT_scale=w2_planes[:, N * e : N * (e + 1)],
                rhs=codes.bitcast(FP8X4),
                rhs_scale=plane,
                start=True,
                stop=True,
            )

        def put_back(engine, e):
            copy(engine, routed_y[e], y["slot", e][:])
            nc.vector.tensor_tensor(
                routed[:].indirect(offsets[:, C * e // 16 : C * (e + 1) // 16]),
                routed_y[e],
                gate_sb[:, C * e : C * (e + 1)],
                MULT,
            )

        def gather_by_expert(s):
            for e in range(E):
                gather(s, 1, C * e, C * (e + 1))

        def early_products(s):
            for block in range(EARLY // P):
                first_product("token", block, s)

        round_x(nc.scalar, 0, 0, 0, SCALAR_ROUNDS[0])
        round_x(nc.vector, 0, 0, SCALAR_ROUNDS[0], T)
        gather(0, 0, 0, S)
        round_x(nc.scalar, 0, 1, 0, SCALAR_ROUNDS[1])
        round_x(nc.vector, 0, 1, EARLY, T)
        round_x(nc.vector, 0, 1, SCALAR_ROUNDS[1], EARLY)
        make_quads(nc.vector, "token", 0, LATE_BLOCKS[0], 2)
        gather_by_expert(0)
        make_quads(nc.vector, "slot", 0, 0, 2)
        make_quads(nc.vector, "slot", 0, 2, 2)
        quantise("expert0_0")
        make_quads(nc.scalar, "token", 0, 0, 2)
        make_quads(nc.gpsimd, "token", 0, 2, 2)
        quantise("early_0")
        quantise("expert1_0")
        early_products(0)

        round_x(nc.scalar, 1, 0, 0, T)
        gather(1, 0, 0, S)
        for unit in range(T // UNIT):
            round_x(nc.scalar, 1, 1, UNIT * unit, UNIT * (unit + 1))
        gather(1, 1, 0, S)
        for unit in range(EARLY // UNIT):
            make_quads(nc.gpsimd, "token", 1, 2 * unit, 2)
        quantise("early_1")
        early_products(1)

        round_x(nc.scalar, LAST, 0, 0, UNIT)
        round_x(nc.scalar, LAST, 0, UNIT, T)
        gather(LAST, 0, 0, S)
        make_quads(nc.gpsimd, "slot", 1, 2, 2)
        make_quads(nc.scalar, "token", 1, LATE_BLOCKS[0], 2)
        round_x(nc.scalar, LAST, 1, 0, P)
        round_x(nc.scalar, LAST, 1, P + LAST_ROUNDS, T)
        round_x(nc.vector, LAST, 1, P, P + LAST_ROUNDS)
        gather_by_expert(LAST)
        make_quads(nc.scalar, "slot", 1, 0, 2)
        quantise("expert0_1")
        make_quads(nc.gpsimd, "token", LAST, 0, 2)
        make_quads(nc.scalar, "token", LAST, 2, 1)
        for e in range(E):
            make_quads(nc.scalar, "slot", LAST, 2 * e, 2)
        make_quads(nc.scalar, "token", LAST, 3, 1)
        make_quads(nc.scalar, "token", LAST, LATE_BLOCKS[0], 2)
        quantise("expert0_2")

        for block in range(S // P):
            first_product("slot", block, 0)
        quantise("expert1_1")
        quantise("expert1_2")
        for e in range(E):
            for s in range(1, PASSES):
                for block in (2 * e, 2 * e + 1):
                    first_product("slot", block, s)
        relu(nc.scalar, "slot", 0)
        relu(nc.vector, "slot", 1)
        for block in (0, 1):
            turn(nc.scalar, "slot", block, 1, bank=block)
        quantise("slot_h0")
        second_product("slot", 0, bank=1)
        relu(nc.scalar, "slot", 2)
        relu(nc.vector, "slot", 3)
        turn(nc.vector, "slot", 2, 2, bank=3)
        put_back(nc.vector, 0)
        quantise("slot_h1")
        second_product("slot", 1, bank=3)

        quantise("unit0_2")
        quantise("late_01")
        quantise("rest_2")
        early_products(LAST)
        relu(nc.scalar, "token", 0)
        relu(nc.scalar, "token", 1)
        turn(nc.scalar, "token", 0, 2, bank=0)
        quantise("token_h0")
        put_back(nc.scalar, 1)
        for block in LATE_BLOCKS:
            for s in range(PASSES):
                first_product("token", block, s)
        for block in range(2, T // P):
            relu(nc.scalar, "token", block)
        turn(nc.scalar, "token", 2, 2, bank=sum_bank("token", 3))
        quantise("token_h1")
        for block in LATE_BLOCKS:
            turn(nc.scalar, "token", block, 1, bank=sum_bank("token", block))
        quantise("token_h2")
        for unit, bank in enumerate((*(sum_bank("token", block) for block in LATE_BLOCKS), 2)):
            second_product("token", unit, bank)
        for unit in range(T // UNIT):
            columns = slice(UNIT * unit, UNIT * (unit + 1))
            nc.vector.tensor_tensor(result[:, columns], y["token", unit][:], routed[:, columns], ADD)
            nc.sync.dma_start(out[:, columns], result[:, columns])
